import numpy as np, ml_dtypes
CORES = [2,3,42,43,82,83,122,123]
N = 8
import mx_ref
BF = ml_dtypes.bfloat16
def gcols(t, e):
    v = np.concatenate([t.reshape(8, 16, -1, 4), np.zeros((8, 16, 1, 4), BF)], axis=2)
    return np.ascontiguousarray(np.stack([v[g][:, e[g]] for g in range(8)])).reshape(128, -1)
def tile(rs):
    return np.stack(rs, axis=2).reshape(128, -1).astype(BF)
def pick(q, e):
    c = np.concatenate([q[0].reshape(128, -1, 4), np.zeros((128, 1, 4), np.uint8)], axis=1); s = np.concatenate([q[1], np.ones((16, 1), np.uint8)], axis=1)
    return (np.ascontiguousarray(c[:, e].reshape(128, -1)), np.ascontiguousarray(s[:, e]))
def join(*qs):
    return (np.concatenate([q[0] for q in qs], axis=1), np.concatenate([q[1] for q in qs], axis=1))
def put(q, e, v):
    c, s = q[0].reshape(128, -1, 4).copy(), q[1].copy(); c[:, e] = v[0].reshape(128, -1, 4); s[:, e] = v[1]
    return (c.reshape(128, -1), s)
def pk(c, s):
    return (np.ascontiguousarray(c), mx_ref.live(s))
def emit(q):
    return q[0], q[1]
def packed(v, rng):
    q = [mx_ref.quantize(np.ascontiguousarray(v[r])) for r in range(N)]
    return np.stack([a for a, b in q]), np.stack([mx_ref.plane(b, rng) for a, b in q])
def values_of_codes():
    e, c = np.zeros((128, 128, 4), np.float32), np.zeros((128, 2, 4), np.uint8)
    e[np.arange(128), np.arange(128), 0] = 1
    c[:127, :, 0] = np.arange(256).reshape(2, 128).T[:127]
    return mx_ref.matmul(mx_ref.quantize(e.reshape(128, 512).astype(BF)), (c.reshape(128, 8), np.full((16, 2), 127, np.uint8))).T.reshape(-1).astype(np.float64)
CODE_VALUE, SCALE_VALUE = values_of_codes(), 2.0 ** (np.arange(256) - 127.0)
def decode(q):
    return (CODE_VALUE[q[0]].reshape(16, 8, -1, 4) * SCALE_VALUE[q[1]][:, None, :, None] + 0.0).reshape(128, -1).astype(np.float32)
def f(rng, *shape):
    return mx_ref.flush((rng.standard_normal(shape, dtype=np.float32) * np.exp2(rng.integers(-2, 3, shape[:-1] + (1,)))).astype(BF))
def wide(rng, *shape, cols=0):
    v = rng.standard_normal(shape, dtype=np.float32) * np.exp2(rng.integers(-12, 13, shape)).astype(np.float32)
    if cols: v *= np.repeat(np.exp2(rng.integers(-cols, cols + 1, shape[:-2] + (1, shape[-1] // 4))) * (rng.random(shape[:-2] + (1, shape[-1] // 4)) > 0.0625), 4, axis=-1).astype(np.float32)
    return mx_ref.flush(v.astype(BF))
C, H = 256, 128
MASK = [1, 2, 4]
def big(v):
    v = v.astype(np.float32)
    v[np.abs(v) < np.float32(2.0 ** -16)] = 0
    return v.astype(BF)
def numbers_of(rng):
    return {"x": big(f(rng, N, 128, 4 * C)), "u": np.array(f(rng, N, 128, 512)), "v": np.array(f(rng, N, 128, 512))}
def layers(rng, k=1.0):
    return big(np.clip(rng.standard_normal((N, 128, 2048), dtype=np.float32), -4, 4) * np.float32(k)).reshape(N, 8, 16, 4, 8, 16, 4)
def weights(rng, w):
    c, p = packed(np.ascontiguousarray(w).reshape(N, 128, 2048), rng)
    return {"wc": c, "ws": p}
def setup_inputs(rng):
    return {**numbers_of(rng), **weights(rng, layers(rng))}
def setup_inputs_ties(rng):
    d = numbers_of(rng)
    e = rng.permutation(N)
    x = d["x"].reshape(N, 8, 16, C, 4)
    for r in range(N):
        k = rng.permutation(C) % 3
        if r == e[0]: k = np.zeros(C, int)
        elif r in e[2::2]: k = rng.permutation(3)[np.arange(C) % 3]
        a = x[r][:, :8, :3].copy()
        a[:, :, 2] = 0
        x[r][:, :8] = a[:, :, k]
    x[e[1]] = 0
    u = d["u"].reshape(N, 8, 16, 128, 4)
    for i in range(3): u[:, :, 8:, i::16] = 0
    w = layers(rng)
    w[:, :, :, :, :, :8] = 0
    return {"x": x.reshape(N, 128, 4 * C), "u": u.reshape(N, 128, 512), "v": d["v"], **weights(rng, w)}
def setup_inputs_near(rng):
    d = numbers_of(rng)
    x = d["x"].astype(np.float32).reshape(N, 8, 16, C, 4)
    x[:, :, 0] = 0
    x[:, :, 8:] = 0
    u = d["u"].reshape(N, 128, 128, 4)
    for i in range(3): u[:, :, i::16] = 0
    o = rng.permutation(N) % 4
    for r in range(N):
        k = 1.0 if o[r] == 0 else 2.0 ** -30
        if o[r] < 2:
            x[r, :, 0, :, 0] = rng.integers(0, 2, (8, C)) * 2.0 - 1.0
            s = rng.integers(0, 16, (8, C))
            x[r, :, 8] = ((s[:, :, None] >> np.arange(4)) & 1) * np.exp2(np.arange(4) - 23.0)
            x[r, :, 9, :, 0] = 2.0 ** -10
            x[r, :, 10:12, :, 0] = rng.integers(-1, 2, (8, 2, C)) * 2.0 ** -23
        else:
            x[r, :, 8, :, 0] = rng.integers(8 if o[r] == 2 else -15, 16, (8, C)) * 2.0 ** -29
            x[r, :, 10:14:2, :, 0] = rng.integers(8, 11, (8, 2, C)) * 2.0 ** -32
            x[r, :, 11:15:2, :, 0] = rng.integers(8, 10, (8, 2, C)) * 2.0 ** -32
        for g in rng.permutation(8)[:4]: x[r, g, 0 if o[r] < 2 else 8, rng.integers(C), 0] = 2.0 ** 19 * rng.choice([-1.0, 1.0])
        for h in range(0, 128, 16):
            if o[r] < 2:
                u[r, h, h, 0] = k
                u[r, h + 8, h] = k
                u[r, h + 9, h, 0] = k
                u[r, h + 10, h + 1, 0] = k
                u[r, h + 11, h + 2, 0] = k
            else:
                u[r, h + 8, h, 0] = k
                for i in range(2):
                    u[r, h + 10 + 2 * i, h + 1 + i, 0] = 1.125 * k
                    u[r, h + 11 + 2 * i, h + 1 + i, 0] = -1.25 * k
    w = layers(rng, 0.125)
    for i in [0, 8, 9, 10, 11, 12, 13, 14, 15]:
        w[:, :, i] = 0
        w[:, :, :, :, :, i] = 0
    return {"x": x.reshape(N, 128, 4 * C).astype(BF), "u": u.reshape(N, 128, 512), "v": d["v"], **weights(rng, w)}
def setup_inputs_late(rng):
    d = numbers_of(rng)
    x = d["x"].astype(np.float32).reshape(N, 8, 16, C, 4)
    k = (1 + 2 * rng.integers(0, 64, (N, 8, 8, C, 4))) * 2.0 ** -7
    a = (1.0 + k) * np.exp2(-rng.integers(8, 15, k.shape).astype(np.float64))
    a[:, :, 0, :, 0] = 1.96875
    x[:, :, 8:] = a * rng.choice([-1.0, 1.0], k.shape) * np.exp2(rng.integers(0, 3, (N, 8, 1, C, 1)).astype(np.float64))
    h = rng.permutation(8)
    x[:, h[0], 8:] *= np.float32(0.125)
    x[:, h[0], 8, :, 0] = np.where(rng.integers(0, 2, (N, C)) == 0, 3.0, 0.9375)
    x[:, h[1], 8:] = 0
    x[:, :, 0] = 0
    i = int(rng.integers(0, 2))
    for r in range(N):
        out = (r + i) % 2 == 0
        x[r, :, 0, :, 0] = 0.25 if out else -0.25
        x[r, :, 0, :, 1] = 0.25 if out or (r // 2) % 2 == 0 else -0.25
        if out:
            x[r, ::2, 0, C - 1, 0] = -0.25
            x[r, ::4, 0, C - 1, 1] = -0.25
    u = d["u"].reshape(N, 128, 128, 4)
    u[:, :, 1::16] = 0
    u[:, :, 2::16] = 0
    for g in range(0, 128, 16):
        u[:, g, g + 1, 0] = 1
        u[:, g, g + 2, 1] = 1
    w = layers(rng)
    w[:, :, :, :, h[:2], 8:] = 0
    for p in range(8, 16):
        for b in range(4):
            if p > 8 or b > 0: w[:, h[0], p, b, h[1], p, b] = 1
    return {"x": x.reshape(N, 128, 4 * C).astype(BF), "u": u.reshape(N, 128, 512), "v": d["v"], **weights(rng, w)}
def setup_inputs_ends(rng):
    d = numbers_of(rng)
    u = d["u"].reshape(N, 8, 16, 128, 4)
    for i in range(3): u[:, :, :, i::16] = 0
    x = np.zeros((N, 8, 16, C, 4))
    w = rng.choice([-1.0, 1.0], (N, 128, 2048)) * 2.0 ** -7
    most, o = 1.2890625 * 2.0 ** 29, rng.permutation(N) % 4
    for r in range(N):
        h = rng.permutation(8)
        if o[r] == 0:
            x[r] = -most * (0.9 + 0.1 * rng.random((8, 16, C, 4)))
            x[r, h[:4]] = -most
            u[r, :, :, ::32] = 2.0 ** 30
            u[r, h[:4], :, 16::32] = 2.0 ** 30
            u[r, :, :, 1::16] = -2.0 ** 30
            u[r, :, :, 2::16] = 2.0 ** 30
            w[r] = 2.0 ** -7
        if o[r] == 1:
            x[r] = most * (0.75 + 0.25 * rng.random((8, 16, C, 4))) * rng.choice([-1.0, 1.0], (8, 1, C, 1))
            for g in range(8):
                for i in (0, 1, 3): u[r, h[(g + i) % 8], :, 16 * g] = 2.0 ** 30
                if g % 2:
                    u[r, h[g - 1], :, 16 * g + 1] = 2.0 ** 30
                    u[r, h[g], :, 16 * g + 2] = -2.0 ** 30
        if o[r] == 2:
            x[r] = 2.0 ** -30
            for g in range(8):
                u[r, g, 0, 16 * g, 0] = 2.0 ** -30
                u[r, g, 0, 16 * g + 1, 0] = 2.0 ** -30 if g % 2 else -2.0 ** -30
                u[r, g, 0, 16 * g + 2, 0] = 2.0 ** -30
            w[r] = 0
        if o[r] == 3:
            x[r] = most * rng.choice([-1.0, 1.0], (8, 16, C, 4))
            for i in range(3): u[r, :, :, i::16] = (2.0 ** 30 * rng.choice([-1.0, 1.0], (8, 16, 8, 4))).astype(np.float32).astype(BF)
    d["v"] = (np.where(d["v"] < 0, -1.0, 1.0) * np.where(rng.permutation(N) % 2, 2.0 ** -30, 2.0 ** 30)[:, None, None]).astype(np.float32).astype(BF)
    return {"x": x.astype(np.float32).reshape(N, 128, 4 * C).astype(BF), "u": u.reshape(N, 128, 512), "v": d["v"], **weights(rng, w.astype(np.float32).astype(BF))}
def setup_inputs_spread(rng):
    d = numbers_of(rng)
    d["x"] = big(wide(rng, N, 128, 4 * C, cols=4))
    return {**d, **weights(rng, layers(rng, 0.125))}
def check_inputs(d):
    b = []
    for k in ("x", "u", "v"):
        a = np.abs(d[k].astype(np.float32))
        if not (np.isfinite(a).all() and ((a == 0) | (a >= 2.0 ** -30) & (a <= 2.0 ** 30)).all()): b.append("a value of " + k)
    none, least, most = [emit(mx_ref.quantize(np.full((128, 16), k, np.float32).astype(BF)))[1][0, 0] for k in (0.0, 2.0 ** -30, 2.0 ** 30)]
    n = 0.0
    for r in range(N):
        if ((d["wc"][r] == 0x7F) | (d["wc"][r] == 0xFF)).any(): b.append("wc: a code that is no number")
        s = mx_ref.live(d["ws"][r])
        if ((s != none) & ((s < least) | (s > most))).any(): b.append("ws: a scale out of range")
        n = max(n, float(np.max(np.abs(decode(pk(d["wc"][r], d["ws"][r]))))))
    m, k = float(np.max(np.abs(d["x"].astype(np.float32)))), 1.0 + 20.0 * n
    if not m * k * k * k <= 2.0 ** 30: b.append("x and W together too large")
    return b
def balls(o, out, turn):
    a, b, last = np.zeros_like(o), np.zeros_like(o), np.zeros_like(o)
    np.put_along_axis(last, o, np.zeros_like(o) + np.arange(C), axis=2)
    i, j = np.zeros((N, 8), np.int64), np.ones((N, 8), np.int64)
    n = j + 1
    for c in range(C):
        a[:, :, c] = np.take_along_axis(o, i[:, :, None], axis=2)[:, :, 0]
        b[:, :, c] = np.take_along_axis(o, j[:, :, None], axis=2)[:, :, 0]
        np.put_along_axis(last, a[:, :, c:c + 1], c, axis=2)
        i, j = np.where(out[:, :, c], n % C, np.where(turn[:, :, c], j, i)), np.where(turn[:, :, c], i, j)
        n = n + out[:, :, c]
    return a, b, last
def reference(x, u, v, wc, ws):
    qu = [mx_ref.quantize(u[r]) for r in range(N)]
    lay = [pk(wc[r], ws[r]) for r in range(N)]
    now = [x[r] for r in range(N)]
    for m in MASK:
        q = [mx_ref.quantize(now[r]) for r in range(N)]
        s = np.stack([mx_ref.matmul(qu[r], q[r]) for r in range(N)]) + np.float32(0.0)
        out = s[:, 1::16] > 0
        turn = (s[:, 2::16] > 0) & ~out
        a, b, last = balls(np.argsort(-s[:, ::16], axis=2, kind="stable"), out, turn)
        qz = []
        for r in range(N):
            t = decode(q[r]).astype(BF)
            z = (gcols(t, a[r]).astype(np.float32) + gcols(t, b[r]).astype(np.float32)) * np.float32(0.5)
            qz.append(mx_ref.quantize(z.astype(BF)))
        new = []
        for r in range(N):
            p = join(pick(qz[r ^ m], np.arange(H)), pick(qz[r], np.arange(H, C)))
            w = tile([mx_ref.matmul(pick(lay[r], np.arange(128 * k, 128 * k + 128)), p) * np.float32(0.03125) for k in range(4)])
            new.append((now[r].astype(np.float32) + gcols(w, last[r]).astype(np.float32)).astype(BF))
        now = new
    y, lb = np.zeros((N, 128, C), np.float32), np.zeros((N, 8, C), np.float32)
    oc, osc = np.zeros((N, 128, 4 * C), np.uint8), np.zeros((N, 16, C), np.uint8)
    for r in range(N):
        q = mx_ref.quantize(now[r])
        y[r] = mx_ref.matmul(mx_ref.quantize(v[r]), q)
        lb[r] = last[r]
        oc[r], osc[r] = emit(q)
    return {"y": y, "lb": lb, "oc": oc, "osc": osc}

@@ -1,0 +1,500 @@
+from concourse.mybir import dt, AluOpType, ActivationFunctionType
+
+A = AluOpType
+F = ActivationFunctionType
+MASK = [1, 2, 4]
+VPL = (15, 14, 13)
+YA, NV = 1, 0
+BF, F32, I32, U16, Q4, U8 = "bfloat16", "float32", "int32", "uint16", "float8_e4m3fn_x4", "uint8"
+
+SCRATCH = {"P": ("psum", [128, 4096], F32)}
+for _d, _names in (
+    (BF, "ub:512 vb:512 sm:176 mD:256 m0:256 m16:256 m4:256 dd:128 gi:128 eb:516 ob:1024 CR:272 PF:272 "
+         "MT:2816 sg:2048 DS:256 O:272 thr:256 nt:256 al:256 Kp:256 Bs:272 N1:256 Dn:256 Y:256 Ya:256 Yp:256 Bp:256 "
+         "rr:256 sN:512 m32:256 sY:256 sB:256 LP:576 LR:256 sL:256 AB:512 s4:512 To:1024 Tp:1024 Zb:1024 Z:1024 V:1024 "
+         "X0:1024 X1:1024 X2:1024 X3:1024"),
+    (F32, "cf:16 mp:256 k16:16 CC:16 DUM:16 Sm:256 Fs:256 RS:2048 y1:16 sel:256 w1:96 LF:256 yo:256"),
+    (I32, "i1:32 i2:32 i3:24 i4:16 i5:16 pc:8"),
+    (U16, "ul:24 il:16 pos:16 PL:32 TG:18 oL:64 oH:64 so0:64 so1:64 so2:64 lo0:64 lo1:64 lo2:64"),
+    (Q4, "uq:128 upq:384 vq:128 wq:512 eq:512 oq:256 mq:704 zq:256 xq0:256 xq1:256 xq2:256 xq3:256 lq0:256 lq1:256 lq2:256"),
+    (U8, "us:128 ups:384 vs:128 wsc:512 es:512 osn:256 ms:704 zs:256 xs0:256 xs1:256 xs2:256 xs3:256 ls0:256 ls1:256 ls2:256"),
+):
+    for _e in _names.split():
+        SCRATCH[_e.split(":")[0]] = ("sbuf", [128, int(_e.split(":")[1])], _d)
+
+SEMAPHORES = ["v", "s", "t", "gq", "dx0", "dx1", "du", "dw", "dv", "o1", "o2", "sent",
+              "aq0", "aq1", "aq2", "al0", "al1", "al2"]
+
+TILE0 = {0: 0, 1: 256, 2: 448, 3: 576}
+
+
+def plane(k):
+    n = 16 - k
+    return TILE0[n // 4], n % 4
+
+
+def rank_program(g, core, T, topo):
+    rank = T.rank_of(core)
+    if rank is None:
+        return
+    Q = {"v": g.vector, "s": g.scalar, "t": g.tensor, "g": g, "y": g.sync}
+    own = {"v": "v", "s": "s", "t": "t", "g": "gq"}
+    cnt = {}
+    waited = {q: {} for q in Q}
+    lastw, readers = {}, {}
+
+    def need(q, dep):
+        sem, val = dep[0], dep[1]
+        if waited[q].get(sem, 0) < val:
+            Q[q].wait_ge(T.sem[sem], val)
+            waited[q][sem] = val
+
+    def op(q, fn, R=(), W=(), sem=None, inc=1, acc=False):
+        deps = {}
+
+        def add(d):
+            deps[d[0]] = max(deps.get(d[0], 0), d[1])
+        for k in R:
+            if k in lastw:
+                add(lastw[k])
+            if k[0] == "P" and k[1:].isdigit():
+                for d in readers.get(k, []):
+                    if d[2] != q:
+                        add(d)
+        for k in W:
+            if k in lastw and not acc:
+                add(lastw[k])
+            for d in readers.get(k, []):
+                add(d)
+        for s_, v_ in deps.items():
+            need(q, (s_, v_))
+        ins = fn()
+        sem = sem or own[q]
+        cnt[sem] = cnt.get(sem, 0) + inc
+        ins.then_inc(T.sem[sem], inc)
+        me = (sem, cnt[sem], q)
+        for k in R:
+            readers.setdefault(k, []).append(me)
+        for k in W:
+            lastw[k] = me
+            readers[k] = []
+
+    vec, sca, ten = g.vector, g.scalar, g.tensor
+
+    def ts(out, in0, s1, s2, o0, o1, R, W):
+        if o1 is None:
+            op("v", lambda: vec.tensor_scalar(out, in0, s1, None, o0), R, W)
+        else:
+            op("v", lambda: vec.tensor_scalar(out, in0, s1, s2, o0, o1), R, W)
+
+    def tt(out, a, b, o, R, W):
+        op("v", lambda: vec.tensor_tensor(out, a, b, o), R, W)
+
+    def scan(out, d0, d1, init, o0, o1, R, W):
+        op("v", lambda: vec.tensor_tensor_scan(out, d0, d1, init, o0, o1), R, W)
+
+    def cp(out, in_, R, W):
+        op("v", lambda: vec.tensor_copy(out, in_), R, W)
+
+    def ms(ap, c, W):
+        op("v", lambda: vec.memset(ap, c), (), W)
+
+    def act(out, in_, f, R, W, **kw):
+        op("s", lambda: sca.activation(out, in_, f, **kw), R, W)
+
+    def qz(q, s, in_, R, W):
+        op("v", lambda: vec.quantize_mx(q, s, in_), R, W)
+
+    def mm(bank, n, lq, lsc, rq, rsc, R, start=True, stop=True):
+        op("t", lambda: ten.matmul_mx(T.P[:, 512 * bank:512 * bank + n], lq, lsc, rq, rsc, start, stop),
+           R, ["P%d" % bank], acc=not start)
+
+    def iota(out, pat, base, cm, W, fl=False):
+        if fl:
+            op("g", lambda: g.iota(out, pat, base, cm, allow_small_or_imprecise_dtypes=True), (), W)
+        else:
+            op("g", lambda: g.iota(out, pat, base, cm), (), W)
+
+    def dma(q, out, in_, R, W, sem):
+        op(q, lambda: Q[q].dma_start(out, in_), R, W, sem=sem, inc=16)
+
+    def bank(b, lo=0, hi=256):
+        return T.P[:, 512 * b + lo:512 * b + hi]
+
+    def col(j):
+        return T.cf[:, j:j + 1]
+
+    def sm(j):
+        return T.sm[:, 16 * j:16 * j + 16]
+
+    nsent = [0]
+
+    def engines(a, b):
+        return topo.engines(a, b)
+
+    def send(peer, dst, src, R, sem):
+        eng = engines(core, peer)
+        rid, pid, _ = topo.addr(peer)
+        for k in R:
+            need("g", lastw[k])
+        g.remote_dma(dst, src, T.sem[sem], T.sem.sent, pid, rid, sum(1 << e for e in eng))
+        nsent[0] += len(eng)
+
+    def arrives(peer, keys, sem, writes):
+        n = len(engines(peer, core)) * writes
+        cnt[sem] = n
+        for k in keys:
+            lastw[k] = (sem, n, "r")
+
+    dma("y", T.ub[:], T.u[:], (), ["ub"], "du")
+    dma("s", T.X0[:, 0:512], T.x[:, 0:512], (), ["X00"], "dx0")
+    dma("y", T.X0[:, 512:1024], T.x[:, 512:1024], (), ["X01"], "dx1")
+    need("y", lastw["X01"])
+    dma("y", T.wq[:].bitcast(dt.uint8), T.wc[:], (), ["w_"], "dw")
+    dma("y", T.wsc[:], T.ws[:], (), ["w"], "dw")
+    dma("y", T.vb[:], T.v[:], (), ["vb"], "dv")
+
+    iota(T.i1[:, 0:16], [[1, 16]], 128, -1, ["i1a"])
+    iota(T.i1[:, 16:32], [[0, 16]], 0, 1, ["i1b"])
+    iota(T.i3[:], [[1, 3], [16, 8]], 0, 0, ["i3"])
+    iota(T.dd[:], [[1, 128]], 0, -1, ["dd"], True)
+    iota(T.gi[:], [[1, 8], [0, 16]], 0, 0, ["gi"], True)
+    iota(T.k16[:], [[16, 16]], 0, 0, ["k16"], True)
+    iota(T.PF[:, 0:256], [[1, 256]], 0, 0, ["PFa"], True)
+    iota(T.PF[:, 256:257], [[0, 1]], 0, 0, ["PF"], True)
+    iota(T.CR[:], [[1, 272]], 0, 0, ["CR", "CRx"], True)
+
+    for a, b in ((2112, 2816), (832, 1024), (1600, 1792)):
+        ms(T.MT[:, a:b], 0.0, ["MTz"])
+    ts(T.i2[:], T.i1[:], 15, None, A.bitwise_and, None, ["i1a", "i1b"], ["i2"])
+    ts(T.pc[:, 1:2], T.i1[:, 16:17], 4, None, A.arith_shift_right, None, ["i1b"], ["pc1"])
+    cp(T.il[:], T.i2[:, 16:32], ["i2"], ["il"])
+    ts(sm(1), T.i2[:, 0:16], 0.0, None, A.is_equal, None, ["i2"], ["sm1"])
+    ts(sm(2), T.i2[:, 0:16], 0.0, None, A.not_equal, None, ["i2"], ["sm2"])
+    act(T.mD[:], sm(1).indirect(T.il[:]), F.Identity, ["sm1", "il"], ["mD"])
+    act(T.m0[:], sm(2).indirect(T.il[:]), F.Identity, ["sm2", "il"], ["m0"])
+    ts(T.pc[:, 2:3], T.i1[:, 16:17], 2, None, A.arith_shift_right, None, ["i1b"], ["pc2"])
+    cp(sm(0), T.i2[:, 0:16], ["i2"], ["sm0"])
+    ts(sm(3), T.i2[:, 0:16], 1.0, -256.0, A.is_equal, A.mult, ["i2"], ["sm3"])
+    ts(sm(4), T.i2[:, 0:16], 0.0, 1024.0, A.is_equal, A.mult, ["i2"], ["sm4"])
+    cp(T.cf[:, 6:8], T.pc[:, 1:3], ["pc1", "pc2"], ["c6", "c7"])
+    cp(T.ul[:], T.i3[:], ["i3"], ["ul"])
+    tt(sm(5), sm(3), sm(4), A.add, ["sm3", "sm4"], ["sm5"])
+    ts(sm(6), T.i2[:, 0:16], 15.0, 1024.0, A.is_equal, A.mult, ["i2"], ["sm6"])
+    ts(sm(7), T.i2[:, 0:16], 0.0, -512.0, A.is_equal, A.mult, ["i2"], ["sm7"])
+    act(T.m16[:], sm(5).indirect(T.il[:]), F.Identity, ["sm5", "il"], ["m16"])
+    ms(T.eb[:], 0.0, ["eb"])
+    tt(sm(8), sm(6), sm(7), A.add, ["sm6", "sm7"], ["sm8"])
+    for t in range(4):
+        ts(T.ob[:, t:512:4], T.gi[:], col(6), None, A.is_equal, None, ["gi", "c6"], ["ob0%d" % t])
+    act(T.mp[:], sm(8).indirect(T.il[:]), F.Identity, ["sm8", "il"], ["mp"])
+    ts(T.eb[:, 3:515:4], T.dd[:], 0.0, None, A.is_equal, None, ["dd"], ["eb"])
+    ob0 = ["ob0%d" % t for t in range(4)]
+    act(T.ob[:, 512:1024], T.ob[:, 0:512], F.Identity, ob0, ["ob1"])
+    op("g", lambda: g.affine_select(T.ob[:, 512:1024:4], T.ob[:, 512:1024:4], [[1, 128]], A.is_gt, 0.0, 0, -1),
+       ["ob1"], ["ob1"])
+    qz(T.mq[:, 576:704], T.ms[:, 576:704], T.MT[:, 2304:2816], ["MTz"], ["mq2"])
+    ms(T.RS[:, 127:128], 0.0, ["RS0"])
+    ms(T.Bs[:, 15:16], 0.0, ["Bs0"])
+    ms(T.N1[:, 0:1], 255.0, ["N10"])
+    ms(T.Y[:, 0:1], -256.0, ["Y0"])
+    nz15, d15 = T.sm[:, 47:48], T.sm[:, 15:16]
+    for b in range(2):
+        qz(T.eq[:, 128 * b:128 * b + 128], T.es[:, 128 * b:128 * b + 128], T.eb[:, 3 - b:515 - b], ["eb"], ["eq%d" % b])
+
+    ts(col(14), T.i1[:, 16:17], col(7), None, A.subtract, None, ["i1b", "c7"], ["c14"])
+    ts(col(9), nz15, 512.0, d15, A.mult, A.add, ["sm2", "sm0"], ["c9"])
+    ts(T.i4[:], T.i1[:, 0:16], col(14), None, A.add, None, ["i1a", "c14"], ["i4"])
+    ts(T.CC[:], T.k16[:], 1025.0, col(9), A.add, A.add, ["k16", "c9"], ["CC"])
+    ts(T.i5[:], T.i4[:], 3, None, A.bitwise_and, None, ["i4"], ["i5"])
+    ts(T.pc[:, 3:4], T.i1[:, 16:17], 3, None, A.bitwise_and, None, ["i1b"], ["pc3"])
+
+    qz(T.uq[:], T.us[:], T.ub[:], ["ub"], ["uq"])
+    act(T.ups[:, 0:128], T.us[:].indirect(T.ul[:, 0:8]), F.Copy, ["uq", "ul"], ["ups"])
+    cp(T.upq[:, 0:128].bitcast(dt.uint32), T.uq[:].bitcast(dt.uint32).indirect(T.ul[:, 0:8]), ["uq", "ul"], ["upq"])
+    act(T.ups[:, 128:384], T.us[:].indirect(T.ul[:, 8:24]), F.Copy, ["uq", "ul"], ["ups2"])
+    act(col(0), nz15, F.Identity, ["sm2"], ["c0"], scale=256.0)
+    act(col(8), nz15, F.Identity, ["sm2"], ["c8"], scale=-256.0, bias=256.0)
+
+    def early_a():
+        ts(sm(3), T.i5[:], 0.0, 1024.0, A.is_equal, A.mult, ["i5"], ["sm3"])
+        ts(sm(4), T.i5[:], 1.0, -256.0, A.is_equal, A.mult, ["i5"], ["sm4"])
+        ts(col(13), T.i5[:, 3:4], 0.0, 256.0, A.not_equal, A.mult, ["i5"], ["c13"])
+        tt(sm(9), sm(3), sm(4), A.add, ["sm3", "sm4"], ["sm9"])
+
+    def late_a():
+        for b in range(2, 4):
+            qz(T.eq[:, 128 * b:128 * b + 128], T.es[:, 128 * b:128 * b + 128], T.eb[:, 3 - b:515 - b], ["eb"], ["eq%d" % b])
+        qz(T.oq[:], T.osn[:], T.ob[:], ob0 + ["ob1"], ["oq"])
+        ts(col(1), T.pc[:, 3:4], 256.0, col(13), A.mult, A.add, ["pc3", "c13"], ["c1"])
+        ts(col(10), d15, col(0), -16.0, A.add, A.add, ["sm0", "c0"], ["c10"])
+
+    def late_b():
+        ts(T.DUM[:], T.k16[:], -1.0, col(10), A.mult, A.add, ["k16", "c10"], ["DUM"])
+        ts(T.sm[:, 160:161], d15, 4.0, col(12), A.mult, A.add, ["sm0", "c12"], ["c5"])
+        ts(T.DUM[:, 15:16], T.DUM[:, 15:16], col(11), None, A.add, None, ["c11", "DUM"], ["DUM"])
+
+    def late_s():
+        act(T.m4[:], sm(9).indirect(T.il[:]), F.Identity, ["sm9", "il"], ["m4"])
+        act(T.m32[:], T.m16[:], F.Identity, ["m16"], ["m32"], scale=2.0)
+        act(col(11), T.sm[:, 31:32], F.Identity, ["sm1"], ["c11"], scale=2000.0)
+        act(col(12), T.sm[:, 31:32], F.Identity, ["sm1"], ["c12"], scale=2000.0, bias=-576.0)
+
+    def unpack(b0, q, s, keys):
+        for b in range(4):
+            mm(b0 + b, 256, T.eq[:, 128 * b:128 * b + 128], T.es[:, 128 * b:128 * b + 128], q[:], s[:], ["eq%d" % b] + keys)
+
+    def unpack_copy(b0, dst, key, bs):
+        for b in bs:
+            act(dst[:, 256 * b:256 * b + 256], bank(b0 + b), F.Identity, ["P%d" % (b0 + b)], [key + str(b)], scale=0.5)
+
+    def sel16(out, v, R, W):
+        scan(out, T.m16[:], v[:], 0.0, A.add, A.min, ["m16"] + R, W)
+
+    def up(j):
+        return T.upq[:, 128 * j:128 * j + 128], T.ups[:, 128 * j:128 * j + 128]
+
+    def pview(k, a, b):
+        c0, t = plane(k)
+        return T.MT[:, 4 * (c0 + a) + t:4 * (c0 + b):4]
+
+    def rcol(k):
+        return T.Fs[:, 16 * k + 15:16 * k + 16]
+
+    def fkey(k):
+        return "F1" if k >= 8 else "F0"
+
+    def vplane(k):
+        ts(pview(k, 0, 16 * k), bank(0, 0, 16 * k), rcol(k), None, A.is_lt, None, ["P0", fkey(k), "MTz"], ["M%d" % k])
+
+    def vsum(k):
+        scan(T.RS[:, 128 * k + 128 - 8 * k:128 * k + 128], pview(k, 0, 8 * k), pview(k, 8 * k, 16 * k), 0.0,
+             A.add, A.add, ["M%d" % k], ["RS%d" % k])
+
+    sgo, o_ = {}, 0
+    for k in range(1, 16):
+        sgo[k] = o_
+        o_ += 16 * k
+
+    def s1(k):
+        b = 5 if k < 8 else 1
+        act(T.sg[:, sgo[k]:sgo[k] + 16 * k], bank(b, 0, 16 * k), F.Sign, ["P%d" % b, fkey(k)], ["sg%d" % k],
+            scale=-1.0, bias=rcol(k))
+
+    def s2(k):
+        act(pview(k, 0, 16 * k), T.sg[:, sgo[k]:sgo[k] + 16 * k], F.Relu, ["sg%d" % k, "MTz"], ["M%d" % k, "RS%d" % k],
+            accum_out=T.RS[:, 128 * k + 127:128 * k + 128])
+
+    def splanes(ks):
+        s1(ks[0])
+        for n, k in enumerate(ks):
+            if n + 1 < len(ks):
+                s1(ks[n + 1])
+            s2(k)
+
+    def state(r, a, b, keys):
+        if r > 0:
+            vk = ["V%d%d" % (h, k) for h in range(2) for k in range(4)] + ["oL", "X%d0" % (r - 1), "X%d1" % (r - 1),
+                                                                          "X%d2" % (r - 1)]
+            tt(T["X%d" % r][:, a:b], T.V[:].indirect(T.oL[:, a // 16:b // 16]), T["X%d" % (r - 1)][:, a:b], A.add, vk, keys)
+
+    def quant(r, h):
+        a, b = 128 * h, 128 * h + 128
+        qz(T["xq%d" % r][:, a:b], T["xs%d" % r][:, a:b], T["X%d" % r][:, 4 * a:4 * b],
+           ["X%d0" % r] if h == 0 else ["X%d1" % r, "X%d2" % r], ["xq%d%d" % (r, h)])
+
+    for r in range(3):
+        peer = T.cores[rank ^ MASK[r]]
+        xq, xs = T["xq%d" % r], T["xs%d" % r]
+        xk = ["xq%d0" % r, "xq%d1" % r]
+        lq, lsc, so, lo = T["lq%d" % r], T["ls%d" % r], T["so%d" % r], T["lo%d" % r]
+        state(r, 0, 512, ["X%d0" % r])
+        quant(r, 0)
+
+        def scores(b, j, lo_, hi_):
+            mm(b, hi_ - lo_, *up(j), xq[:, lo_:hi_], xs[:, lo_:hi_],
+               (["upq", "ups"] if j == 0 else ["upq2", "ups2"]) + xk[lo_ // 128:hi_ // 128])
+
+        scores(4, 0, 0, 128)
+        scores(5, 0, 0, 128)
+        if r > 0:
+            scores(6, 1, 0, 128)
+            scores(7, 2, 0, 128)
+        state(r, 512, 768, ["X%d1" % r])
+        if r == 0:
+            quant(r, 1)
+        tt(T.Sm[:, 0:128], bank(4, 0, 128), T.mD[:, 0:128], A.mult, ["P4", "mD"], ["Sm0"])
+        scan(T.Fs[:, 0:128], T.m0[:, 0:128], T.Sm[:, 0:128], 0.0, A.mult, A.add, ["m0", "Sm0"], ["F0"])
+        state(r, 768, 1024, ["X%d2" % r])
+        if r > 0:
+            quant(r, 1)
+        else:
+            cp(T.upq[:, 128:384].bitcast(dt.uint32), T.uq[:].bitcast(dt.uint32).indirect(T.ul[:, 8:24]), ["uq", "ul"], ["upq2"])
+            scores(0, 0, 0, 256)
+            scores(1, 0, 0, 256)
+            scores(6, 1, 0, 128)
+            scores(7, 2, 0, 128)
+            early_a()
+        scores(2, 1, 128, 256)
+        if r > 0:
+            scores(0, 0, 0, 256)
+        scores(3, 2, 128, 256)
+        if r > 0:
+            scores(1, 0, 0, 256)
+        if r == 0:
+            send(peer, lq[:].bitcast(dt.uint8), xq[:].bitcast(dt.uint8), xk, "aq%d" % r)
+        else:
+            send(peer, lq[:, 0:128].bitcast(dt.uint8), xq[:, 0:128].bitcast(dt.uint8), xk[:1], "aq%d" % r)
+            send(peer, lq[:, 128:256].bitcast(dt.uint8), xq[:, 128:256].bitcast(dt.uint8), xk, "aq%d" % r)
+        send(peer, lsc[:], xs[:], xk, "aq%d" % r)
+        arrives(peer, ["lq%d" % r], "aq%d" % r, 2 if r == 0 else 3)
+        arrives(peer, ["lo%d" % r], "al%d" % r, 1)
+        splanes([7, 6, 5, 4, 3, 2, 1])
+
+        U = 2.0 ** 80
+        ts(T.thr[:, 0:128], bank(6, 0, 128), 0.0, U, A.is_gt, A.mult, ["P6"], ["thr0"])
+        tt(pview(16, 0, 128), bank(4, 0, 128), T.Fs[:, 0:128], A.is_le, ["P4", "F0"], ["M16a"])
+        tt(T.nt[:, 0:128], bank(7, 0, 128), T.thr[:, 0:128], A.is_le, ["P7", "thr0"], ["nt0"])
+        ts(T.thr[:, 128:256], bank(2, 0, 128), 0.0, U, A.is_gt, A.mult, ["P2"], ["thr1"])
+        tt(T.Sm[:, 128:256], bank(0, 128, 256), T.mD[:, 128:256], A.mult, ["P0", "mD"], ["Sm1"])
+        tt(T.nt[:, 128:256], bank(3, 0, 128), T.thr[:, 128:256], A.is_le, ["P3", "thr1"], ["nt1"])
+        scan(T.Fs[:, 128:256], T.m0[:, 128:256], T.Sm[:, 128:256], 0.0, A.mult, A.add, ["m0", "Sm1"], ["F1"])
+        act(T.Kp[:], T.thr[:], F.Identity, ["thr0", "thr1"], ["Kp"], scale=511.0 / U, bias=-256.0)
+        act(T.Bs[:, 16:272], T.thr[:], F.Identity, ["thr0", "thr1"], ["Bs"], scale=-512.0 / U, bias=256.0)
+        act(T.al[:], T.nt[:], F.Identity, ["nt0", "nt1"], ["al"], scale=2.0, bias=-1.0)
+        big = [k for k in range(15, 8, -1) if k not in VPL]
+        splanes([8] + big[:YA])
+        vplane(VPL[0])
+        tt(pview(16, 128, 256), bank(0, 128, 256), T.Fs[:, 128:256], A.is_le, ["P0", "F1"], ["M16b"])
+        scan(T.Dn[:], T.Kp[:], T.Bs[:, 15:271], 0.0, A.add, A.add, ["Kp", "Bs", "Bs0"], ["Dn"])
+        scan(T.N1[:, 1:256], T.Kp[:, 0:255], T.Bs[:, 16:271], 255.0, A.add, A.add, ["Kp", "Bs"], ["N1"])
+        scan(T.Y[:, 1:256], T.al[:, 0:255], T.Dn[:, 0:255], -256.0, A.mult, A.max, ["al", "Dn"], ["Y"])
+        act(T.Ya[:], T.Y[:], F.Abs, ["Y", "Y0"], ["Ya"])
+        splanes(big[YA:])
+        for k in VPL[1:]:
+            vplane(k)
+        if r == 0:
+            late_a()
+        unpack(4, xq, xs, xk)
+        for k in VPL:
+            vsum(k)
+        scan(T.DS[:], T.m0[:], pview(16, 0, 256), 0.0, A.mult, A.add, ["m0", "M16a", "M16b"], ["DS"])
+        sel16(T.sN[:, 0:256], T.N1, ["N1", "N10"], ["sN"])
+        sel16(T.sN[:, 256:512], T.Ya, ["Ya"], ["sA"])
+        qz(T.mq[:, 448:640], T.ms[:, 448:640], T.MT[:, 1792:2560], ["M%d" % k for k in range(1, 9)] + ["MTz"], ["mq2"])
+        qz(T.mq[:, 0:256], T.ms[:, 0:256], T.MT[:, 0:1024], ["M16a", "M16b", "M15", "M14", "M13", "MTz"], ["mq0"])
+        ones = (T.oq[:, 0:128], T.osn[:, 0:128])
+        mm(2, 256, T.oq[:, 128:256], T.osn[:, 128:256], T.mq[:, 0:256], T.ms[:, 0:256], ["oq", "mq0"], True, False)
+        mm(2, 128, *ones, T.mq[:, 448:576], T.ms[:, 448:576], ["oq", "mq2"], False, False)
+        mm(2, 128, *ones, T.mq[:, 576:704], T.ms[:, 576:704], ["oq", "mq2"], False, False)
+        tt(T.y1[:], T.CC[:], T.DS[:, 15::16], A.subtract, ["CC", "DS"], ["y1"])
+        qz(T.mq[:, 256:448], T.ms[:, 256:448], T.MT[:, 1024:1792], ["M12", "M11", "M10", "M9", "MTz"], ["mq1"])
+        mm(2, 192, *ones, T.mq[:, 256:448], T.ms[:, 256:448], ["oq", "mq1"], False, True)
+        tt(T.mp[:, 15::16], T.y1[:], T.RS[:, 127::128], A.subtract, ["y1"] + ["RS%d" % k for k in range(16)], ["mp"])
+        ts(T.PL[:], T.sN[:, 15::16], -1.0, col(8), A.mult, A.add, ["sN", "sA", "c8"], ["PL1", "PL2"])
+        scan(T.rr[:, 0:255], T.nt[:, 0:255], T.nt[:, 0:255], 0.0, A.mult, A.add, ["nt0", "nt1"], ["rr"])
+        scan(T.sel[:], bank(2), T.mp[:], 2048.0, A.min, A.add, ["P2", "mp"], ["sel"])
+        ts(T.pos[:], T.sel[:, 15::16], -1024.0, None, A.add, None, ["sel"], ["pos"])
+        cp(T.O[:, 0:256].indirect(T.pos[:]), T.PF[:, 0:256], ["pos", "PF"], ["O"])
+        if r == 0:
+            late_s()
+        act(T.Yp[:], T.Y[:], F.Relu, ["Y", "Y0"], ["Yp"], scale=-1.0)
+        act(T.Bp[:], T.Bs[:, 16:272], F.Relu, ["Bs"], ["Bp"], scale=-2.0)
+        act(T.CR[:, 271:272], T.rr[:, 254:255], F.Abs, ["rr"], ["CRx"], scale=-1.0, bias=254.0)
+        act(T.LP[:, 0:257], T.PF[:, 0:257], F.Identity, ["PF"], ["LP"])
+        unpack_copy(4, T.To, "To", (0, 1, 2, 3))
+        unpack(0, lq, lsc, ["lq%d" % r])
+        w = [T.w1[:, 16 * n:16 * n + 16] for n in range(5)]
+        act(T.AB[:, 0:128], T.O[:, 0:256].indirect(T.PL[:, 0:8]), F.Identity, ["O", "PL1"], ["AB0"])
+        cp(T.AB[:, 128:256], T.O[:, 0:256].indirect(T.PL[:, 16:24]), ["O", "PL2"], ["AB1"])
+        act(T.O[:, 256:257], T.O[:, 0:1], F.Identity, ["O"], ["Ox"])
+        act(T.AB[:, 384:512], T.O[:, 0:256].indirect(T.PL[:, 24:32]), F.Identity, ["O", "PL2"], ["AB3"])
+        act(T.AB[:, 256:384], T.O[:, 0:257].indirect(T.PL[:, 8:16]), F.Identity, ["O", "Ox", "PL1"], ["AB2"])
+        unpack_copy(0, T.Tp, "Tp", (0,))
+        sel16(T.sY[:], T.Yp, ["Yp"], ["sY"])
+        scan(T.s4[:, 0:256], T.m4[:], T.AB[:, 0:256], 0.0, A.add, A.min, ["m4", "AB0", "AB1"], ["s40"])
+        scan(T.sB[:], T.m32[:], T.Bp[:], 0.0, A.add, A.min, ["m32", "Bp"], ["sB"])
+        ts(so[:], T.s4[:, 3:256:4], col(1), None, A.add, None, ["s40", "c1"], ["so%d" % r])
+        send(peer, lo[:], so[:], ["so%d" % r], "al%d" % r)
+        if r == 0:
+            late_b()
+        tt(w[1], T.sY[:, 15::16], T.sN[:, 15:256:16], A.max, ["sY", "sN"], ["w1"])
+        tt(w[3], T.sB[:, 15::16], T.DUM[:], A.add, ["sB", "DUM"], ["w3"])
+        ts(T.w1[:, 80:81], T.Y[:, 255:256], T.N1[:, 255:256], T.sm[:, 160:161], A.max, A.min, ["Y", "N1", "c5"], ["w5"])
+        scan(T.s4[:, 256:512], T.m4[:], T.AB[:, 256:512], 0.0, A.add, A.min, ["m4", "AB2", "AB3"], ["s41"])
+        tt(w[4], w[1], w[3], A.min, ["w1", "w3"], ["w4"])
+        ts(T.oH[:], T.s4[:, 259:512:4], col(1), None, A.add, None, ["s41", "c1"], ["oH"])
+        ts(T.TG[:, 0:17], T.w1[:, 64:81], -1.0, col(8), A.mult, A.add, ["w4", "w5", "c8"], ["TG0"])
+        if r == 0:
+            qz(T.vq[:], T.vs[:], T.vb[:], ["vb"], ["vq"])
+        cp(T.LP[:].indirect(T.TG[:, 0:17]), T.CR[:], ["TG0", "CR", "CRx"], ["LP"])
+
+        def gather_b(h, Tw, tk, off, ok):
+            for n in range(2):
+                a = 512 * h + 256 * n
+                act(T.Zb[:, a:a + 256], Tw[:].indirect(off[:, 32 + 16 * n:48 + 16 * n]), F.Identity,
+                    [tk + str(b) for b in range(4)] + [ok], ["Zb%d%d" % (h, n)])
+
+        def gather_a(h, Tw, tk, off, ok):
+            for n in range(2):
+                a = 512 * h + 256 * n
+                tt(T.Z[:, a:a + 256], Tw[:].indirect(off[:, 16 * n:16 * n + 16]), T.Zb[:, a:a + 256], A.add,
+                   [tk + str(b) for b in range(4)] + [ok, "Zb%d%d" % (h, n)], ["Z%d%d" % (h, n)])
+            qz(T.zq[:, 128 * h:128 * h + 128], T.zs[:, 128 * h:128 * h + 128], T.Z[:, 512 * h:512 * h + 512],
+               ["Z%d0" % h, "Z%d1" % h], ["zq%d" % h])
+
+        def layer(h, b0):
+            for k in range(4):
+                mm(b0 + k, 128, T.wq[:, 128 * k:128 * k + 128], T.wsc[:, 128 * k:128 * k + 128],
+                   T.zq[:, 128 * h:128 * h + 128], T.zs[:, 128 * h:128 * h + 128], ["w", "zq%d" % h])
+
+        def vcopy(q, h, k, b):
+            out = T.V[:, 256 * k + 128 * h:256 * k + 128 * h + 128]
+            if q == "s":
+                act(out, bank(b, 0, 128), F.Identity, ["P%d" % b], ["V%d%d" % (h, k)], scale=0.03125)
+            else:
+                ts(out, bank(b, 0, 128), 0.03125, None, A.mult, None, ["P%d" % b], ["V%d%d" % (h, k)])
+
+        gather_b(1, T.To, "To", T.oH, "oH")
+        unpack_copy(0, T.Tp, "Tp", (1,))
+        act(T.LP[:, 0:1], T.LP[:, 0:1], F.Identity, ["LP"], ["LP"], bias=T.LP[:, 256:257])
+        unpack_copy(0, T.Tp, "Tp", (2, 3))
+        gather_a(1, T.To, "To", T.oH, "oH")
+        layer(1, 4)
+        cp(T.LR[:], T.LP[:, 0:256].indirect(T.pos[:]), ["LP", "pos"], ["LR"])
+        gather_b(0, T.Tp, "Tp", lo, "lo%d" % r)
+        for k in range(NV):
+            vcopy("v", 1, k, 4 + k)
+        gather_a(0, T.Tp, "Tp", lo, "lo%d" % r)
+        for k in range(NV, 4):
+            vcopy("s", 1, k, 4 + k)
+        layer(0, 0)
+        scan(T.sL[:], T.m4[:], T.LR[:], 0.0, A.add, A.min, ["m4", "LR"], ["sL"])
+        vcopy("s", 0, 0, 0)
+        ts(T.oL[:], T.sL[:, 3:256:4], col(1), None, A.add, None, ["sL", "c1"], ["oL"])
+        vcopy("v", 0, 1, 1)
+        vcopy("s", 0, 2, 2)
+        vcopy("v", 0, 3, 3)
+
+    act(T.LF[:], T.LR[:], F.Identity, ["LR"], ["LF"])
+    dma("y", T.lb[:], T.LF[0:128:16, :], ["LF"], ["lb"], "o1")
+    for h in range(2):
+        a, b = 128 * h, 128 * h + 128
+        state(3, 4 * a, 4 * b, ["X3%d" % h])
+        quant(3, h)
+        key = "xq3%d" % h
+        mm(4 + h, 128, T.vq[:], T.vs[:], T.xq3[:, a:b], T.xs3[:, a:b], ["vq", key])
+        dma("y", T.oc[:, 4 * a:4 * b], T.xq3[:, a:b].bitcast(dt.uint8), [key], ["oc%d" % h], "o1")
+        if h == 0:
+            act(T.yo[:, a:b], bank(4, 0, 128), F.Identity, ["P4"], ["yo0"])
+            dma("s", T.y[:, a:b], T.yo[:, a:b], ["yo0"], ["y0"], "o2")
+        else:
+            cp(T.yo[:, a:b], bank(5, 0, 128), ["P5"], ["yo1"])
+            for k in range(4):
+                dma("s" if k < 3 else "y", T.osc[4 * k:4 * k + 4, :], T.xs3[32 * k:32 * k + 4, :], ["xq30", "xq31"],
+                    ["osc%d" % k], "o2" if k < 3 else "o1")
+            dma("y", T.y[:, a:b], T.yo[:, a:b], ["yo1"], ["y1o"], "o1")
+
+    g.wait_ge(T.sem.sent, nsent[0])
+    for s_, v_ in cnt.items():
+        need("y", (s_, v_))

@@ -3,8 +3,10 @@ from concourse.mybir import dt, AluOpType, ActivationFunctionType
 A = AluOpType
 F = ActivationFunctionType
 MASK = [1, 2, 4]
-VPL = (15, 14, 13)
-YA, NV = 1, 0
+VPL = (15, 14, 13, 9)
+YA, NV = 4, (1, 3)
+OWN, FAR = (4, 5, 6, 7), (0, 1, 3, 2)
+TP = ((0, 1), (2, 3))
 BF, F32, I32, U16, Q4, U8 = "bfloat16", "float32", "int32", "uint16", "float8_e4m3fn_x4", "uint8"
 
 SCRATCH = {"P": ("psum", [128, 4096], F32)}
@@ -195,7 +197,7 @@ def rank_program(g, core, T, topo):
        ["ob1"], ["ob1"])
     qz(T.mq[:, 576:704], T.ms[:, 576:704], T.MT[:, 2304:2816], ["MTz"], ["mq2"])
     ms(T.RS[:, 127:128], 0.0, ["RS0"])
-    ms(T.Bs[:, 15:16], 0.0, ["Bs0"])
+    ms(T.Bs[:, 15:16], 0.0, ["Bsz"])
     ms(T.N1[:, 0:1], 255.0, ["N10"])
     ms(T.Y[:, 0:1], -256.0, ["Y0"])
     nz15, d15 = T.sm[:, 47:48], T.sm[:, 15:16]
@@ -242,11 +244,11 @@ def rank_program(g, core, T, topo):
 
     def unpack(b0, q, s, keys):
         for b in range(4):
-            mm(b0 + b, 256, T.eq[:, 128 * b:128 * b + 128], T.es[:, 128 * b:128 * b + 128], q[:], s[:], ["eq%d" % b] + keys)
+            mm(b0[b], 256, T.eq[:, 128 * b:128 * b + 128], T.es[:, 128 * b:128 * b + 128], q[:], s[:], ["eq%d" % b] + keys)
 
     def unpack_copy(b0, dst, key, bs):
         for b in bs:
-            act(dst[:, 256 * b:256 * b + 256], bank(b0 + b), F.Identity, ["P%d" % (b0 + b)], [key + str(b)], scale=0.5)
+            act(dst[:, 256 * b:256 * b + 256], bank(b0[b]), F.Identity, ["P%d" % b0[b]], [key + str(b)], scale=0.5)
 
     def sel16(out, v, R, W):
         scan(out, T.m16[:], v[:], 0.0, A.add, A.min, ["m16"] + R, W)
@@ -286,29 +288,32 @@ def rank_program(g, core, T, topo):
             accum_out=T.RS[:, 128 * k + 127:128 * k + 128])
 
     def splanes(ks):
-        s1(ks[0])
+        for k in ks[:2]:
+            s1(k)
         for n, k in enumerate(ks):
-            if n + 1 < len(ks):
-                s1(ks[n + 1])
+            if n + 2 < len(ks):
+                s1(ks[n + 2])
             s2(k)
 
     def state(r, a, b, keys):
         if r > 0:
-            vk = ["V%d%d" % (h, k) for h in range(2) for k in range(4)] + ["oL", "X%d0" % (r - 1), "X%d1" % (r - 1),
-                                                                          "X%d2" % (r - 1)]
+            vk = ["V%d%d" % (h, k) for h in range(2) for k in range(4)] + ["oL%d" % (a // 512), "X%d0" % (r - 1), "X%d1" % (r - 1),
+                                                                          "X%d2" % (r - 1), "X%d3" % (r - 1)]
             tt(T["X%d" % r][:, a:b], T.V[:].indirect(T.oL[:, a // 16:b // 16]), T["X%d" % (r - 1)][:, a:b], A.add, vk, keys)
 
     def quant(r, h):
         a, b = 128 * h, 128 * h + 128
         qz(T["xq%d" % r][:, a:b], T["xs%d" % r][:, a:b], T["X%d" % r][:, 4 * a:4 * b],
-           ["X%d0" % r] if h == 0 else ["X%d1" % r, "X%d2" % r], ["xq%d%d" % (r, h)])
+           ["X%d0" % r] if h == 0 else ["X%d1" % r, "X%d2" % r, "X%d3" % r], ["xq%d%d" % (r, h)])
 
     for r in range(3):
         peer = T.cores[rank ^ MASK[r]]
         xq, xs = T["xq%d" % r], T["xs%d" % r]
         xk = ["xq%d0" % r, "xq%d1" % r]
         lq, lsc, so, lo = T["lq%d" % r], T["ls%d" % r], T["so%d" % r], T["lo%d" % r]
+        U = 2.0 ** 80
         state(r, 0, 512, ["X%d0" % r])
+        state(r, 512, 640, ["X%d1" % r])
         quant(r, 0)
 
         def scores(b, j, lo_, hi_):
@@ -316,17 +321,27 @@ def rank_program(g, core, T, topo):
                (["upq", "ups"] if j == 0 else ["upq2", "ups2"]) + xk[lo_ // 128:hi_ // 128])
 
         scores(4, 0, 0, 128)
-        scores(5, 0, 0, 128)
         if r > 0:
             scores(6, 1, 0, 128)
+        scores(5, 0, 0, 128)
+        if r > 0:
             scores(7, 2, 0, 128)
-        state(r, 512, 768, ["X%d1" % r])
+        state(r, 640, 896, ["X%d2" % r])
         if r == 0:
             quant(r, 1)
         tt(T.Sm[:, 0:128], bank(4, 0, 128), T.mD[:, 0:128], A.mult, ["P4", "mD"], ["Sm0"])
+        state(r, 896, 1024, ["X%d3" % r])
         scan(T.Fs[:, 0:128], T.m0[:, 0:128], T.Sm[:, 0:128], 0.0, A.mult, A.add, ["m0", "Sm0"], ["F0"])
-        state(r, 768, 1024, ["X%d2" % r])
+        act(T.LP[:, 0:257], T.PF[:, 0:257], F.Identity, ["PF"], ["LP"])
+
+        def steps(a, b, R, tag):
+            act(T.Kp[:, a:b], T.thr[:, a:b], F.Identity, R, ["Kp" + tag], scale=511.0 / U, bias=-256.0)
+            act(T.Bs[:, 16 + a:16 + b], T.thr[:, a:b], F.Identity, R, ["Bs" + tag], scale=-512.0 / U, bias=256.0)
+
         if r > 0:
+            act(T.Kp[:, 128:256], bank(6, 0, 128), F.Sign, ["P6"], ["Kp"])
+            act(T.thr[:, 0:128], T.Kp[:, 128:256], F.Relu, ["Kp"], ["thr0"], scale=U)
+            steps(0, 128, ["thr0"], "0")
             quant(r, 1)
         else:
             cp(T.upq[:, 128:384].bitcast(dt.uint32), T.uq[:].bitcast(dt.uint32).indirect(T.ul[:, 8:24]), ["uq", "ul"], ["upq2"])
@@ -351,82 +366,83 @@ def rank_program(g, core, T, topo):
         arrives(peer, ["lo%d" % r], "al%d" % r, 1)
         splanes([7, 6, 5, 4, 3, 2, 1])
 
-        U = 2.0 ** 80
-        ts(T.thr[:, 0:128], bank(6, 0, 128), 0.0, U, A.is_gt, A.mult, ["P6"], ["thr0"])
+        if r == 0:
+            ts(T.thr[:, 0:128], bank(6, 0, 128), 0.0, U, A.is_gt, A.mult, ["P6"], ["thr0"])
         tt(pview(16, 0, 128), bank(4, 0, 128), T.Fs[:, 0:128], A.is_le, ["P4", "F0"], ["M16a"])
         tt(T.nt[:, 0:128], bank(7, 0, 128), T.thr[:, 0:128], A.is_le, ["P7", "thr0"], ["nt0"])
         ts(T.thr[:, 128:256], bank(2, 0, 128), 0.0, U, A.is_gt, A.mult, ["P2"], ["thr1"])
         tt(T.Sm[:, 128:256], bank(0, 128, 256), T.mD[:, 128:256], A.mult, ["P0", "mD"], ["Sm1"])
         tt(T.nt[:, 128:256], bank(3, 0, 128), T.thr[:, 128:256], A.is_le, ["P3", "thr1"], ["nt1"])
         scan(T.Fs[:, 128:256], T.m0[:, 128:256], T.Sm[:, 128:256], 0.0, A.mult, A.add, ["m0", "Sm1"], ["F1"])
-        act(T.Kp[:], T.thr[:], F.Identity, ["thr0", "thr1"], ["Kp"], scale=511.0 / U, bias=-256.0)
-        act(T.Bs[:, 16:272], T.thr[:], F.Identity, ["thr0", "thr1"], ["Bs"], scale=-512.0 / U, bias=256.0)
+        scan(T.DS[:, 0:128], T.m0[:, 0:128], pview(16, 0, 128), 0.0, A.mult, A.add, ["m0", "M16a"], ["DS0"])
+        steps(128 if r > 0 else 0, 256, ["thr0", "thr1"], "")
         act(T.al[:], T.nt[:], F.Identity, ["nt0", "nt1"], ["al"], scale=2.0, bias=-1.0)
         big = [k for k in range(15, 8, -1) if k not in VPL]
         splanes([8] + big[:YA])
-        vplane(VPL[0])
+        for k in VPL:
+            vplane(k)
         tt(pview(16, 128, 256), bank(0, 128, 256), T.Fs[:, 128:256], A.is_le, ["P0", "F1"], ["M16b"])
-        scan(T.Dn[:], T.Kp[:], T.Bs[:, 15:271], 0.0, A.add, A.add, ["Kp", "Bs", "Bs0"], ["Dn"])
-        scan(T.N1[:, 1:256], T.Kp[:, 0:255], T.Bs[:, 16:271], 255.0, A.add, A.add, ["Kp", "Bs"], ["N1"])
+        vsum(VPL[0])
+        scan(T.Dn[:], T.Kp[:], T.Bs[:, 15:271], 0.0, A.add, A.add, ["Kp", "Bs", "Kp0", "Bs0", "Bsz"], ["Dn"])
+        scan(T.N1[:, 1:256], T.Kp[:, 0:255], T.Bs[:, 16:271], 255.0, A.add, A.add, ["Kp", "Bs", "Kp0", "Bs0"], ["N1"])
+        vsum(VPL[1])
         scan(T.Y[:, 1:256], T.al[:, 0:255], T.Dn[:, 0:255], -256.0, A.mult, A.max, ["al", "Dn"], ["Y"])
         act(T.Ya[:], T.Y[:], F.Abs, ["Y", "Y0"], ["Ya"])
-        splanes(big[YA:])
-        for k in VPL[1:]:
-            vplane(k)
+        if big[YA:]:
+            splanes(big[YA:])
         if r == 0:
             late_a()
-        unpack(4, xq, xs, xk)
-        for k in VPL:
+        unpack(OWN, xq, xs, xk)
+        for k in VPL[2:]:
             vsum(k)
-        scan(T.DS[:], T.m0[:], pview(16, 0, 256), 0.0, A.mult, A.add, ["m0", "M16a", "M16b"], ["DS"])
+        scan(T.DS[:, 128:256], T.m0[:, 128:256], pview(16, 128, 256), 0.0, A.mult, A.add, ["m0", "M16b"], ["DS"])
         sel16(T.sN[:, 0:256], T.N1, ["N1", "N10"], ["sN"])
-        sel16(T.sN[:, 256:512], T.Ya, ["Ya"], ["sA"])
         qz(T.mq[:, 448:640], T.ms[:, 448:640], T.MT[:, 1792:2560], ["M%d" % k for k in range(1, 9)] + ["MTz"], ["mq2"])
         qz(T.mq[:, 0:256], T.ms[:, 0:256], T.MT[:, 0:1024], ["M16a", "M16b", "M15", "M14", "M13", "MTz"], ["mq0"])
         ones = (T.oq[:, 0:128], T.osn[:, 0:128])
         mm(2, 256, T.oq[:, 128:256], T.osn[:, 128:256], T.mq[:, 0:256], T.ms[:, 0:256], ["oq", "mq0"], True, False)
         mm(2, 128, *ones, T.mq[:, 448:576], T.ms[:, 448:576], ["oq", "mq2"], False, False)
         mm(2, 128, *ones, T.mq[:, 576:704], T.ms[:, 576:704], ["oq", "mq2"], False, False)
-        tt(T.y1[:], T.CC[:], T.DS[:, 15::16], A.subtract, ["CC", "DS"], ["y1"])
+        tt(T.y1[:], T.CC[:], T.DS[:, 15::16], A.subtract, ["CC", "DS", "DS0"], ["y1"])
         qz(T.mq[:, 256:448], T.ms[:, 256:448], T.MT[:, 1024:1792], ["M12", "M11", "M10", "M9", "MTz"], ["mq1"])
         mm(2, 192, *ones, T.mq[:, 256:448], T.ms[:, 256:448], ["oq", "mq1"], False, True)
         tt(T.mp[:, 15::16], T.y1[:], T.RS[:, 127::128], A.subtract, ["y1"] + ["RS%d" % k for k in range(16)], ["mp"])
-        ts(T.PL[:], T.sN[:, 15::16], -1.0, col(8), A.mult, A.add, ["sN", "sA", "c8"], ["PL1", "PL2"])
+        sel16(T.sN[:, 256:512], T.Ya, ["Ya"], ["sA"])
         scan(T.rr[:, 0:255], T.nt[:, 0:255], T.nt[:, 0:255], 0.0, A.mult, A.add, ["nt0", "nt1"], ["rr"])
-        scan(T.sel[:], bank(2), T.mp[:], 2048.0, A.min, A.add, ["P2", "mp"], ["sel"])
-        ts(T.pos[:], T.sel[:, 15::16], -1024.0, None, A.add, None, ["sel"], ["pos"])
-        cp(T.O[:, 0:256].indirect(T.pos[:]), T.PF[:, 0:256], ["pos", "PF"], ["O"])
+        ts(T.PL[:], T.sN[:, 15::16], -1.0, col(8), A.mult, A.add, ["sN", "sA", "c8"], ["PL1", "PL2"])
+        act(T.Yp[:], T.Y[:], F.Relu, ["Y", "Y0"], ["Yp"], scale=-1.0)
         if r == 0:
             late_s()
-        act(T.Yp[:], T.Y[:], F.Relu, ["Y", "Y0"], ["Yp"], scale=-1.0)
-        act(T.Bp[:], T.Bs[:, 16:272], F.Relu, ["Bs"], ["Bp"], scale=-2.0)
-        act(T.CR[:, 271:272], T.rr[:, 254:255], F.Abs, ["rr"], ["CRx"], scale=-1.0, bias=254.0)
-        act(T.LP[:, 0:257], T.PF[:, 0:257], F.Identity, ["PF"], ["LP"])
-        unpack_copy(4, T.To, "To", (0, 1, 2, 3))
-        unpack(0, lq, lsc, ["lq%d" % r])
+            late_b()
+        act(T.Bp[:], T.Bs[:, 16:272], F.Relu, ["Bs", "Bs0"], ["Bp"], scale=-2.0)
         w = [T.w1[:, 16 * n:16 * n + 16] for n in range(5)]
+        ts(T.w1[:, 80:81], T.Y[:, 255:256], T.N1[:, 255:256], T.sm[:, 160:161], A.max, A.min, ["Y", "N1", "c5"], ["w5"])
+        scan(T.sel[:], bank(2), T.mp[:], 2048.0, A.min, A.add, ["P2", "mp"], ["sel"])
+        sel16(T.sY[:], T.Yp, ["Yp"], ["sY"])
+        ts(T.pos[:], T.sel[:, 15::16], -1024.0, None, A.add, None, ["sel"], ["pos"])
+        scan(T.sB[:], T.m32[:], T.Bp[:], 0.0, A.add, A.min, ["m32", "Bp"], ["sB"])
+        cp(T.O[:, 0:256].indirect(T.pos[:]), T.PF[:, 0:256], ["pos", "PF"], ["O"])
+        tt(w[1], T.sY[:, 15::16], T.sN[:, 15:256:16], A.max, ["sY", "sN"], ["w1"])
+        tt(w[3], T.sB[:, 15::16], T.DUM[:], A.add, ["sB", "DUM"], ["w3"])
+        unpack_copy(OWN, T.To, "To", (0, 1, 2, 3))
+        unpack(FAR, lq, lsc, ["lq%d" % r])
+        unpack_copy(FAR, T.Tp, "Tp", TP[0])
         act(T.AB[:, 0:128], T.O[:, 0:256].indirect(T.PL[:, 0:8]), F.Identity, ["O", "PL1"], ["AB0"])
         cp(T.AB[:, 128:256], T.O[:, 0:256].indirect(T.PL[:, 16:24]), ["O", "PL2"], ["AB1"])
         act(T.O[:, 256:257], T.O[:, 0:1], F.Identity, ["O"], ["Ox"])
         act(T.AB[:, 384:512], T.O[:, 0:256].indirect(T.PL[:, 24:32]), F.Identity, ["O", "PL2"], ["AB3"])
         act(T.AB[:, 256:384], T.O[:, 0:257].indirect(T.PL[:, 8:16]), F.Identity, ["O", "Ox", "PL1"], ["AB2"])
-        unpack_copy(0, T.Tp, "Tp", (0,))
-        sel16(T.sY[:], T.Yp, ["Yp"], ["sY"])
+        act(T.CR[:, 271:272], T.rr[:, 254:255], F.Abs, ["rr"], ["CRx"], scale=-1.0, bias=254.0)
+        unpack_copy(FAR, T.Tp, "Tp", TP[1])
+        tt(w[4], w[1], w[3], A.min, ["w1", "w3"], ["w4"])
         scan(T.s4[:, 0:256], T.m4[:], T.AB[:, 0:256], 0.0, A.add, A.min, ["m4", "AB0", "AB1"], ["s40"])
-        scan(T.sB[:], T.m32[:], T.Bp[:], 0.0, A.add, A.min, ["m32", "Bp"], ["sB"])
+        ts(T.TG[:, 0:17], T.w1[:, 64:81], -1.0, col(8), A.mult, A.add, ["w4", "w5", "c8"], ["TG0"])
         ts(so[:], T.s4[:, 3:256:4], col(1), None, A.add, None, ["s40", "c1"], ["so%d" % r])
         send(peer, lo[:], so[:], ["so%d" % r], "al%d" % r)
         if r == 0:
-            late_b()
-        tt(w[1], T.sY[:, 15::16], T.sN[:, 15:256:16], A.max, ["sY", "sN"], ["w1"])
-        tt(w[3], T.sB[:, 15::16], T.DUM[:], A.add, ["sB", "DUM"], ["w3"])
-        ts(T.w1[:, 80:81], T.Y[:, 255:256], T.N1[:, 255:256], T.sm[:, 160:161], A.max, A.min, ["Y", "N1", "c5"], ["w5"])
-        scan(T.s4[:, 256:512], T.m4[:], T.AB[:, 256:512], 0.0, A.add, A.min, ["m4", "AB2", "AB3"], ["s41"])
-        tt(w[4], w[1], w[3], A.min, ["w1", "w3"], ["w4"])
-        ts(T.oH[:], T.s4[:, 259:512:4], col(1), None, A.add, None, ["s41", "c1"], ["oH"])
-        ts(T.TG[:, 0:17], T.w1[:, 64:81], -1.0, col(8), A.mult, A.add, ["w4", "w5", "c8"], ["TG0"])
-        if r == 0:
             qz(T.vq[:], T.vs[:], T.vb[:], ["vb"], ["vq"])
+        scan(T.s4[:, 256:512], T.m4[:], T.AB[:, 256:512], 0.0, A.add, A.min, ["m4", "AB2", "AB3"], ["s41"])
+        ts(T.oH[:], T.s4[:, 259:512:4], col(1), None, A.add, None, ["s41", "c1"], ["oH"])
         cp(T.LP[:].indirect(T.TG[:, 0:17]), T.CR[:], ["TG0", "CR", "CRx"], ["LP"])
 
         def gather_b(h, Tw, tk, off, ok):
@@ -435,11 +451,12 @@ def rank_program(g, core, T, topo):
                 act(T.Zb[:, a:a + 256], Tw[:].indirect(off[:, 32 + 16 * n:48 + 16 * n]), F.Identity,
                     [tk + str(b) for b in range(4)] + [ok], ["Zb%d%d" % (h, n)])
 
-        def gather_a(h, Tw, tk, off, ok):
-            for n in range(2):
-                a = 512 * h + 256 * n
-                tt(T.Z[:, a:a + 256], Tw[:].indirect(off[:, 16 * n:16 * n + 16]), T.Zb[:, a:a + 256], A.add,
-                   [tk + str(b) for b in range(4)] + [ok, "Zb%d%d" % (h, n)], ["Z%d%d" % (h, n)])
+        def gather_a(h, n, Tw, tk, off, ok):
+            a = 512 * h + 256 * n
+            tt(T.Z[:, a:a + 256], Tw[:].indirect(off[:, 16 * n:16 * n + 16]), T.Zb[:, a:a + 256], A.add,
+               [tk + str(b) for b in range(4)] + [ok, "Zb%d%d" % (h, n)], ["Z%d%d" % (h, n)])
+
+        def quant_z(h):
             qz(T.zq[:, 128 * h:128 * h + 128], T.zs[:, 128 * h:128 * h + 128], T.Z[:, 512 * h:512 * h + 512],
                ["Z%d0" % h, "Z%d1" % h], ["zq%d" % h])
 
@@ -455,32 +472,37 @@ def rank_program(g, core, T, topo):
             else:
                 ts(out, bank(b, 0, 128), 0.03125, None, A.mult, None, ["P%d" % b], ["V%d%d" % (h, k)])
 
+        lk = "lo%d" % r
         gather_b(1, T.To, "To", T.oH, "oH")
-        unpack_copy(0, T.Tp, "Tp", (1,))
         act(T.LP[:, 0:1], T.LP[:, 0:1], F.Identity, ["LP"], ["LP"], bias=T.LP[:, 256:257])
-        unpack_copy(0, T.Tp, "Tp", (2, 3))
-        gather_a(1, T.To, "To", T.oH, "oH")
+        gather_b(0, T.Tp, "Tp", lo, lk)
+        gather_a(1, 0, T.To, "To", T.oH, "oH")
+        gather_a(1, 1, T.To, "To", T.oH, "oH")
+        cp(T.LR[:, 0:128], T.LP[:, 0:256].indirect(T.pos[:, 0:8]), ["LP", "pos"], ["LR0"])
+        quant_z(1)
         layer(1, 4)
-        cp(T.LR[:], T.LP[:, 0:256].indirect(T.pos[:]), ["LP", "pos"], ["LR"])
-        gather_b(0, T.Tp, "Tp", lo, "lo%d" % r)
-        for k in range(NV):
-            vcopy("v", 1, k, 4 + k)
-        gather_a(0, T.Tp, "Tp", lo, "lo%d" % r)
-        for k in range(NV, 4):
+        gather_a(0, 0, T.Tp, "Tp", lo, lk)
+        gather_a(0, 1, T.Tp, "Tp", lo, lk)
+        for k in range(4):
             vcopy("s", 1, k, 4 + k)
+        scan(T.sL[:, 0:128], T.m4[:, 0:128], T.LR[:, 0:128], 0.0, A.add, A.min, ["m4", "LR0"], ["sL0"])
+        quant_z(0)
         layer(0, 0)
-        scan(T.sL[:], T.m4[:], T.LR[:], 0.0, A.add, A.min, ["m4", "LR"], ["sL"])
-        vcopy("s", 0, 0, 0)
-        ts(T.oL[:], T.sL[:, 3:256:4], col(1), None, A.add, None, ["sL", "c1"], ["oL"])
-        vcopy("v", 0, 1, 1)
-        vcopy("s", 0, 2, 2)
-        vcopy("v", 0, 3, 3)
+        cp(T.LR[:, 128:256], T.LP[:, 0:256].indirect(T.pos[:, 8:16]), ["LP", "pos"], ["LR1"])
+        ts(T.oL[:, 0:32], T.sL[:, 3:128:4], col(1), None, A.add, None, ["sL0", "c1"], ["oL0"])
+        scan(T.sL[:, 128:256], T.m4[:, 128:256], T.LR[:, 128:256], 0.0, A.add, A.min, ["m4", "LR1"], ["sL1"])
+        for k in range(4):
+            vcopy("v" if k in NV else "s", 0, k, k)
+        ts(T.oL[:, 32:64], T.sL[:, 131:256:4], col(1), None, A.add, None, ["sL1", "c1"], ["oL1"])
 
-    act(T.LF[:], T.LR[:], F.Identity, ["LR"], ["LF"])
+    act(T.LF[:], T.LR[:], F.Identity, ["LR0", "LR1"], ["LF"])
     dma("y", T.lb[:], T.LF[0:128:16, :], ["LF"], ["lb"], "o1")
+    state(3, 0, 512, ["X30"])
+    state(3, 512, 640, ["X31"])
     for h in range(2):
         a, b = 128 * h, 128 * h + 128
-        state(3, 4 * a, 4 * b, ["X3%d" % h])
+        if h == 1:
+            state(3, 640, 1024, ["X32"])
         quant(3, h)
         key = "xq3%d" % h
         mm(4 + h, 128, T.vq[:], T.vs[:], T.xq3[:, a:b], T.xs3[:, a:b], ["vq", key])

@@ -3,8 +3,9 @@ from concourse.mybir import dt, AluOpType, ActivationFunctionType
 A = AluOpType
 F = ActivationFunctionType
 MASK = [1, 2, 4]
-VPL = (15, 14, 13, 9)
-YA, NV = 4, (1, 3)
+VPL = (15, 14, 9)
+YA, NV = 9, (1, 3)
+VLO, SPLIT = (7, 6), (2, 4)
 OWN, FAR = (4, 5, 6, 7), (0, 1, 3, 2)
 TP = ((0, 1), (2, 3))
 BF, F32, I32, U16, Q4, U8 = "bfloat16", "float32", "int32", "uint16", "float8_e4m3fn_x4", "uint8"
@@ -166,10 +167,12 @@ def rank_program(g, core, T, topo):
     iota(T.PF[:, 256:257], [[0, 1]], 0, 0, ["PF"], True)
     iota(T.CR[:], [[1, 272]], 0, 0, ["CR", "CRx"], True)
 
-    for a, b in ((2112, 2816), (832, 1024), (1600, 1792)):
-        ms(T.MT[:, a:b], 0.0, ["MTz"])
+    ms(T.MT[:, 2112:2816], 0.0, ["MTy"])
+    ms(T.MT[:, 832:1024], 0.0, ["MTx"])
+    ms(T.eb[:], 0.0, ["eb"])
     ts(T.i2[:], T.i1[:], 15, None, A.bitwise_and, None, ["i1a", "i1b"], ["i2"])
     ts(T.pc[:, 1:2], T.i1[:, 16:17], 4, None, A.arith_shift_right, None, ["i1b"], ["pc1"])
+    ms(T.MT[:, 1600:1792], 0.0, ["MTz"])
     cp(T.il[:], T.i2[:, 16:32], ["i2"], ["il"])
     ts(sm(1), T.i2[:, 0:16], 0.0, None, A.is_equal, None, ["i2"], ["sm1"])
     ts(sm(2), T.i2[:, 0:16], 0.0, None, A.not_equal, None, ["i2"], ["sm2"])
@@ -185,7 +188,9 @@ def rank_program(g, core, T, topo):
     ts(sm(6), T.i2[:, 0:16], 15.0, 1024.0, A.is_equal, A.mult, ["i2"], ["sm6"])
     ts(sm(7), T.i2[:, 0:16], 0.0, -512.0, A.is_equal, A.mult, ["i2"], ["sm7"])
     act(T.m16[:], sm(5).indirect(T.il[:]), F.Identity, ["sm5", "il"], ["m16"])
-    ms(T.eb[:], 0.0, ["eb"])
+    ts(col(14), T.i1[:, 16:17], col(7), None, A.subtract, None, ["i1b", "c7"], ["c14"])
+    ts(T.pc[:, 3:4], T.i1[:, 16:17], 3, None, A.bitwise_and, None, ["i1b"], ["pc3"])
+    ms(T.RS[:, 127:128], 0.0, ["RS0"])
     tt(sm(8), sm(6), sm(7), A.add, ["sm6", "sm7"], ["sm8"])
     for t in range(4):
         ts(T.ob[:, t:512:4], T.gi[:], col(6), None, A.is_equal, None, ["gi", "c6"], ["ob0%d" % t])
@@ -195,38 +200,41 @@ def rank_program(g, core, T, topo):
     act(T.ob[:, 512:1024], T.ob[:, 0:512], F.Identity, ob0, ["ob1"])
     op("g", lambda: g.affine_select(T.ob[:, 512:1024:4], T.ob[:, 512:1024:4], [[1, 128]], A.is_gt, 0.0, 0, -1),
        ["ob1"], ["ob1"])
-    qz(T.mq[:, 576:704], T.ms[:, 576:704], T.MT[:, 2304:2816], ["MTz"], ["mq2"])
-    ms(T.RS[:, 127:128], 0.0, ["RS0"])
+    qz(T.mq[:, 576:704], T.ms[:, 576:704], T.MT[:, 2304:2816], ["MTx", "MTy", "MTz"], ["mq2"])
+    nz15, d15 = T.sm[:, 47:48], T.sm[:, 15:16]
+    ts(T.i4[:], T.i1[:, 0:16], col(14), None, A.add, None, ["i1a", "c14"], ["i4"])
+    ts(col(9), nz15, 512.0, d15, A.mult, A.add, ["sm2", "sm0"], ["c9"])
+
+    def quant_e(b):
+        qz(T.eq[:, 128 * b:128 * b + 128], T.es[:, 128 * b:128 * b + 128], T.eb[:, 3 - b:515 - b], ["eb"], ["eq%d" % b])
+
+    quant_e(0)
+    ts(T.i5[:], T.i4[:], 3, None, A.bitwise_and, None, ["i4"], ["i5"])
+    quant_e(1)
+    ts(T.CC[:], T.k16[:], 1025.0, col(9), A.add, A.add, ["k16", "c9"], ["CC"])
+    ts(sm(3), T.i5[:], 0.0, 1024.0, A.is_equal, A.mult, ["i5"], ["sm3"])
+    ts(sm(4), T.i5[:], 1.0, -256.0, A.is_equal, A.mult, ["i5"], ["sm4"])
+
+    qz(T.uq[:], T.us[:], T.ub[:], ["ub"], ["uq"])
+    tt(sm(9), sm(3), sm(4), A.add, ["sm3", "sm4"], ["sm9"])
     ms(T.Bs[:, 15:16], 0.0, ["Bsz"])
     ms(T.N1[:, 0:1], 255.0, ["N10"])
     ms(T.Y[:, 0:1], -256.0, ["Y0"])
-    nz15, d15 = T.sm[:, 47:48], T.sm[:, 15:16]
-    for b in range(2):
-        qz(T.eq[:, 128 * b:128 * b + 128], T.es[:, 128 * b:128 * b + 128], T.eb[:, 3 - b:515 - b], ["eb"], ["eq%d" % b])
-
-    ts(col(14), T.i1[:, 16:17], col(7), None, A.subtract, None, ["i1b", "c7"], ["c14"])
-    ts(col(9), nz15, 512.0, d15, A.mult, A.add, ["sm2", "sm0"], ["c9"])
-    ts(T.i4[:], T.i1[:, 0:16], col(14), None, A.add, None, ["i1a", "c14"], ["i4"])
-    ts(T.CC[:], T.k16[:], 1025.0, col(9), A.add, A.add, ["k16", "c9"], ["CC"])
-    ts(T.i5[:], T.i4[:], 3, None, A.bitwise_and, None, ["i4"], ["i5"])
-    ts(T.pc[:, 3:4], T.i1[:, 16:17], 3, None, A.bitwise_and, None, ["i1b"], ["pc3"])
-
-    qz(T.uq[:], T.us[:], T.ub[:], ["ub"], ["uq"])
     act(T.ups[:, 0:128], T.us[:].indirect(T.ul[:, 0:8]), F.Copy, ["uq", "ul"], ["ups"])
     cp(T.upq[:, 0:128].bitcast(dt.uint32), T.uq[:].bitcast(dt.uint32).indirect(T.ul[:, 0:8]), ["uq", "ul"], ["upq"])
     act(T.ups[:, 128:384], T.us[:].indirect(T.ul[:, 8:24]), F.Copy, ["uq", "ul"], ["ups2"])
     act(col(0), nz15, F.Identity, ["sm2"], ["c0"], scale=256.0)
     act(col(8), nz15, F.Identity, ["sm2"], ["c8"], scale=-256.0, bias=256.0)
+    act(col(11), T.sm[:, 31:32], F.Identity, ["sm1"], ["c11"], scale=2000.0)
+    act(col(12), T.sm[:, 31:32], F.Identity, ["sm1"], ["c12"], scale=2000.0, bias=-576.0)
+    act(T.m4[:], sm(9).indirect(T.il[:]), F.Identity, ["sm9", "il"], ["m4"])
 
     def early_a():
-        ts(sm(3), T.i5[:], 0.0, 1024.0, A.is_equal, A.mult, ["i5"], ["sm3"])
-        ts(sm(4), T.i5[:], 1.0, -256.0, A.is_equal, A.mult, ["i5"], ["sm4"])
         ts(col(13), T.i5[:, 3:4], 0.0, 256.0, A.not_equal, A.mult, ["i5"], ["c13"])
-        tt(sm(9), sm(3), sm(4), A.add, ["sm3", "sm4"], ["sm9"])
+        quant_e(2)
 
     def late_a():
-        for b in range(2, 4):
-            qz(T.eq[:, 128 * b:128 * b + 128], T.es[:, 128 * b:128 * b + 128], T.eb[:, 3 - b:515 - b], ["eb"], ["eq%d" % b])
+        quant_e(3)
         qz(T.oq[:], T.osn[:], T.ob[:], ob0 + ["ob1"], ["oq"])
         ts(col(1), T.pc[:, 3:4], 256.0, col(13), A.mult, A.add, ["pc3", "c13"], ["c1"])
         ts(col(10), d15, col(0), -16.0, A.add, A.add, ["sm0", "c0"], ["c10"])
@@ -237,10 +245,7 @@ def rank_program(g, core, T, topo):
         ts(T.DUM[:, 15:16], T.DUM[:, 15:16], col(11), None, A.add, None, ["c11", "DUM"], ["DUM"])
 
     def late_s():
-        act(T.m4[:], sm(9).indirect(T.il[:]), F.Identity, ["sm9", "il"], ["m4"])
         act(T.m32[:], T.m16[:], F.Identity, ["m16"], ["m32"], scale=2.0)
-        act(col(11), T.sm[:, 31:32], F.Identity, ["sm1"], ["c11"], scale=2000.0)
-        act(col(12), T.sm[:, 31:32], F.Identity, ["sm1"], ["c12"], scale=2000.0, bias=-576.0)
 
     def unpack(b0, q, s, keys):
         for b in range(4):
@@ -267,7 +272,8 @@ def rank_program(g, core, T, topo):
         return "F1" if k >= 8 else "F0"
 
     def vplane(k):
-        ts(pview(k, 0, 16 * k), bank(0, 0, 16 * k), rcol(k), None, A.is_lt, None, ["P0", fkey(k), "MTz"], ["M%d" % k])
+        b = 4 if k < 8 else 0
+        ts(pview(k, 0, 16 * k), bank(b, 0, 16 * k), rcol(k), None, A.is_lt, None, ["P%d" % b, fkey(k), "MTz"], ["M%d" % k])
 
     def vsum(k):
         scan(T.RS[:, 128 * k + 128 - 8 * k:128 * k + 128], pview(k, 0, 8 * k), pview(k, 8 * k, 16 * k), 0.0,
@@ -326,36 +332,28 @@ def rank_program(g, core, T, topo):
         scores(5, 0, 0, 128)
         if r > 0:
             scores(7, 2, 0, 128)
-        state(r, 640, 896, ["X%d2" % r])
+        state(r, 640, 960, ["X%d2" % r])
         if r == 0:
             quant(r, 1)
-        tt(T.Sm[:, 0:128], bank(4, 0, 128), T.mD[:, 0:128], A.mult, ["P4", "mD"], ["Sm0"])
-        state(r, 896, 1024, ["X%d3" % r])
-        scan(T.Fs[:, 0:128], T.m0[:, 0:128], T.Sm[:, 0:128], 0.0, A.mult, A.add, ["m0", "Sm0"], ["F0"])
-        act(T.LP[:, 0:257], T.PF[:, 0:257], F.Identity, ["PF"], ["LP"])
-
-        def steps(a, b, R, tag):
-            act(T.Kp[:, a:b], T.thr[:, a:b], F.Identity, R, ["Kp" + tag], scale=511.0 / U, bias=-256.0)
-            act(T.Bs[:, 16 + a:16 + b], T.thr[:, a:b], F.Identity, R, ["Bs" + tag], scale=-512.0 / U, bias=256.0)
-
-        if r > 0:
-            act(T.Kp[:, 128:256], bank(6, 0, 128), F.Sign, ["P6"], ["Kp"])
-            act(T.thr[:, 0:128], T.Kp[:, 128:256], F.Relu, ["Kp"], ["thr0"], scale=U)
-            steps(0, 128, ["thr0"], "0")
-            quant(r, 1)
-        else:
             cp(T.upq[:, 128:384].bitcast(dt.uint32), T.uq[:].bitcast(dt.uint32).indirect(T.ul[:, 8:24]), ["uq", "ul"], ["upq2"])
-            scores(0, 0, 0, 256)
-            scores(1, 0, 0, 256)
             scores(6, 1, 0, 128)
             scores(7, 2, 0, 128)
+        tt(T.Sm[:, 0:128], bank(4, 0, 128), T.mD[:, 0:128], A.mult, ["P4", "mD"], ["Sm0"])
+        state(r, 960, 1024, ["X%d3" % r])
+        if r == 0:
             early_a()
+        else:
+            ts(T.thr[:, 0:128], bank(6, 0, 128), 0.0, U, A.is_gt, A.mult, ["P6"], ["thr0"])
+        scan(T.Fs[:, 0:128], T.m0[:, 0:128], T.Sm[:, 0:128], 0.0, A.mult, A.add, ["m0", "Sm0"], ["F0"])
+        if r > 0:
+            act(T.LP[:, 0:257], T.PF[:, 0:257], F.Identity, ["PF"], ["LP"])
+            quant(r, 1)
+        else:
+            ts(T.thr[:, 0:128], bank(6, 0, 128), 0.0, U, A.is_gt, A.mult, ["P6"], ["thr0"])
         scores(2, 1, 128, 256)
-        if r > 0:
-            scores(0, 0, 0, 256)
+        scores(0, 0, 0, 256)
         scores(3, 2, 128, 256)
-        if r > 0:
-            scores(1, 0, 0, 256)
+        scores(1, 0, 0, 256)
         if r == 0:
             send(peer, lq[:].bitcast(dt.uint8), xq[:].bitcast(dt.uint8), xk, "aq%d" % r)
         else:
@@ -364,19 +362,23 @@ def rank_program(g, core, T, topo):
         send(peer, lsc[:], xs[:], xk, "aq%d" % r)
         arrives(peer, ["lq%d" % r], "aq%d" % r, 2 if r == 0 else 3)
         arrives(peer, ["lo%d" % r], "al%d" % r, 1)
-        splanes([7, 6, 5, 4, 3, 2, 1])
+        splanes([k for k in range(7, 0, -1) if k not in VLO])
 
-        if r == 0:
-            ts(T.thr[:, 0:128], bank(6, 0, 128), 0.0, U, A.is_gt, A.mult, ["P6"], ["thr0"])
         tt(pview(16, 0, 128), bank(4, 0, 128), T.Fs[:, 0:128], A.is_le, ["P4", "F0"], ["M16a"])
         tt(T.nt[:, 0:128], bank(7, 0, 128), T.thr[:, 0:128], A.is_le, ["P7", "thr0"], ["nt0"])
+        for k in VLO:
+            vplane(k)
         ts(T.thr[:, 128:256], bank(2, 0, 128), 0.0, U, A.is_gt, A.mult, ["P2"], ["thr1"])
+        scan(T.DS[:, 0:128], T.m0[:, 0:128], pview(16, 0, 128), 0.0, A.mult, A.add, ["m0", "M16a"], ["DS0"])
         tt(T.Sm[:, 128:256], bank(0, 128, 256), T.mD[:, 128:256], A.mult, ["P0", "mD"], ["Sm1"])
         tt(T.nt[:, 128:256], bank(3, 0, 128), T.thr[:, 128:256], A.is_le, ["P3", "thr1"], ["nt1"])
+        vsum(VLO[0])
         scan(T.Fs[:, 128:256], T.m0[:, 128:256], T.Sm[:, 128:256], 0.0, A.mult, A.add, ["m0", "Sm1"], ["F1"])
-        scan(T.DS[:, 0:128], T.m0[:, 0:128], pview(16, 0, 128), 0.0, A.mult, A.add, ["m0", "M16a"], ["DS0"])
-        steps(128 if r > 0 else 0, 256, ["thr0", "thr1"], "")
-        act(T.al[:], T.nt[:], F.Identity, ["nt0", "nt1"], ["al"], scale=2.0, bias=-1.0)
+        for k in VLO[1:]:
+            vsum(k)
+        act(T.Kp[:], T.thr[:], F.Identity, ["thr0", "thr1"], ["Kp"], scale=511.0 / U, bias=-256.0)
+        act(T.Bs[:, 16:272], T.thr[:], F.Identity, ["thr0", "thr1"], ["Bs"], scale=-512.0 / U, bias=256.0)
+        ts(T.al[:], T.nt[:], 2.0, -1.0, A.mult, A.add, ["nt0", "nt1"], ["al"])
         big = [k for k in range(15, 8, -1) if k not in VPL]
         splanes([8] + big[:YA])
         for k in VPL:
@@ -396,7 +398,6 @@ def rank_program(g, core, T, topo):
         for k in VPL[2:]:
             vsum(k)
         scan(T.DS[:, 128:256], T.m0[:, 128:256], pview(16, 128, 256), 0.0, A.mult, A.add, ["m0", "M16b"], ["DS"])
-        sel16(T.sN[:, 0:256], T.N1, ["N1", "N10"], ["sN"])
         qz(T.mq[:, 448:640], T.ms[:, 448:640], T.MT[:, 1792:2560], ["M%d" % k for k in range(1, 9)] + ["MTz"], ["mq2"])
         qz(T.mq[:, 0:256], T.ms[:, 0:256], T.MT[:, 0:1024], ["M16a", "M16b", "M15", "M14", "M13", "MTz"], ["mq0"])
         ones = (T.oq[:, 0:128], T.osn[:, 0:128])
@@ -407,43 +408,53 @@ def rank_program(g, core, T, topo):
         qz(T.mq[:, 256:448], T.ms[:, 256:448], T.MT[:, 1024:1792], ["M12", "M11", "M10", "M9", "MTz"], ["mq1"])
         mm(2, 192, *ones, T.mq[:, 256:448], T.ms[:, 256:448], ["oq", "mq1"], False, True)
         tt(T.mp[:, 15::16], T.y1[:], T.RS[:, 127::128], A.subtract, ["y1"] + ["RS%d" % k for k in range(16)], ["mp"])
+        sel16(T.sN[:, 0:256], T.N1, ["N1", "N10"], ["sN"])
         sel16(T.sN[:, 256:512], T.Ya, ["Ya"], ["sA"])
-        scan(T.rr[:, 0:255], T.nt[:, 0:255], T.nt[:, 0:255], 0.0, A.mult, A.add, ["nt0", "nt1"], ["rr"])
-        ts(T.PL[:], T.sN[:, 15::16], -1.0, col(8), A.mult, A.add, ["sN", "sA", "c8"], ["PL1", "PL2"])
         act(T.Yp[:], T.Y[:], F.Relu, ["Y", "Y0"], ["Yp"], scale=-1.0)
         if r == 0:
             late_s()
             late_b()
-        act(T.Bp[:], T.Bs[:, 16:272], F.Relu, ["Bs", "Bs0"], ["Bp"], scale=-2.0)
+        act(T.Bp[:], T.Bs[:, 16:272], F.Relu, ["Bs"], ["Bp"], scale=-2.0)
         w = [T.w1[:, 16 * n:16 * n + 16] for n in range(5)]
-        ts(T.w1[:, 80:81], T.Y[:, 255:256], T.N1[:, 255:256], T.sm[:, 160:161], A.max, A.min, ["Y", "N1", "c5"], ["w5"])
-        scan(T.sel[:], bank(2), T.mp[:], 2048.0, A.min, A.add, ["P2", "mp"], ["sel"])
+        scan(T.rr[:, 0:255], T.nt[:, 0:255], T.nt[:, 0:255], 0.0, A.mult, A.add, ["nt0", "nt1"], ["rr"])
         sel16(T.sY[:], T.Yp, ["Yp"], ["sY"])
-        ts(T.pos[:], T.sel[:, 15::16], -1024.0, None, A.add, None, ["sel"], ["pos"])
+        scan(T.sel[:], bank(2), T.mp[:], 2048.0, A.min, A.add, ["P2", "mp"], ["sel"])
         scan(T.sB[:], T.m32[:], T.Bp[:], 0.0, A.add, A.min, ["m32", "Bp"], ["sB"])
-        cp(T.O[:, 0:256].indirect(T.pos[:]), T.PF[:, 0:256], ["pos", "PF"], ["O"])
+        ts(T.PL[:], T.sN[:, 15::16], -1.0, col(8), A.mult, A.add, ["sN", "sA", "c8"], ["PL1", "PL2"])
+        ts(T.pos[:], T.sel[:, 15::16], -1024.0, None, A.add, None, ["sel"], ["pos"])
         tt(w[1], T.sY[:, 15::16], T.sN[:, 15:256:16], A.max, ["sY", "sN"], ["w1"])
+        ts(T.w1[:, 80:81], T.Y[:, 255:256], T.N1[:, 255:256], T.sm[:, 160:161], A.max, A.min, ["Y", "N1", "c5"], ["w5"])
         tt(w[3], T.sB[:, 15::16], T.DUM[:], A.add, ["sB", "DUM"], ["w3"])
+        cp(T.O[:, 0:256].indirect(T.pos[:]), T.PF[:, 0:256], ["pos", "PF"], ["O"])
+        tt(w[4], w[1], w[3], A.min, ["w1", "w3"], ["w4"])
+        if r == 0:
+            act(T.LP[:, 0:257], T.PF[:, 0:257], F.Identity, ["PF"], ["LP"])
         unpack_copy(OWN, T.To, "To", (0, 1, 2, 3))
         unpack(FAR, lq, lsc, ["lq%d" % r])
+        act(T.CR[:, 271:272], T.rr[:, 254:255], F.Abs, ["rr"], ["CRx"], scale=-1.0, bias=254.0)
         unpack_copy(FAR, T.Tp, "Tp", TP[0])
         act(T.AB[:, 0:128], T.O[:, 0:256].indirect(T.PL[:, 0:8]), F.Identity, ["O", "PL1"], ["AB0"])
         cp(T.AB[:, 128:256], T.O[:, 0:256].indirect(T.PL[:, 16:24]), ["O", "PL2"], ["AB1"])
         act(T.O[:, 256:257], T.O[:, 0:1], F.Identity, ["O"], ["Ox"])
         act(T.AB[:, 384:512], T.O[:, 0:256].indirect(T.PL[:, 24:32]), F.Identity, ["O", "PL2"], ["AB3"])
         act(T.AB[:, 256:384], T.O[:, 0:257].indirect(T.PL[:, 8:16]), F.Identity, ["O", "Ox", "PL1"], ["AB2"])
-        act(T.CR[:, 271:272], T.rr[:, 254:255], F.Abs, ["rr"], ["CRx"], scale=-1.0, bias=254.0)
         unpack_copy(FAR, T.Tp, "Tp", TP[1])
-        tt(w[4], w[1], w[3], A.min, ["w1", "w3"], ["w4"])
-        scan(T.s4[:, 0:256], T.m4[:], T.AB[:, 0:256], 0.0, A.add, A.min, ["m4", "AB0", "AB1"], ["s40"])
+        def balls(a, b):
+            cp(T.LP[:].indirect(T.TG[:, a:b]), T.CR[:, 16 * a:16 * b], ["TG0", "CR"] + (["CRx"] if b == 17 else []), ["LP"])
+
         ts(T.TG[:, 0:17], T.w1[:, 64:81], -1.0, col(8), A.mult, A.add, ["w4", "w5", "c8"], ["TG0"])
+        scan(T.s4[:, 0:256], T.m4[:], T.AB[:, 0:256], 0.0, A.add, A.min, ["m4", "AB0", "AB1"], ["s40"])
+        if SPLIT[0]:
+            balls(0, SPLIT[0])
         ts(so[:], T.s4[:, 3:256:4], col(1), None, A.add, None, ["s40", "c1"], ["so%d" % r])
         send(peer, lo[:], so[:], ["so%d" % r], "al%d" % r)
         if r == 0:
             qz(T.vq[:], T.vs[:], T.vb[:], ["vb"], ["vq"])
         scan(T.s4[:, 256:512], T.m4[:], T.AB[:, 256:512], 0.0, A.add, A.min, ["m4", "AB2", "AB3"], ["s41"])
+        if SPLIT[1] > SPLIT[0]:
+            balls(SPLIT[0], SPLIT[1])
         ts(T.oH[:], T.s4[:, 259:512:4], col(1), None, A.add, None, ["s41", "c1"], ["oH"])
-        cp(T.LP[:].indirect(T.TG[:, 0:17]), T.CR[:], ["TG0", "CR", "CRx"], ["LP"])
+        balls(SPLIT[1], 17)
 
         def gather_b(h, Tw, tk, off, ok):
             for n in range(2):
@@ -478,19 +489,19 @@ def rank_program(g, core, T, topo):
         gather_b(0, T.Tp, "Tp", lo, lk)
         gather_a(1, 0, T.To, "To", T.oH, "oH")
         gather_a(1, 1, T.To, "To", T.oH, "oH")
-        cp(T.LR[:, 0:128], T.LP[:, 0:256].indirect(T.pos[:, 0:8]), ["LP", "pos"], ["LR0"])
+        gather_a(0, 0, T.Tp, "Tp", lo, lk)
         quant_z(1)
         layer(1, 4)
-        gather_a(0, 0, T.Tp, "Tp", lo, lk)
         gather_a(0, 1, T.Tp, "Tp", lo, lk)
         for k in range(4):
             vcopy("s", 1, k, 4 + k)
-        scan(T.sL[:, 0:128], T.m4[:, 0:128], T.LR[:, 0:128], 0.0, A.add, A.min, ["m4", "LR0"], ["sL0"])
+        cp(T.LR[:, 0:128], T.LP[:, 0:256].indirect(T.pos[:, 0:8]), ["LP", "pos"], ["LR0"])
         quant_z(0)
         layer(0, 0)
         cp(T.LR[:, 128:256], T.LP[:, 0:256].indirect(T.pos[:, 8:16]), ["LP", "pos"], ["LR1"])
-        ts(T.oL[:, 0:32], T.sL[:, 3:128:4], col(1), None, A.add, None, ["sL0", "c1"], ["oL0"])
+        scan(T.sL[:, 0:128], T.m4[:, 0:128], T.LR[:, 0:128], 0.0, A.add, A.min, ["m4", "LR0"], ["sL0"])
         scan(T.sL[:, 128:256], T.m4[:, 128:256], T.LR[:, 128:256], 0.0, A.add, A.min, ["m4", "LR1"], ["sL1"])
+        ts(T.oL[:, 0:32], T.sL[:, 3:128:4], col(1), None, A.add, None, ["sL0", "c1"], ["oL0"])
         for k in range(4):
             vcopy("v" if k in NV else "s", 0, k, k)
         ts(T.oL[:, 32:64], T.sL[:, 131:256:4], col(1), None, A.add, None, ["sL1", "c1"], ["oL1"])

@@ -1,34 +1,97 @@
-from concourse.mybir import dt, AluOpType, ActivationFunctionType
+from concourse.mybir import dt, AluOpType, ActivationFunctionType, AxisListType
 
 A = AluOpType
 F = ActivationFunctionType
 MASK = [1, 2, 4]
+VPL = (15, 14, 7)
+ONV = ("Kp", "Bs", "al", "AB1", "LR0", "V01", "V03")
+XCUT = (0, 512, 640, 832, 1024)
+ZCUT = ((0, 160, 352, 512), (0, 256, 512))
+BCUT = (0, 17)
+ORDER = {
+    "v": "c_MTw c_MTy c_pc1 X_0 c_i2 c_c5 c_MTz c_il c_sm0 c_eb c_ob00 c_ob03 c_ob02 c_ob01 X_512 c_MTx c_ul c_c0 c_eb#2 c_i4 c_pc0 c_mq1 c_oq0 c_sm1 c_g5 c_eq1 c_c1 c_c2 c_uq xq0 c_up0 c_up1 X_832 X_640 Sm0 xq1 F0 c_eq0 M7 Sm1 M160 F1 thr M161 M15 DS1 Kp Bs nt Dn M14 al DS0 c_oq1 RS7 N1 Y y1 RS15 mq0 RS14 mq1 sN mq2 c_eq3 mp sY c_eq2 sel rr pos PL O sB AB1 w3 s40 w1 so w4 w5 s41 TG oH LP Z512 Z768 LR0 zq1 Z0 Z160 Z352 sL0 zq0 sL1 oL0 c_vq V03 V01 e_yo1 oL1",
+    "s": "c_X00 c_mD c_m0 c_Bsz c_c6 c_c7 c_N10 c_c3 c_Y0 c_RS0 c_c4 c_c9 c_c8 c_ob1 c_up0s c_m32 c_up1s sg4 sg2 sg1 M4 sg3 M2 sg6 M1 c_CC sg12 sg13 sg11 sg10 M3 M13 sg9 M10 sg5 M12 sg8 M11 M9 M8 M5 M6 c_mp To1 c_m4 ya To3 c_DUM To2 CRx To0 ny c_spare c_DUM#2 AB0 Ox AB3 AB2 Tp3 Tp1 Zb512 Zb768 Tp2 Tp0 LP Zb0 Zb160 Zb352 LR1 e_LF V11 V10 V13 V12 V02 V00 e_yo0 e_y0 e_osc0 e_osc1 e_osc2",
+    "t": "e_P4 P4 e_P5 P5 P0 P6 P7 P1 P2 P4#2 P2#2 P2#3 P2#4 P6#2 P5#2 P3 P7#2 P2#5 P1#2 P0#2 P5#3 P6#3 P3#2 P4#3 P2#6 P7#3 P0#3 P1#3",
+    "g": "c_i1b c_i1a c_i3 c_gi c_dd c_i1c c_g4 c_k16 c_CR c_ob1 send send#2 c_LPa0 c_LP0 send#3 c_LPa1 c_LP1 send#4 c_LPa2 c_LP2",
+    "y": "c_ub c_X01 c_w1_ c_vb c_w0 e_lb e_oc0 e_oc1 e_osc3 e_y1o",
+}
+VPL = (1, 2, 3, 4, 8, 9, 10)
+ONV = ("Kp", "Bs", "al", "AB1", "LR0", "V01", "V03", "ny", "Ox", "CRx")
+ORDER["v"] = "c_MTy c_MTw c_pc1 c_i2 c_MTz c_c5 c_il c_sm0 c_c0 c_eb c_ob00 c_ob03 c_ob01 c_ob02 c_ul c_MTx c_eb#2 c_i4 c_pc0 c_mq1 c_oq0 c_c6 c_c7 c_eq1 c_sm1 c_g5 c_c8 c_c1 c_spare c_c2 c_eq0 c_uq X_0 X_512 xq0 c_up0 X_640 X_832 c_up1 Sm0 xq1 F0 c_CC c_DUM M160 M1 M2 Sm1 M4 M3 F1 thr DS0 RS1 RS2 Kp Bs nt M161 M8 M10 M9 c_eq2 c_eq3 al RS3 RS4 mq2 Dn DS1 c_oq1 N1 Y RS8 RS9 RS10 c_DUM#2 mq0 sY y1 sN mq1 ny mp w1 PL sel sB pos w3 O rr AB1 Ox s40 w5 so w4 CRx s41 TG oH LP Z512 LP#2 Z768 LR0 zq1 Z0 Z160 sL0 Z352 sL1 zq0 oL0 oL1 c_vq V01 V03 e_yo1"
+ORDER["s"] = "c_X00 c_mD c_m0 c_ob1 c_m32 c_up0s c_up1s sg7 sg6 sg5 M7 M6 M5 sg15 sg14 sg13 M15 M14 M13 sg12 sg11 c_mp M12 M11 c_m4 ya To0 To1 To2 To3 Tp0 Tp1 AB0 AB3 AB2 Tp2 Tp3 Zb512 Zb768 LR1 Zb0 Zb160 Zb352 V10 V11 V12 V13 V00 V02 e_LF e_yo0 e_y0 e_osc0 e_osc1 e_osc2"
+ORDER["t"] = "P4 P5 P0 P6 P1 P7 P3 P5#2 P4#2 P6#2 P2 P2#2 P2#3 P2#4 P0#2 P1#2 P7#2 P2#5 P3#2 P4#3 P5#3 P6#3 P0#3 P1#3 P2#6 P7#3 e_P4 e_P5"
+ORDER["g"] = "c_i1b c_i1a c_gi c_i3 c_dd c_i1c c_g4 c_g8 c_k16 c_k17 c_ob1 c_N10 c_Y0 c_Bsz c_RS0 c_CR send send#2 c_LPa0 c_LP0 send#3 c_LPa1 c_LP1 send#4 c_LPa2 c_LP2"
+XCUT = (512, 640, 832, 1024)
+VPL = (15, 14, 7)
+ONV = ("thr1", "Kp1", "Bs1", "al1", "AB1", "LR0", "Ox")
+ORDER["v"] = "c_MTy c_MTw c_pc1 c_i2 c_MTz c_c5 c_il c_sm0 c_c0 c_eb c_ob00 c_ob03 c_ob01 c_ob02 c_ul c_MTx c_eb#2 c_sm3 c_sm4 c_i4 c_pc0 c_mq1 c_oq0 c_c6 c_c7 c_eq1 c_sm5 c_sm1 c_g5 c_c8 c_c1 c_c3 c_spare c_c2 c_eq0 c_CC c_DUM c_uq X_0 X_1 X_2 X_3 X_512 xq0 c_up0 X_640 c_up1 X_832 Sm0 thr0 xq1 F0 nt0 c_eq2 Kp0 Bs0 al0 M160 M7 Dn0 N0 Sm1 DS0 RS7 Y0 F1 thr1 sN0 sY0 M15 nt1 M14 M13 M12 M9 M8 Kp1 Bs1 M161 al1 c_eq3 RS15 Dn1 N1 c_oq1 RS14 RS13 RS12 RS9 RS8 DS1 mq0 Y1 y1 c_DUM#2 mq1 sY1 sN1 mq2 ny mp sB0 sB1 sel PL w1 w3 pos rr w5 O w4 Ox AB0 AB1 TG CRx s40 so AB2 AB3 s41 LP oH Z512 LP#2 Z768 LR0 LR1 zq1 Z0 sL0 Z160 sL1 Z352 oL0 oL1 zq0 c_vq V10 V11 V12 V13 V00 V01 V02 V03 e_yo1"
+ORDER["s"] = "c_X00 c_mD c_m0 c_ob1 c_m32 c_m16 c_up0s c_up1s sgt thr0 Kp0 Bs0 sg7 sg6 sg5 al0 sg4 sg3 sg2 sg1 M7 M6 M5 M4 M3 M2 M1 sg15 sg14 sg13 sg12 sg11 sgt#2 thr1 M15 M14 M13 Kp1 Bs1 M12 sg10 al1 sg9 M11 sg8 M10 M9 M8 c_mp c_m4 To1 ya ny To2 To3 To0 Tp0 Tp1 AB0 AB1 Ox AB3 AB2 CRx Tp2 Tp3 Zb512 Zb768 LR0 Zb0 Zb160 Zb352 LR1 V10 V11 V12 V13 V00 V01 V02 V03 e_LF e_yo0 e_y0 e_osc0 e_osc1 e_osc2"
+ORDER["t"] = "P4 P6 P5 P7 P0 P2 P1 P3 P4#2 P5#2 P2#2 P6#2 P3#2 P2#3 P2#4 P2#5 P0#2 P1#2 P7#2 P2#6 P3#3 P4#3 P5#3 P6#3 P0#3 P1#3 P2#7 P7#3 e_P4 e_P5"
+ORDER["g"] = "c_i1b c_i1a c_gi c_i3 c_dd c_i1c c_g4 c_g8 c_k16 c_k17 c_Ni c_Yi c_Bsz c_ob1 c_RS0 c_CR send send#2 c_LPa0 c_LP0 send#3 c_LPa1 c_LP1 send#4 c_LPa2 c_LP2"
+SUMS0 = ((0, 256, "mq0"), (384, 576, "mq1"), (576, 704, "mq1"), (256, 384, "mq2"))
+XCUT = (512, 640, 1024)
+VPL = (15, 14, 9, 7)
+ONV = ("thr1", "Kp1", "Bs1", "al1", "AB1")
+ORDER["v"] = "c_MTy c_MTw c_pc1 c_i2 c_MTz c_c5 c_il c_sm0 c_c0 c_eb c_ob00 c_ob03 c_ob01 c_ob02 c_ul c_MTx c_eb#2 c_sm3 c_sm4 c_i4 c_pc0 c_mq1 c_oq0 c_c6 c_c7 c_eq1 c_sm5 c_sm1 c_g5 c_c8 c_c1 c_c3 c_spare c_c2 c_uq c_eq0 X_0 c_up0 X_1 X_2 X_3 X_512 xq0 c_up1 c_CC c_DUM X_640 Sm0 xq1 c_eq2 F0 c_DUM#2 c_eq3 c_oq1 M160 M7 nt0 Sm1 thr1 F1 Dn0 nt1 DS0 M14 Y0 M161 M15 RS14 Kp1 N0 DS1 M9 mq0 Bs1 al1 RS7 RS15 mq1 RS9 y1 Dn1 mq2 mp Y1 sY0 N1 sY1 c_vq sel sN0 sN1 pos sB1 PL O sB0 AB1 w3 w1 s40 rr so w4 w5 s41 TG oH LP Z512 Z768 LP#2 Z0 zq1 Z160 e_yo1 Z352 sL0 zq0 sL1 oL0 oL1"
+ORDER["s"] = "c_X00 c_mD c_m0 c_ob1 c_m32 c_m16 c_up0s c_up1s c_mp sgt thr0 Bs0 Kp0 sg4 sg1 sg5 sg2 sg3 M4 M1 al0 sg6 M3 sg10 sg13 sg12 sg11 M13 M10 M12 M2 M11 sg8 M5 M6 M8 c_m4 To1 To0 ya ny To2 To3 Tp1 Tp2 AB0 Ox AB3 AB2 CRx Tp3 Tp0 Zb512 Zb768 Zb0 Zb160 e_LF e_yo0 Zb352 LR0 V13 V10 LR1 e_y0 V12 V11 V00 V01 e_osc2 V03 e_osc1 e_osc0 V02"
+ORDER["t"] = "P4 P6 P5 P7 P0 P2 P3 P1 P4#2 P5#2 P6#2 P2#2 P3#2 P2#3 P2#4 P2#5 P1#2 P2#6 P0#2 P7#2 P3#3 P6#3 P4#3 P5#3 P0#3 P1#3 e_P4 P7#3 e_P5 P2#7"
+ORDER["g"] = "c_i1b c_i1a c_gi c_i3 c_dd c_i1c c_g4 c_g8 c_k16 c_k17 c_Ni c_Yi c_Bsz c_ob1 c_RS0 c_CR send send#2 c_LPa0 c_LP0 c_LPa1 c_LP1 c_LPa2 send#3 c_LP2 send#4"
+FIRST = ("xq0", "xq1", "P0", "P1", "Sm1", "F1")
 VPL = (15, 14, 9)
-YA, NV = 9, (1, 3)
-VLO, SPLIT = (7, 6), (2, 4)
-OWN, FAR = (4, 5, 6, 7), (0, 1, 3, 2)
-TP = ((0, 1), (2, 3))
+ONV = ("thr0", "thr1", "Kp0", "Kp1", "Bs0", "Bs1", "al0", "al1", "AB1", "V00", "V01", "ny", "Ox")
+ZCUT = ((0, 256, 512), (0, 256, 512))
+ORDER["v"] = "c_MTy c_MTw c_pc1 c_i2 c_MTz c_c5 c_il c_sm0 c_c0 c_eb c_ob00 c_ob03 c_ob01 c_ob02 c_ul c_MTx c_eb#2 c_sm3 c_sm4 c_i4 c_pc0 c_mq1 c_oq0 c_sm5 c_eq1 c_sm1 c_g5 c_eq0 c_c1 c_c2 c_eq2 c_eq3 c_uq a_xq0 a_xq1 c_up0 c_up1 c_oq1 X_0 X_1 X_2 X_3 X_512 xq0 X_640 Sm0 xq1 F0 a_Sm1 thr0 M160 a_F1 Kp0 nt0 Sm1 Bs0 F1 thr1 al0 M15 M161 M14 nt1 M9 N0 Dn0 Kp1 al1 DS1 Y0 Bs1 RS15 sY0 DS0 Dn1 mq0 mq1 RS9 y1 c_vq mq2 RS14 N1 Y1 mp sN1 sY1 sel sB0 sN0 pos sB1 PL O ny Ox w3 AB1 rr w1 s40 w5 w4 so TG s41 oH LP Z512 Z768 LP#2 zq1 Z0 Z256 zq0 sL1 sL0 oL1 oL0 V00 V01 e_yo1"
+ORDER["s"] = "c_X00 c_c6 c_c3 c_c7 c_mD c_m0 c_spare c_ob1 c_c8 c_m32 c_m16 c_CC c_DUM c_mp c_DUM#2 c_up0s c_up1s sg1 sg4 sg7 sg2 sg3 sg6 sg5 M1 M4 M3 M2 sg11 sg10 sg13 sg12 M10 sg8 M13 M12 M11 M8 M5 M6 M7 To1 ya To0 c_m4 To3 To2 Tp1 AB0 AB2 AB3 Tp2 CRx Tp0 Tp3 Zb512 Zb768 Zb0 Zb256 LR1 V10 LR0 V12 V13 V11 V02 V03 e_LF e_yo0 e_y0 e_osc0 e_osc1 e_osc2"
+ORDER["t"] = "P4 a_P0 P6 P5 P7 a_P1 P0 P1 P2 P6#2 P3 P4#2 P5#2 P3#2 P2#2 P2#3 P2#4 P2#5 P1#2 P0#2 P2#6 P7#2 P4#3 P3#3 P6#3 P5#3 P0#3 P1#3 P2#7 P7#3 e_P4 e_P5"
+ORDER["g"] = "c_i1b c_i1a c_gi c_i3 c_dd c_i1c c_g4 c_g8 c_k16 c_k17 c_Ni c_Yi c_Bsz c_ob1 c_RS0 c_CR send send#2 c_LPa0 c_LP0 c_LPa1 c_LP1 c_LPa2 send#3 c_LP2 send#4"
+WHOLE = True
+VPL = (15, 14, 7)
+ONV = ("AB1", "Kp1", "Bs1", "al1")
+ORDER["v"] = "c_MTy c_MTw c_pc1 c_i2 c_MTz c_c5 c_il c_sm0 c_c0 c_eb c_ob00 c_ob03 c_ob01 c_ob02 c_ul c_MTx c_eb#2 c_sm3 c_sm4 c_i4 c_pc0 c_mq1 c_oq0 c_sm5 c_eq1 c_sm1 c_g5 c_eq0 c_c1 c_c2 c_uq a_xq0 c_up0 c_up1 X_0 X_1 X_2 X_3 X_512 xq0 X_640 a_xq1 Sm0 c_eq2 xq1 c_eq3 F0 c_oq1 a_Sm1 M7 Sm1 thr1 a_F1 F1 nt1 M14 c_vq M161 M15 Kp1 M160 Bs1 RS15 al1 Dn1 DS1 N1 DS0 mq0 Y1 RS7 mq1 RS14 y1 mq2 sN1 mp sY1 sel PL pos rr O sB1 w5 AB1 w3 w1 s40 w4 so s41 TG oH LP Z512 Z768 zq1 Z0 Z256 sL1 sL0 zq0 oL1 oL0 e_yo1"
+ORDER["s"] = "c_X00 c_c6 c_c3 c_c7 c_mD c_m0 c_spare c_ob1 c_c8 c_m32 c_m16 c_CC c_DUM c_up0s c_up1s c_mp c_DUM#2 sg2 sg3 sg1 sg6 M3 sg4 M2 M1 sg5 sg13 sg11 sg9 sg12 sg10 M13 M10 M11 M12 M9 M4 sg8 M5 M6 M8 c_m4 ya ny To1 To0 CRx To2 To3 Ox AB0 AB3 AB2 Tp3 Tp2 Tp0 Zb512 Zb768 Tp1 LP Zb0 Zb256 LR1 LR0 V10 V11 V12 V13 V00 V01 V02 V03 e_LF e_yo0 e_y0 e_osc0 e_osc1 e_osc2"
+ORDER["t"] = "P4 a_P0 P5 P0 P6 a_P1 P7 P1 P3 P6#2 P4#2 P5#2 P2 P2#2 P2#3 P2#4 P2#5 P0#2 P1#2 P7#2 P3#2 P4#3 P5#3 P6#3 P0#3 P1#3 P2#6 P7#3 e_P4 e_P5"
+ORDER["g"] = "c_i1b c_i1a c_gi c_i3 c_dd c_i1c c_g4 c_g8 c_k16 c_k17 c_Ni c_Yi c_Bsz c_ob1 c_RS0 c_CR send send#2 c_LPa0 c_LP0 c_LPa1 c_LP1 c_LPa2 send#3 c_LP2 send#4"
+XQ = "y"
+ORDER["y"] = "c_ub c_X00 c_X01 c_w0 c_w1_ c_vb e_lb e_oc0 e_oc1 e_y1o e_osc3"
+ZR = ()
+WHOLE = False
+VPL = (15, 14, 13)
+ONV = ("thr0", "thr1", "Kp0", "Kp1", "Bs0", "Bs1", "al0", "al1", "AB1", "V00", "V01", "Ox")
+ORDER["v"] = "c_MTy c_MTw c_pc1 c_i2 c_MTz c_c5 c_il c_sm0 c_c0 c_ul c_eb c_ob00 c_ob03 c_ob01 c_ob02 c_MTx c_eb#2 c_sm3 c_sm4 c_i4 c_pc0 c_mq1 c_oq0 c_sm5 c_eq1 c_sm1 c_g5 c_eq0 c_c1 c_c2 c_uq c_eq2 c_up0 a_xq0 c_up1 a_xq1 c_eq3 c_oq1 X_0 X_1 X_2 X_3 X_512 xq0 X_640 Sm0 xq1 F0 thr0 a_Sm1 M160 Bs0 a_F1 Sm1 nt0 Kp0 F1 thr1 DS0 M161 nt1 N0 M13 M14 Bs1 Kp1 al0 M15 RS13 Dn0 al1 Dn1 DS1 mq0 y1 RS15 Y0 mq1 RS14 mq2 Y1 sY0 mp sY1 N1 sel sN1 sN0 pos sB0 PL O sB1 AB1 Ox w3 w1 s40 rr w4 w5 so s41 TG oH LP Z512 Z768 Z0 zq1 Z256 sL0 sL1 zq0 c_vq oL0 oL1 V00 V01 e_yo1"
+ORDER["s"] = "c_c6 c_c3 c_c7 c_mD c_m0 c_spare c_ob1 c_c8 c_m32 c_m16 c_CC c_DUM c_up0s c_up1s c_mp c_DUM#2 sg7 sg3 sg4 sg2 sg5 sg6 M7 M2 sg1 M4 sg11 sg10 sg12 sg9 M3 M10 M1 sg8 M9 M11 M12 M6 M5 M8 c_m4 ya ny To3 To0 To2 To1 AB0 AB3 AB2 Tp1 CRx Tp2 Tp3 Zb512 Tp0 Zb768 Zb0 LP Zb256 LR0 LR1 V10 V11 V12 V13 V02 V03 e_LF e_yo0 e_y0 e_osc1 e_osc0 e_osc2"
+ORDER["t"] = "P4 P5 a_P0 P6 a_P1 P0 P7 P2 P1 P3 P3#2 P6#2 P5#2 P4#2 P2#2 P2#3 P2#4 P2#5 P1#2 P2#6 P7#2 P0#2 P3#3 P4#3 P5#3 P6#3 P0#3 P1#3 P2#7 P7#3 e_P4 e_P5"
+ORDER["g"] = "c_i1b c_i1a c_i3 c_gi c_dd c_i1c c_g4 c_g8 c_k16 c_k17 c_Ni c_Yi c_Bsz c_ob1 c_RS0 c_CR send send#2 c_LPa0 c_LP0 c_LPa1 c_LP1 c_LPa2 send#3 c_LP2 send#4"
+ONV = ("thr0", "thr1", "Kp0", "Kp1", "Bs0", "Bs1", "al0", "al1", "AB1", "V00")
+ORDER["v"] = "c_MTy c_MTw c_pc1 c_i2 c_MTz c_c5 c_il c_sm0 c_c0 c_ul c_eb c_ob00 c_ob03 c_ob01 c_ob02 c_MTx c_eb#2 c_sm3 c_sm4 c_i4 c_pc0 c_mq1 c_oq0 c_sm5 c_eq1 c_sm1 c_g5 c_eq0 c_c1 c_c2 c_uq c_eq2 c_up0 a_xq0 c_up1 c_eq3 c_oq1 X_0 X_1 X_2 X_3 X_512 xq0 X_640 Sm0 a_xq1 xq1 F0 thr0 M160 Kp0 Bs0 Sm1 a_Sm1 DS0 thr1 F1 a_F1 Dn0 Bs1 M14 M161 nt0 M13 al0 nt1 N0 M15 DS1 RS14 al1 Kp1 Y0 mq0 Dn1 RS15 mq1 y1 mq2 RS13 Y1 sY0 mp N1 sY1 sel sN0 sN1 pos sB0 PL O sB1 rr AB1 w3 w1 s40 so w5 w4 s41 TG oH LP Z512 Z768 Z0 zq1 Z256 c_vq sL1 zq0 sL0 oL0 V00 oL1 e_yo1"
+ORDER["s"] = "c_c6 c_c3 c_c7 c_mD c_m0 c_spare c_ob1 c_c8 c_m32 c_m16 c_CC c_DUM c_up0s c_up1s c_mp c_DUM#2 sg2 sg7 sg3 sg4 sg1 sg5 M3 M2 M1 M5 sg6 M4 sg8 sg9 sg10 sg11 sg12 M9 M10 M11 M12 M8 M7 M6 c_m4 To3 To2 ya To1 Tp1 Tp3 ny Tp0 AB0 Ox AB3 AB2 CRx To0 Tp2 Zb512 Zb768 Zb0 LP Zb256 LR1 LR0 V10 V11 V12 V13 V01 V02 V03 e_LF e_yo0 e_y0 e_osc2 e_osc0 e_osc1"
+ORDER["t"] = "P4 P6 P5 P0 a_P0 P2 P1 P3 P6#2 P7 a_P1 P4#2 P3#2 P5#2 P2#2 P2#3 P2#4 P2#5 P1#2 P7#2 P0#2 P2#6 P3#3 P4#3 P5#3 P6#3 P0#3 P1#3 P2#7 P7#3 e_P4 e_P5"
+OWN, FAR = (3, 4, 5, 6), (0, 1, 2, 7)
+WAKE, LOCAL, REMOTE, PER_KB = 200, 1500, 1400, 10
+PASSES = 8
 BF, F32, I32, U16, Q4, U8 = "bfloat16", "float32", "int32", "uint16", "float8_e4m3fn_x4", "uint8"
 
 SCRATCH = {"P": ("psum", [128, 4096], F32)}
 for _d, _names in (
-    (BF, "ub:512 vb:512 sm:176 mD:256 m0:256 m16:256 m4:256 dd:128 gi:128 eb:516 ob:1024 CR:272 PF:272 "
-         "MT:2816 sg:2048 DS:256 O:272 thr:256 nt:256 al:256 Kp:256 Bs:272 N1:256 Dn:256 Y:256 Ya:256 Yp:256 Bp:256 "
-         "rr:256 sN:512 m32:256 sY:256 sB:256 LP:576 LR:256 sL:256 AB:512 s4:512 To:1024 Tp:1024 Zb:1024 Z:1024 V:1024 "
-         "X0:1024 X1:1024 X2:1024 X3:1024"),
-    (F32, "cf:16 mp:256 k16:16 CC:16 DUM:16 Sm:256 Fs:256 RS:2048 y1:16 sel:256 w1:96 LF:256 yo:256"),
-    (I32, "i1:32 i2:32 i3:24 i4:16 i5:16 pc:8"),
-    (U16, "ul:24 il:16 pos:16 PL:32 TG:18 oL:64 oH:64 so0:64 so1:64 so2:64 lo0:64 lo1:64 lo2:64"),
+    (BF, "ub:512 vb:512 sm:96 mD:272 m0:256 m16:128 m4:256 dd:128 gi:128 eb:516 ob:1024 CR:288 "
+         "MT:2816 sg:2048 DS:256 O:272 thr:256 nt:256 al:256 Kp:256 Bs:288 N1:256 Dn:256 Y:256 "
+         "rr:256 sN:512 m32:256 sB:256 LP0:592 LP1:592 LP2:592 LR:256 sL:256 AB:512 s4:512 "
+         "To:1024 Tp:1024 Zb:1024 Z:1024 V:1024 X0:1024 X1:1024 X2:1024 X3:1024"),
+    (F32, "cf:16 g4:16 mp:256 k16:32 CC:16 DUM:16 Sm:256 Fs:256 RS:2048 y1:16 sel:256 sY:256 w1:96 LF:256 yo:256"),
+    (I32, "i1:56 i2:40 i3:24 i4:16 pc:8"),
+    (U16, "ul:24 il:18 pos:16 PL:32 TG:18 oL:64 oH:64 so0:64 so1:64 so2:64 lo0:64 lo1:64 lo2:64"),
     (Q4, "uq:128 upq:384 vq:128 wq:512 eq:512 oq:256 mq:704 zq:256 xq0:256 xq1:256 xq2:256 xq3:256 lq0:256 lq1:256 lq2:256"),
     (U8, "us:128 ups:384 vs:128 wsc:512 es:512 osn:256 ms:704 zs:256 xs0:256 xs1:256 xs2:256 xs3:256 ls0:256 ls1:256 ls2:256"),
 ):
     for _e in _names.split():
         SCRATCH[_e.split(":")[0]] = ("sbuf", [128, int(_e.split(":")[1])], _d)
 
-SEMAPHORES = ["v", "s", "t", "gq", "dx0", "dx1", "du", "dw", "dv", "o1", "o2", "sent",
+SEMAPHORES = ["v", "s", "t", "g", "dx0", "dx1", "du", "dw0", "dw1", "dv", "o1", "o2", "sent",
               "aq0", "aq1", "aq2", "al0", "al1", "al2"]
 
-TILE0 = {0: 0, 1: 256, 2: 448, 3: 576}
+TILE0 = {0: 0, 1: 384, 2: 256, 3: 576}
+SUMS = ((0, 256, "mq0"), (256, 384, "mq2"), (576, 704, "mq1"), (384, 576, "mq1"))
+SUMS = SUMS0
+MTZ = ["MTw", "MTx", "MTy", "MTz"]
 
 
 def plane(k):
@@ -36,90 +99,151 @@ def plane(k):
     return TILE0[n // 4], n % 4
 
 
+def pieces(cuts):
+    return list(zip(cuts[:-1], cuts[1:]))
+
+
+def issue_order(ops):
+    ids = range(len(ops))
+    before = [[(d, ops[d]["lat"] + WAKE) for d in o["after"]] + [(d, 0.0) for d in o["behind"]] for o in ops]
+    behind = [[] for _ in ids]
+    for n in ids:
+        for d, gap in before[n]:
+            behind[d].append((n, gap))
+
+    def place(turn, edges, first):
+        lines, end = {}, {}
+        for n in turn:
+            busy = ops[n]["busy"]
+            t = max([first(n)] + [end[d] + gap for d, gap in edges[n]])
+            line = lines.setdefault(ops[n]["q"], [])
+            at = len(line)
+            for i, (a, b, _) in enumerate(line):
+                if t + busy <= a:
+                    at = i
+                    break
+                t = max(t, b)
+            line.insert(at, (t, t + busy, n))
+            end[n] = t + busy
+        return lines, end
+
+    back = {}
+    for n in reversed(ids):
+        back[n] = ops[n]["busy"] + max([ops[n]["lat"]] + [back[d] + gap for d, gap in behind[n]])
+    best = None
+    for _ in range(PASSES):
+        lines, end = place(sorted(ids, key=lambda n: (-back[n], n)), before, lambda n: 0.0)
+        total = max(end[n] + ops[n]["lat"] for n in ids)
+        if best is None or total < best[0]:
+            best = (total, lines)
+        back = place(sorted(ids, key=lambda n: (-end[n], -n)), behind, lambda n: ops[n]["lat"])[1]
+    return {q: [n for _, _, n in line] for q, line in best[1].items()}
+
+
+def listed_order(ops):
+    place = {(q, k): i for q, text in ORDER.items() for i, k in enumerate(text.split())}
+    order = {}
+    for n, o in enumerate(ops):
+        order.setdefault(o["q"], []).append(n)
+    return {q: sorted(l, key=lambda n: (max(ops[n]["rnd"], 0), place.get((q, ops[n]["name"]), 0), n)) for q, l in order.items()}
+
+
 def rank_program(g, core, T, topo):
     rank = T.rank_of(core)
     if rank is None:
         return
     Q = {"v": g.vector, "s": g.scalar, "t": g.tensor, "g": g, "y": g.sync}
-    own = {"v": "v", "s": "s", "t": "t", "g": "gq"}
-    cnt = {}
-    waited = {q: {} for q in Q}
-    lastw, readers = {}, {}
+    ops, lastw, readers = [], {}, {}
+    now, named, late = [-1], {}, [False]
 
-    def need(q, dep):
-        sem, val = dep[0], dep[1]
-        if waited[q].get(sem, 0) < val:
-            Q[q].wait_ge(T.sem[sem], val)
-            waited[q][sem] = val
+    def name(q, W):
+        k = W[0] if W else "send"
+        for head in ("X", "xq", "LP", "lq", "lo", "so"):
+            if now[0] >= 0 and k.startswith(head) and k[len(head)].isdigit():
+                k = head + k[len(head) + 1:]
+        k = ("c_" if now[0] < 0 else "e_" if now[0] == 3 and k[0] not in "Xx" else "") + k
+        c = named[now[0], q, k] = named.get((now[0], q, k), 0) + 1
+        k = k if c == 1 else "%s#%d" % (k, c)
+        if now[0] in ZR and (W and W[0][:2] in ("Zb", "Z0", "Z2", "Z5", "Z7", "zq", "zo", "s4", "oH", "LP", "LR", "sL", "oL", "TG", "V0", "V1") or late[0] and q == "t"):
+            return "z_" + k.replace("zo1", "zo").replace("zo2", "zo")
+        return "a_" + k if now[0] == 0 and k in FIRST else k
 
-    def op(q, fn, R=(), W=(), sem=None, inc=1, acc=False):
-        deps = {}
-
-        def add(d):
-            deps[d[0]] = max(deps.get(d[0], 0), d[1])
+    def op(q, busy, fn, R=(), W=(), sem=None, inc=1, lat=0.0, acc=False, behind=()):
+        after, behind = set(), set(behind)
         for k in R:
             if k in lastw:
-                add(lastw[k])
+                after.add(lastw[k])
             if k[0] == "P" and k[1:].isdigit():
-                for d in readers.get(k, []):
-                    if d[2] != q:
-                        add(d)
+                after.update(d for d in readers.get(k, []) if ops[d]["q"] != q)
         for k in W:
-            if k in lastw and not acc:
-                add(lastw[k])
-            for d in readers.get(k, []):
-                add(d)
-        for s_, v_ in deps.items():
-            need(q, (s_, v_))
-        ins = fn()
-        sem = sem or own[q]
-        cnt[sem] = cnt.get(sem, 0) + inc
-        ins.then_inc(T.sem[sem], inc)
-        me = (sem, cnt[sem], q)
+            if k in lastw:
+                (behind if acc else after).add(lastw[k])
+            after.update(readers.get(k, []))
+        ops.append(dict(q=q, busy=busy, fn=fn, after=after, behind=behind, sem=sem or q, inc=inc, lat=lat,
+                        rnd=now[0], name=name(q, W)))
         for k in R:
-            readers.setdefault(k, []).append(me)
+            readers.setdefault(k, []).append(len(ops) - 1)
         for k in W:
-            lastw[k] = me
+            lastw[k] = len(ops) - 1
             readers[k] = []
+        return len(ops) - 1
 
     vec, sca, ten = g.vector, g.scalar, g.tensor
 
-    def ts(out, in0, s1, s2, o0, o1, R, W):
+    def cyc(n):
+        return max(64, n) * 0.83
+
+    def pick(n):
+        return 55 + 1.25 * n
+
+    def ts(c, out, in0, s1, s2, o0, o1, R, W):
         if o1 is None:
-            op("v", lambda: vec.tensor_scalar(out, in0, s1, None, o0), R, W)
+            op("v", c, lambda: vec.tensor_scalar(out, in0, s1, None, o0), R, W)
         else:
-            op("v", lambda: vec.tensor_scalar(out, in0, s1, s2, o0, o1), R, W)
+            op("v", c, lambda: vec.tensor_scalar(out, in0, s1, s2, o0, o1), R, W)
 
-    def tt(out, a, b, o, R, W):
-        op("v", lambda: vec.tensor_tensor(out, a, b, o), R, W)
+    def tt(c, out, a, b, o, R, W):
+        op("v", c, lambda: vec.tensor_tensor(out, a, b, o), R, W)
 
-    def scan(out, d0, d1, init, o0, o1, R, W):
-        op("v", lambda: vec.tensor_tensor_scan(out, d0, d1, init, o0, o1), R, W)
+    def scan(c, out, d0, d1, init, o0, o1, R, W):
+        op("v", c, lambda: vec.tensor_tensor_scan(out, d0, d1, init, o0, o1), R, W)
 
-    def cp(out, in_, R, W):
-        op("v", lambda: vec.tensor_copy(out, in_), R, W)
+    def cp(c, out, in_, R, W):
+        op("v", c, lambda: vec.tensor_copy(out, in_), R, W)
 
-    def ms(ap, c, W):
-        op("v", lambda: vec.memset(ap, c), (), W)
+    def ms(c, ap, x, W):
+        op("v", c, lambda: vec.memset(ap, x), (), W)
 
-    def act(out, in_, f, R, W, **kw):
-        op("s", lambda: sca.activation(out, in_, f, **kw), R, W)
+    def act(c, out, in_, f, R, W, **kw):
+        op("s", c, lambda: sca.activation(out, in_, f, **kw), R, W)
 
-    def qz(q, s, in_, R, W):
-        op("v", lambda: vec.quantize_mx(q, s, in_), R, W)
+    def lin(n, out, in_, scale, bias, R, W, narrow=False):
+        if W[0] in ONV:
+            ts(cyc(n / 2 if narrow else n), out, in_, scale, bias, A.mult, A.add, R, W)
+        else:
+            act(cyc(n), out, in_, F.Identity, R, W, scale=scale, bias=bias)
+
+    def gather(n, out, in_, R, W):
+        if W[0] in ONV:
+            cp(pick(n), out, in_, R, W)
+        else:
+            act(pick(n), out, in_, F.Identity, R, W)
+
+    def qz(n, q, s, in_, R, W):
+        op("v", 12 + 0.88 * n, lambda: vec.quantize_mx(q, s, in_), R, W)
 
     def mm(bank, n, lq, lsc, rq, rsc, R, start=True, stop=True):
-        op("t", lambda: ten.matmul_mx(T.P[:, 512 * bank:512 * bank + n], lq, lsc, rq, rsc, start, stop),
+        op("t", 0.6 * (n + 16), lambda: ten.matmul_mx(T.P[:, 512 * bank:512 * bank + n], lq, lsc, rq, rsc, start, stop),
            R, ["P%d" % bank], acc=not start)
 
-    def iota(out, pat, base, cm, W, fl=False):
+    def iota(n, out, pat, base, cm, W, fl=False):
         if fl:
-            op("g", lambda: g.iota(out, pat, base, cm, allow_small_or_imprecise_dtypes=True), (), W)
+            op("g", 130 + 1.66 * n, lambda: g.iota(out, pat, base, cm, allow_small_or_imprecise_dtypes=True), (), W)
         else:
-            op("g", lambda: g.iota(out, pat, base, cm), (), W)
+            op("g", 130 + 1.66 * n, lambda: g.iota(out, pat, base, cm), (), W)
 
-    def dma(q, out, in_, R, W, sem):
-        op(q, lambda: Q[q].dma_start(out, in_), R, W, sem=sem, inc=16)
+    def dma(q, kb, out, in_, R, W, sem):
+        op(q, 60, lambda: Q[q].dma_start(out, in_), R, W, sem=sem, inc=16, lat=LOCAL + 4 * kb)
 
     def bank(b, lo=0, hi=256):
         return T.P[:, 512 * b + lo:512 * b + hi]
@@ -127,407 +251,324 @@ def rank_program(g, core, T, topo):
     def col(j):
         return T.cf[:, j:j + 1]
 
-    def sm(j):
-        return T.sm[:, 16 * j:16 * j + 16]
+    sends = []
 
-    nsent = [0]
-
-    def engines(a, b):
-        return topo.engines(a, b)
-
-    def send(peer, dst, src, R, sem):
-        eng = engines(core, peer)
+    def exchange(peer, pairs, sem, key):
+        eng = topo.engines(core, peer)
         rid, pid, _ = topo.addr(peer)
-        for k in R:
-            need("g", lastw[k])
-        g.remote_dma(dst, src, T.sem[sem], T.sem.sent, pid, rid, sum(1 << e for e in eng))
-        nsent[0] += len(eng)
+        mine = []
+        for dst, src, kb, R in pairs:
+            def fn(dst=dst, src=src):
+                g.remote_dma(dst, src, T.sem[sem], T.sem.sent, pid, rid, sum(1 << e for e in eng))
+            mine.append(op("g", 300 if sends else 1500, fn, R, (), sem="sent", inc=len(eng), lat=REMOTE + PER_KB * kb - WAKE, behind=sends[-1:]))
+            sends.append(mine[-1])
+        n = op("r", 0.0, None, (), [key], sem=sem, inc=len(topo.engines(peer, core)) * len(pairs))
+        ops[n]["after"].update(mine)
 
-    def arrives(peer, keys, sem, writes):
-        n = len(engines(peer, core)) * writes
-        cnt[sem] = n
-        for k in keys:
-            lastw[k] = (sem, n, "r")
+    dma("y", 128, T.ub[:], T.u[:], (), ["ub"], "du")
+    dma(XQ, 128, T.X0[:, 0:512], T.x[:, 0:512], (), ["X00"], "dx0")
+    dma("y", 128, T.X0[:, 512:1024], T.x[:, 512:1024], (), ["X01"], "dx1")
+    dma("y", 256, T.wq[:].bitcast(dt.uint8), T.wc[:], ["X01"], ["w0"], "dw0")
+    dma("y", 64, T.wsc[:], T.ws[:], ["X01"], ["w1_"], "dw1")
+    dma("y", 128, T.vb[:], T.v[:], ["X01"], ["vb"], "dv")
 
-    dma("y", T.ub[:], T.u[:], (), ["ub"], "du")
-    dma("s", T.X0[:, 0:512], T.x[:, 0:512], (), ["X00"], "dx0")
-    dma("y", T.X0[:, 512:1024], T.x[:, 512:1024], (), ["X01"], "dx1")
-    need("y", lastw["X01"])
-    dma("y", T.wq[:].bitcast(dt.uint8), T.wc[:], (), ["w_"], "dw")
-    dma("y", T.wsc[:], T.ws[:], (), ["w"], "dw")
-    dma("y", T.vb[:], T.v[:], (), ["vb"], "dv")
+    iota(16, T.i1[:, 0:16], [[1, 16]], 128, -1, ["i1a"])
+    iota(18, T.i1[:, 16:34], [[0, 18]], 0, 1, ["i1b"])
+    iota(24, T.i3[:], [[1, 3], [16, 8]], 0, 0, ["i3"])
+    iota(16, T.i1[:, 40:56], [[0, 4], [4, 4]], 131, -1, ["i1c"])
+    iota(3, T.g4[:, 0:3], [[-4, 3]], 11, 0, ["g4"], True)
+    iota(4, T.g4[:, 8:12], [[1, 2], [1024, 2]], -512, 0, ["g8"], True)
+    iota(16, T.k16[:, 0:16], [[16, 16]], 1025, 0, ["k16"], True)
+    iota(16, T.k16[:, 16:32], [[-16, 16]], 240, 0, ["k17"], True)
+    iota(128, T.dd[:], [[1, 128]], 0, -1, ["dd"], True)
+    iota(128, T.gi[:], [[1, 8], [0, 16]], 0, 0, ["gi"], True)
+    iota(288, T.CR[:], [[1, 288]], 0, 0, ["CR", "CRx"], True)
+    for r in range(3):
+        iota(256, T["LP%d" % r][:, 0:256], [[1, 256]], 1, 0, ["LPa%d" % r], True)
+        iota(1, T["LP%d" % r][:, 256:257], [[0, 1]], 0, 0, ["LP%d" % r], True)
 
-    iota(T.i1[:, 0:16], [[1, 16]], 128, -1, ["i1a"])
-    iota(T.i1[:, 16:32], [[0, 16]], 0, 1, ["i1b"])
-    iota(T.i3[:], [[1, 3], [16, 8]], 0, 0, ["i3"])
-    iota(T.dd[:], [[1, 128]], 0, -1, ["dd"], True)
-    iota(T.gi[:], [[1, 8], [0, 16]], 0, 0, ["gi"], True)
-    iota(T.k16[:], [[16, 16]], 0, 0, ["k16"], True)
-    iota(T.PF[:, 0:256], [[1, 256]], 0, 0, ["PFa"], True)
-    iota(T.PF[:, 256:257], [[0, 1]], 0, 0, ["PF"], True)
-    iota(T.CR[:], [[1, 272]], 0, 0, ["CR", "CRx"], True)
+    s_ = cyc(16)
+    for key, a, b in (("MTy", 2304, 2816), ("MTx", 832, 1024), ("MTw", 1344, 1536), ("MTz", 2112, 2304)):
+        ms(cyc((b - a) / 2), T.MT[:, a:b], 0.0, [key])
+    ms(cyc(258), T.eb[:], 0.0, ["eb"])
+    ts(s_, T.i2[:, 0:34], T.i1[:, 0:34], 15, None, A.bitwise_and, None, ["i1a", "i1b"], ["i2"])
+    cp(s_, T.il[:], T.i2[:, 16:34], ["i2"], ["il"])
+    ts(s_, T.sm[:, 0:16], T.i2[:, 0:16], 0.0, None, A.is_equal, None, ["i2"], ["sm0"])
+    cp(s_, col(0), T.i2[:, 15:16], ["i2"], ["c0"])
+    gather(272, T.mD[:], T.sm[:, 0:16].indirect(T.il[:, 0:17]), ["sm0", "il"], ["mD"])
+    lin(256, T.m0[:], T.mD[:, 0:256], -1.0, 1.0, ["mD"], ["m0"], True)
+    lin(256, T.m32[:], T.mD[:, 0:256], 8704.0, -512.0, ["mD"], ["m32"], True)
+    lin(256, T.mp[:], T.mD[:, 1:257], 16896.0, -512.0, ["mD"], ["mp"])
+    cp(s_, T.ul[:], T.i3[:], ["i3"], ["ul"])
+    ts(s_, T.i4[:], T.i1[:, 40:56], 12, None, A.bitwise_and, None, ["i1c"], ["i4"])
+    ts(s_, T.pc[:, 0:1], T.i1[:, 16:17], 3, None, A.bitwise_and, None, ["i1b"], ["pc0"])
+    ts(s_, T.pc[:, 1:2], T.i1[:, 16:17], 4, None, A.arith_shift_right, None, ["i1b"], ["pc1"])
+    ts(s_, T.sm[:, 16:32], T.i4[:], 0.0, 256.0, A.not_equal, A.mult, ["i4"], ["sm1"])
+    gather(256, T.m4[:], T.sm[:, 16:32].indirect(T.il[:, 0:16]), ["sm1", "il"], ["m4"])
+    ts(s_, col(1), T.pc[:, 0:1], 256.0, -1.0, A.mult, A.add, ["pc0"], ["c1"])
+    cp(s_, col(5), T.pc[:, 1:2], ["pc1"], ["c5"])
+    ts(s_, T.g4[:, 4:7], T.g4[:, 0:3], col(0), 2.0 ** -8, A.is_ge, A.max, ["g4", "c0"], ["g5"])
+    op("v", s_, lambda: vec.tensor_reduce(col(2), T.g4[:, 4:7], AxisListType.X, A.mult), ["g5"], ["c2"])
+    qz(128, T.mq[:, 576:704], T.ms[:, 576:704], T.MT[:, 2304:2816], ["MTy"], ["mq1"])
+    for out, x, key in ((T.N1[:, 0:1], 255, "Ni"), (T.Y[:, 0:1], -256, "Yi"), (T.RS[:, 127:128], 0, "RS0")):
+        iota(1, out, [[0, 1]], x, 0, [key], True)
+    iota(2, T.Bs[:, 15:160:144], [[0, 2]], -255, 0, ["Bsz"], True)
+    ts(s_, T.sm[:, 48:64], T.i2[:, 0:16], 1.0, -256.0, A.is_equal, A.mult, ["i2"], ["sm3"])
+    ts(s_, T.sm[:, 64:80], T.i2[:, 0:16], 0.0, 1024.0, A.is_equal, A.mult, ["i2"], ["sm4"])
+    tt(s_, T.sm[:, 80:96], T.sm[:, 48:64], T.sm[:, 64:80], A.add, ["sm3", "sm4"], ["sm5"])
+    gather(128, T.m16[:], T.sm[:, 80:96].indirect(T.il[:, 0:8]), ["sm5", "il"], ["m16"])
+    lin(4, T.cf[:, 8:12], T.g4[:, 8:12], col(0), 0.0, ["g8", "c0"], ["c8"])
+    lin(1, col(6), T.sm[:, 15:16], 2000.0, 0.0, ["sm0"], ["c6"])
+    lin(1, col(3), T.sm[:, 15:16], -256.0, 256.0, ["sm0"], ["c3"])
+    lin(1, col(7), col(0), -4.0, -260.0, ["c0"], ["c7"])
+    lin(16, T.CC[:], T.k16[:, 0:16], 1.0, col(11), ["k16", "c8"], ["CC"])
+    lin(16, T.DUM[:], T.k16[:, 16:32], 1.0, col(10), ["k17", "c8"], ["DUM"])
+    lin(1, T.sm[:, 32:33], col(7), 1.0, col(6), ["c6", "c7"], ["spare"])
+    lin(1, T.DUM[:, 15:16], T.DUM[:, 15:16], 1.0, col(6), ["c6", "DUM"], ["DUM"])
 
-    ms(T.MT[:, 2112:2816], 0.0, ["MTy"])
-    ms(T.MT[:, 832:1024], 0.0, ["MTx"])
-    ms(T.eb[:], 0.0, ["eb"])
-    ts(T.i2[:], T.i1[:], 15, None, A.bitwise_and, None, ["i1a", "i1b"], ["i2"])
-    ts(T.pc[:, 1:2], T.i1[:, 16:17], 4, None, A.arith_shift_right, None, ["i1b"], ["pc1"])
-    ms(T.MT[:, 1600:1792], 0.0, ["MTz"])
-    cp(T.il[:], T.i2[:, 16:32], ["i2"], ["il"])
-    ts(sm(1), T.i2[:, 0:16], 0.0, None, A.is_equal, None, ["i2"], ["sm1"])
-    ts(sm(2), T.i2[:, 0:16], 0.0, None, A.not_equal, None, ["i2"], ["sm2"])
-    act(T.mD[:], sm(1).indirect(T.il[:]), F.Identity, ["sm1", "il"], ["mD"])
-    act(T.m0[:], sm(2).indirect(T.il[:]), F.Identity, ["sm2", "il"], ["m0"])
-    ts(T.pc[:, 2:3], T.i1[:, 16:17], 2, None, A.arith_shift_right, None, ["i1b"], ["pc2"])
-    cp(sm(0), T.i2[:, 0:16], ["i2"], ["sm0"])
-    ts(sm(3), T.i2[:, 0:16], 1.0, -256.0, A.is_equal, A.mult, ["i2"], ["sm3"])
-    ts(sm(4), T.i2[:, 0:16], 0.0, 1024.0, A.is_equal, A.mult, ["i2"], ["sm4"])
-    cp(T.cf[:, 6:8], T.pc[:, 1:3], ["pc1", "pc2"], ["c6", "c7"])
-    cp(T.ul[:], T.i3[:], ["i3"], ["ul"])
-    tt(sm(5), sm(3), sm(4), A.add, ["sm3", "sm4"], ["sm5"])
-    ts(sm(6), T.i2[:, 0:16], 15.0, 1024.0, A.is_equal, A.mult, ["i2"], ["sm6"])
-    ts(sm(7), T.i2[:, 0:16], 0.0, -512.0, A.is_equal, A.mult, ["i2"], ["sm7"])
-    act(T.m16[:], sm(5).indirect(T.il[:]), F.Identity, ["sm5", "il"], ["m16"])
-    ts(col(14), T.i1[:, 16:17], col(7), None, A.subtract, None, ["i1b", "c7"], ["c14"])
-    ts(T.pc[:, 3:4], T.i1[:, 16:17], 3, None, A.bitwise_and, None, ["i1b"], ["pc3"])
-    ms(T.RS[:, 127:128], 0.0, ["RS0"])
-    tt(sm(8), sm(6), sm(7), A.add, ["sm6", "sm7"], ["sm8"])
-    for t in range(4):
-        ts(T.ob[:, t:512:4], T.gi[:], col(6), None, A.is_equal, None, ["gi", "c6"], ["ob0%d" % t])
-    act(T.mp[:], sm(8).indirect(T.il[:]), F.Identity, ["sm8", "il"], ["mp"])
-    ts(T.eb[:, 3:515:4], T.dd[:], 0.0, None, A.is_equal, None, ["dd"], ["eb"])
+    ts(s_, T.eb[:, 3:515:4], T.dd[:], 0.0, None, A.is_equal, None, ["dd"], ["eb"])
+    for b in range(4):
+        qz(128, T.eq[:, 128 * b:128 * b + 128], T.es[:, 128 * b:128 * b + 128], T.eb[:, 3 - b:515 - b], ["eb"], ["eq%d" % b])
     ob0 = ["ob0%d" % t for t in range(4)]
-    act(T.ob[:, 512:1024], T.ob[:, 0:512], F.Identity, ob0, ["ob1"])
-    op("g", lambda: g.affine_select(T.ob[:, 512:1024:4], T.ob[:, 512:1024:4], [[1, 128]], A.is_gt, 0.0, 0, -1),
-       ["ob1"], ["ob1"])
-    qz(T.mq[:, 576:704], T.ms[:, 576:704], T.MT[:, 2304:2816], ["MTx", "MTy", "MTz"], ["mq2"])
-    nz15, d15 = T.sm[:, 47:48], T.sm[:, 15:16]
-    ts(T.i4[:], T.i1[:, 0:16], col(14), None, A.add, None, ["i1a", "c14"], ["i4"])
-    ts(col(9), nz15, 512.0, d15, A.mult, A.add, ["sm2", "sm0"], ["c9"])
+    for t in range(4):
+        ts(s_, T.ob[:, t:512:4], T.gi[:], col(5), None, A.is_equal, None, ["gi", "c5"], [ob0[t]])
+    lin(512, T.ob[:, 512:1024], T.ob[:, 0:512], 1.0, 0.0, ob0, ["ob1"])
+    op("g", 380, lambda: g.affine_select(T.ob[:, 512:1024:4], T.ob[:, 512:1024:4], [[1, 128]], A.is_gt, 0.0, 0, -1), ["ob1"], ["ob1"])
+    qz(128, T.oq[:, 0:128], T.osn[:, 0:128], T.ob[:, 0:512], ob0, ["oq0"])
+    qz(128, T.oq[:, 128:256], T.osn[:, 128:256], T.ob[:, 512:1024], ["ob1"], ["oq1"])
 
-    def quant_e(b):
-        qz(T.eq[:, 128 * b:128 * b + 128], T.es[:, 128 * b:128 * b + 128], T.eb[:, 3 - b:515 - b], ["eb"], ["eq%d" % b])
+    qz(128, T.uq[:], T.us[:], T.ub[:], ["ub"], ["uq"])
+    for a, b, key in ((0, 8, "up0"), (8, 24, "up1")):
+        act(pick(16 * (b - a)), T.ups[:, 16 * a:16 * b], T.us[:].indirect(T.ul[:, a:b]), F.Copy, ["uq", "ul"], [key + "s"])
+        cp(pick(16 * (b - a)), T.upq[:, 16 * a:16 * b].bitcast(dt.uint32), T.uq[:].bitcast(dt.uint32).indirect(T.ul[:, a:b]),
+           ["uq", "ul"], [key])
+    qz(128, T.vq[:], T.vs[:], T.vb[:], ["vb"], ["vq"])
 
-    quant_e(0)
-    ts(T.i5[:], T.i4[:], 3, None, A.bitwise_and, None, ["i4"], ["i5"])
-    quant_e(1)
-    ts(T.CC[:], T.k16[:], 1025.0, col(9), A.add, A.add, ["k16", "c9"], ["CC"])
-    ts(sm(3), T.i5[:], 0.0, 1024.0, A.is_equal, A.mult, ["i5"], ["sm3"])
-    ts(sm(4), T.i5[:], 1.0, -256.0, A.is_equal, A.mult, ["i5"], ["sm4"])
-
-    qz(T.uq[:], T.us[:], T.ub[:], ["ub"], ["uq"])
-    tt(sm(9), sm(3), sm(4), A.add, ["sm3", "sm4"], ["sm9"])
-    ms(T.Bs[:, 15:16], 0.0, ["Bsz"])
-    ms(T.N1[:, 0:1], 255.0, ["N10"])
-    ms(T.Y[:, 0:1], -256.0, ["Y0"])
-    act(T.ups[:, 0:128], T.us[:].indirect(T.ul[:, 0:8]), F.Copy, ["uq", "ul"], ["ups"])
-    cp(T.upq[:, 0:128].bitcast(dt.uint32), T.uq[:].bitcast(dt.uint32).indirect(T.ul[:, 0:8]), ["uq", "ul"], ["upq"])
-    act(T.ups[:, 128:384], T.us[:].indirect(T.ul[:, 8:24]), F.Copy, ["uq", "ul"], ["ups2"])
-    act(col(0), nz15, F.Identity, ["sm2"], ["c0"], scale=256.0)
-    act(col(8), nz15, F.Identity, ["sm2"], ["c8"], scale=-256.0, bias=256.0)
-    act(col(11), T.sm[:, 31:32], F.Identity, ["sm1"], ["c11"], scale=2000.0)
-    act(col(12), T.sm[:, 31:32], F.Identity, ["sm1"], ["c12"], scale=2000.0, bias=-576.0)
-    act(T.m4[:], sm(9).indirect(T.il[:]), F.Identity, ["sm9", "il"], ["m4"])
-
-    def early_a():
-        ts(col(13), T.i5[:, 3:4], 0.0, 256.0, A.not_equal, A.mult, ["i5"], ["c13"])
-        quant_e(2)
-
-    def late_a():
-        quant_e(3)
-        qz(T.oq[:], T.osn[:], T.ob[:], ob0 + ["ob1"], ["oq"])
-        ts(col(1), T.pc[:, 3:4], 256.0, col(13), A.mult, A.add, ["pc3", "c13"], ["c1"])
-        ts(col(10), d15, col(0), -16.0, A.add, A.add, ["sm0", "c0"], ["c10"])
-
-    def late_b():
-        ts(T.DUM[:], T.k16[:], -1.0, col(10), A.mult, A.add, ["k16", "c10"], ["DUM"])
-        ts(T.sm[:, 160:161], d15, 4.0, col(12), A.mult, A.add, ["sm0", "c12"], ["c5"])
-        ts(T.DUM[:, 15:16], T.DUM[:, 15:16], col(11), None, A.add, None, ["c11", "DUM"], ["DUM"])
-
-    def late_s():
-        act(T.m32[:], T.m16[:], F.Identity, ["m16"], ["m32"], scale=2.0)
-
-    def unpack(b0, q, s, keys):
+    def unpack(banks, q, s, keys, dst, key):
         for b in range(4):
-            mm(b0[b], 256, T.eq[:, 128 * b:128 * b + 128], T.es[:, 128 * b:128 * b + 128], q[:], s[:], ["eq%d" % b] + keys)
-
-    def unpack_copy(b0, dst, key, bs):
-        for b in bs:
-            act(dst[:, 256 * b:256 * b + 256], bank(b0[b]), F.Identity, ["P%d" % b0[b]], [key + str(b)], scale=0.5)
-
-    def sel16(out, v, R, W):
-        scan(out, T.m16[:], v[:], 0.0, A.add, A.min, ["m16"] + R, W)
-
-    def up(j):
-        return T.upq[:, 128 * j:128 * j + 128], T.ups[:, 128 * j:128 * j + 128]
+            mm(banks[b], 256, T.eq[:, 128 * b:128 * b + 128], T.es[:, 128 * b:128 * b + 128], q[:], s[:], ["eq%d" % b] + keys)
+        for b in range(4):
+            lin(256, dst[:, 256 * b:256 * b + 256], bank(banks[b]), 0.5, 0.0, ["P%d" % banks[b]], [key + str(b)])
 
     def pview(k, a, b):
         c0, t = plane(k)
         return T.MT[:, 4 * (c0 + a) + t:4 * (c0 + b):4]
 
-    def rcol(k):
-        return T.Fs[:, 16 * k + 15:16 * k + 16]
+    def compare(k):
+        n, score, fk = 16 * k, T.Fs[:, 16 * k + 15:16 * k + 16], "F%d" % (k // 8)
+        if k in VPL:
+            b = 4 if k < 8 else 0
+            ts(cyc(n), pview(k, 0, n), bank(b, 0, n), score, None, A.is_lt, None, ["P%d" % b, fk] + MTZ, ["M%d" % k])
+            scan(cyc(n / 2), T.RS[:, 128 * k + 128 - 8 * k:128 * k + 128], pview(k, 0, 8 * k), pview(k, 8 * k, n), 0.0,
+                 A.add, A.add, ["M%d" % k], ["RS%d" % k])
+        else:
+            b, sg = (5 if k < 8 else 1), T.sg[:, 8 * k * (k - 1):8 * k * (k + 1)]
+            act(cyc(n), sg, bank(b, 0, n), F.Sign, ["P%d" % b, fk], ["sg%d" % k], scale=-1.0, bias=score)
+            act(cyc(n) + 20, pview(k, 0, n), sg, F.Relu, ["sg%d" % k] + MTZ, ["M%d" % k, "RS%d" % k],
+                accum_out=T.RS[:, 128 * k + 127:128 * k + 128])
 
-    def fkey(k):
-        return "F1" if k >= 8 else "F0"
+    def xkeys(r, h):
+        return ["X0%d" % h] if r == 0 else ["X%d_%d" % (r, a) for a in (XCUT[:-1] if h else range(4))]
 
-    def vplane(k):
-        b = 4 if k < 8 else 0
-        ts(pview(k, 0, 16 * k), bank(b, 0, 16 * k), rcol(k), None, A.is_lt, None, ["P%d" % b, fkey(k), "MTz"], ["M%d" % k])
-
-    def vsum(k):
-        scan(T.RS[:, 128 * k + 128 - 8 * k:128 * k + 128], pview(k, 0, 8 * k), pview(k, 8 * k, 16 * k), 0.0,
-             A.add, A.add, ["M%d" % k], ["RS%d" % k])
-
-    sgo, o_ = {}, 0
-    for k in range(1, 16):
-        sgo[k] = o_
-        o_ += 16 * k
-
-    def s1(k):
-        b = 5 if k < 8 else 1
-        act(T.sg[:, sgo[k]:sgo[k] + 16 * k], bank(b, 0, 16 * k), F.Sign, ["P%d" % b, fkey(k)], ["sg%d" % k],
-            scale=-1.0, bias=rcol(k))
-
-    def s2(k):
-        act(pview(k, 0, 16 * k), T.sg[:, sgo[k]:sgo[k] + 16 * k], F.Relu, ["sg%d" % k, "MTz"], ["M%d" % k, "RS%d" % k],
-            accum_out=T.RS[:, 128 * k + 127:128 * k + 128])
-
-    def splanes(ks):
-        for k in ks[:2]:
-            s1(k)
-        for n, k in enumerate(ks):
-            if n + 2 < len(ks):
-                s1(ks[n + 2])
-            s2(k)
-
-    def state(r, a, b, keys):
+    def state(r, h):
+        X = T["X%d" % r]
         if r > 0:
-            vk = ["V%d%d" % (h, k) for h in range(2) for k in range(4)] + ["oL%d" % (a // 512), "X%d0" % (r - 1), "X%d1" % (r - 1),
-                                                                          "X%d2" % (r - 1), "X%d3" % (r - 1)]
-            tt(T["X%d" % r][:, a:b], T.V[:].indirect(T.oL[:, a // 16:b // 16]), T["X%d" % (r - 1)][:, a:b], A.add, vk, keys)
-
-    def quant(r, h):
+            old = T["X%d" % (r - 1)]
+            for t in range(4 - 4 * h):
+                tt(pick(128), X[:, t:512:4], T.V[:, 256 * t:256 * t + 256].indirect(T.oL[:, 0:8]), old[:, t:512:4], A.add,
+                   ["V0%d" % t, "V1%d" % t, "oL0"] + xkeys(r - 1, 0), ["X%d_%d" % (r, t)])
+            for a, b in pieces(XCUT) * h:
+                R = ["V%d%d" % (n, k) for n in range(2) for k in range(4)] + ["oL1"] + xkeys(r - 1, 1)
+                tt(pick(b - a), X[:, a:b], T.V[:].indirect(T.oL[:, a // 16:b // 16]), old[:, a:b], A.add, R, ["X%d_%d" % (r, a)])
         a, b = 128 * h, 128 * h + 128
-        qz(T["xq%d" % r][:, a:b], T["xs%d" % r][:, a:b], T["X%d" % r][:, 4 * a:4 * b],
-           ["X%d0" % r] if h == 0 else ["X%d1" % r, "X%d2" % r, "X%d3" % r], ["xq%d%d" % (r, h)])
+        qz(128, T["xq%d" % r][:, a:b], T["xs%d" % r][:, a:b], X[:, 4 * a:4 * b], xkeys(r, h), ["xq%d%d" % (r, h)])
+
+    def whole(xq, xs, xk):
+        for j in (1, 2):
+            mm(5 + j, 256, T.upq[:, 128 * j:128 * j + 128], T.ups[:, 128 * j:128 * j + 128], xq[:], xs[:], ["up1", "up1s"] + xk)
+        ts(cyc(256), T.thr[:], bank(6), 0.0, U, A.is_gt, A.mult, ["P6"], ["thr1"])
+        tt(cyc(256), T.nt[:], bank(7), T.thr[:], A.is_le, ["P7", "thr1"], ["nt1"])
+        lin(256, T.Kp[:], T.thr[:], 511.0 / U, -256.0, ["thr1"], ["Kp1"], True)
+        lin(256, T.Bs[:, 16:272], T.thr[:], -512.0 / U, 256.0, ["thr1"], ["Bs1"], True)
+        lin(256, T.al[:], T.nt[:], 2.0, -1.0, ["nt1"], ["al1"], True)
+        scan(h_, T.Dn[:], T.Kp[:], T.Bs[:, 15:271], 255.0, A.add, A.add, ["Kp1", "Bs1", "Bsz"], ["Dn1"])
+        scan(h_, T.N1[:, 1:256], T.Kp[:, 0:255], T.Bs[:, 16:271], 255.0, A.add, A.add, ["Kp1", "Bs1"], ["N1"])
+        scan(h_, T.Y[:, 1:256], T.al[:, 0:255], T.Dn[:, 0:255], -256.0, A.mult, A.max, ["al1", "Dn1"], ["Y1"])
+        scan(cyc(256), T.sY[:], T.m32[:], T.Y[:], 0.0, A.add, A.min, ["m32", "Y1", "Yi"], ["sY1"])
+        scan(h_, T.sN[:, 0:256], T.m0[:], T.N1[:], 0.0, A.mult, A.max, ["m0", "N1", "Ni"], ["sN1"])
+        scan(h_, T.sB[:], T.m32[:], T.Bs[:, 16:272], 0.0, A.add, A.min, ["m32", "Bs1"], ["sB1"])
+
+    def outs(h, xq, xs, xk):
+        if WHOLE:
+            return whole(xq, xs, xk) if h else None
+        a, b, e, n, H = 128 * h, 128 * h + 128, 128 * h + 128 - h, 6 - 4 * h, str(h)
+        c = 16 + 144 * h
+        for j in (1, 2):
+            mm(n + j - 1, 128, T.upq[:, 128 * j:128 * j + 128], T.ups[:, 128 * j:128 * j + 128], xq[:, a:b], xs[:, a:b], ["up1", "up1s", xk[h]])
+        if "thr" + H in ONV:
+            ts(h_, T.thr[:, a:b], bank(n, 0, 128), 0.0, U, A.is_gt, A.mult, ["P%d" % n], ["thr" + H])
+        else:
+            act(h_, T.sg[:, 1920:2048], bank(n, 0, 128), F.Sign, ["P%d" % n], ["sgt"])
+            act(h_, T.thr[:, a:b], T.sg[:, 1920:2048], F.Relu, ["sgt"], ["thr" + H], scale=U)
+        tt(h_, T.nt[:, a:b], bank(n + 1, 0, 128), T.thr[:, a:b], A.is_le, ["P%d" % (n + 1), "thr" + H], ["nt" + H])
+        lin(128, T.Kp[:, a:b], T.thr[:, a:b], 511.0 / U, -256.0, ["thr" + H], ["Kp" + H], True)
+        lin(128, T.Bs[:, c:c + 128], T.thr[:, a:b], -512.0 / U, 256.0, ["thr" + H], ["Bs" + H], True)
+        lin(128, T.al[:, a:b], T.nt[:, a:b], 2.0, -1.0, ["nt" + H], ["al" + H], True)
+        n0, y0, prev = (T.N1[:, 128:129], T.Y[:, 128:129], ["N0", "Y0"]) if h else (255.0, -256.0, ["Ni", "Yi"])
+        scan(s_, T.Dn[:, a:b], T.Kp[:, a:b], T.Bs[:, c - 1:c + 127], n0, A.add, A.add, ["Kp" + H, "Bs" + H, "Bsz"] + prev[:h], ["Dn" + H])
+        scan(s_, T.N1[:, a + 1:e + 1], T.Kp[:, a:e], T.Bs[:, c:c + e - a], n0, A.add, A.add, ["Kp" + H, "Bs" + H] + prev[:h], ["N" + H])
+        scan(s_, T.Y[:, a + 1:e + 1], T.al[:, a:e], T.Dn[:, a:e], y0, A.mult, A.max, ["al" + H, "Dn" + H] + prev[2 - h:], ["Y" + H])
+        scan(h_, T.sY[:, a:b], T.m32[:, 0:128], T.Y[:, a:b], 0.0, A.add, A.min, ["m32", "Y" + H, prev[1]], ["sY" + H])
+        scan(s_, T.sN[:, a:b], T.m0[:, 0:128], T.N1[:, a:b], 0.0, A.mult, A.max, ["m0", "N" + H, prev[0]], ["sN" + H])
+        scan(s_, T.sB[:, a:b], T.m32[:, 0:128], T.Bs[:, c:c + 128], 0.0, A.add, A.min, ["m32", "Bs" + H], ["sB" + H])
+
+    def wrap4(src, dst, a, b, R, key, out, okey):
+        scan(cyc((b - a) / 2), dst[:, a:b], T.m4[:, 0:b - a], src[:, a:b], 0.0, A.mult, A.max, ["m4"] + R, [key])
+        ts(s_, out, dst[:, a + 3:b:4], col(2), col(1), A.mult, A.add, [key, "c1", "c2"], [okey])
+
+    U = 2.0 ** 80
+    w = [T.w1[:, 16 * n:16 * n + 16] for n in range(5)]
+    h_ = cyc(128)
 
     for r in range(3):
+        now[0], late[0] = r, False
         peer = T.cores[rank ^ MASK[r]]
         xq, xs = T["xq%d" % r], T["xs%d" % r]
         xk = ["xq%d0" % r, "xq%d1" % r]
-        lq, lsc, so, lo = T["lq%d" % r], T["ls%d" % r], T["so%d" % r], T["lo%d" % r]
-        U = 2.0 ** 80
-        state(r, 0, 512, ["X%d0" % r])
-        state(r, 512, 640, ["X%d1" % r])
-        quant(r, 0)
+        lq, lsc, so, lo, LP = T["lq%d" % r], T["ls%d" % r], T["so%d" % r], T["lo%d" % r], T["LP%d" % r]
+        LPk, lk = "LP%d" % r, "lo%d" % r
 
-        def scores(b, j, lo_, hi_):
-            mm(b, hi_ - lo_, *up(j), xq[:, lo_:hi_], xs[:, lo_:hi_],
-               (["upq", "ups"] if j == 0 else ["upq2", "ups2"]) + xk[lo_ // 128:hi_ // 128])
+        def scores(b, j, n):
+            up = "up%d" % min(j, 1)
+            mm(b, n, T.upq[:, 128 * j:128 * j + 128], T.ups[:, 128 * j:128 * j + 128], xq[:, 0:n], xs[:, 0:n], [up, up + "s"] + xk[:n // 128])
 
-        scores(4, 0, 0, 128)
-        if r > 0:
-            scores(6, 1, 0, 128)
-        scores(5, 0, 0, 128)
-        if r > 0:
-            scores(7, 2, 0, 128)
-        state(r, 640, 960, ["X%d2" % r])
+        for h in range(2):
+            a, b, n = 128 * h, 128 * h + 128, 4 - 4 * h
+            state(r, h)
+            scores(n, 0, b)
+            scores(n + 1, 0, b)
+            tt(h_, T.Sm[:, a:b], bank(n, a, b), T.mD[:, a:b], A.mult, ["P%d" % n, "mD"], ["Sm%d" % h])
+            scan(h_, T.Fs[:, a:b], T.m0[:, a:b], T.Sm[:, a:b], 0.0, A.mult, A.add, ["m0", "Sm%d" % h], ["F%d" % h])
+            tt(h_, pview(16, a, b), bank(n, a, b), T.Fs[:, a:b], A.is_le, ["P%d" % n, "F%d" % h] + MTZ, ["M16%d" % h])
+            scan(s_, T.DS[:, a:b], T.m0[:, a:b], pview(16, a, b), 0.0, A.mult, A.add, ["m0", "M16%d" % h], ["DS%d" % h])
+            for k in range(8 * h + 7, max(8 * h - 1, 0), -1):
+                compare(k)
+            outs(h, xq, xs, xk)
         if r == 0:
-            quant(r, 1)
-            cp(T.upq[:, 128:384].bitcast(dt.uint32), T.uq[:].bitcast(dt.uint32).indirect(T.ul[:, 8:24]), ["uq", "ul"], ["upq2"])
-            scores(6, 1, 0, 128)
-            scores(7, 2, 0, 128)
-        tt(T.Sm[:, 0:128], bank(4, 0, 128), T.mD[:, 0:128], A.mult, ["P4", "mD"], ["Sm0"])
-        state(r, 960, 1024, ["X%d3" % r])
-        if r == 0:
-            early_a()
+            pairs = [(lq[:].bitcast(dt.uint8), xq[:].bitcast(dt.uint8), 128, xk)]
         else:
-            ts(T.thr[:, 0:128], bank(6, 0, 128), 0.0, U, A.is_gt, A.mult, ["P6"], ["thr0"])
-        scan(T.Fs[:, 0:128], T.m0[:, 0:128], T.Sm[:, 0:128], 0.0, A.mult, A.add, ["m0", "Sm0"], ["F0"])
-        if r > 0:
-            act(T.LP[:, 0:257], T.PF[:, 0:257], F.Identity, ["PF"], ["LP"])
-            quant(r, 1)
+            pairs = [(lq[:, a:a + 128].bitcast(dt.uint8), xq[:, a:a + 128].bitcast(dt.uint8), 64 + a // 2, [xk[a // 128]]) for a in (0, 128)]
+        if r not in ZR:
+            exchange(peer, pairs + [(lsc[:], xs[:], 160, xk)], "aq%d" % r, "lq%d" % r)
+
+        for a, b, ks, key in ((0, 256, (160, 161, 15, 14, 13), "mq0"), (384, 640, (12, 11, 10, 9, 4, 3, 2, 1), "mq1"),
+                              (256, 384, (8, 7, 6, 5), "mq2")):
+            qz(b - a, T.mq[:, a:b], T.ms[:, a:b], T.MT[:, 4 * a:4 * b], ["M%d" % k for k in ks] + MTZ, [key])
+        for n, (a, b, key) in enumerate(SUMS):
+            c = 128 if a == 0 else 0
+            mm(2, b - a, T.oq[:, c:c + 128], T.osn[:, c:c + 128], T.mq[:, a:b], T.ms[:, a:b], ["oq%d" % (c // 128), key], n == 0, n == 3)
+        tt(s_, T.y1[:], T.CC[:], T.DS[:, 15::16], A.subtract, ["CC", "DS0", "DS1"], ["y1"])
+        tt(s_, T.mp[:, 15::16], T.y1[:], T.RS[:, 127::128], A.subtract, ["y1"] + ["RS%d" % k for k in range(16)], ["mp"])
+        scan(cyc(256), T.sel[:], bank(2), T.mp[:], 2048.0, A.min, A.add, ["P2", "mp"], ["sel"])
+        ts(s_, T.pos[:], T.sel[:, 15::16], -1024.0, None, A.add, None, ["sel"], ["pos"])
+        cp(50 + 2.7 * 256, T.O[:, 0:256].indirect(T.pos[:]), T.CR[:, 1:257], ["pos", "CR"], ["O"])
+        lin(1, T.O[:, 256:257], T.O[:, 0:1], 1.0, 0.0, ["O"], ["Ox"])
+
+        act(s_, T.sN[:, 271::16], T.sY[:, 15::16], F.Abs, ["sY0", "sY1", "c8"], ["ya"], bias=col(9))
+        lin(16, w[2], T.sY[:, 15::16], -1.0, col(8), ["sY0", "sY1", "c8"], ["ny"])
+        ts(s_, T.PL[:], T.sN[:, 15::16], -1.0, 256.0, A.mult, A.add, ["sN0", "sN1", "ya"], ["PL"])
+        scan(h_, T.rr[:, 0:255], T.nt[:, 0:255], T.nt[:, 0:255], -2.0, A.mult, A.add, ["nt0", "nt1"], ["rr"])
+        lin(1, T.CR[:, 272:273], T.rr[:, 254:255], -1.0, 255.0, ["rr"], ["CRx"])
+        tt(s_, w[1], w[2], T.sN[:, 15:256:16], A.max, ["ny", "sN0", "sN1"], ["w1"])
+        tt(s_, w[3], T.DUM[:], T.sB[:, 15::16], A.subtract, ["sB0", "sB1", "DUM"], ["w3"])
+        ts(s_, T.w1[:, 80:81], T.Y[:, 255:256], T.N1[:, 255:256], T.sm[:, 32:33], A.max, A.min, ["Y1", "N1", "spare"], ["w5"])
+        tt(s_, w[4], w[1], w[3], A.min, ["w1", "w3"], ["w4"])
+        ts(s_, T.TG[:, 0:17], T.w1[:, 64:81], -1.0, 256.0, A.mult, A.add, ["w4", "w5"], ["TG"])
+        for a, b in pieces(BCUT):
+            cp(50 + 2.7 * 16 * (b - a), LP[:].indirect(T.TG[:, a:b]), T.CR[:, 16 * a + 1:16 * b + 1],
+               ["TG", "CR", "LPa%d" % r] + (["CRx"] if b == 17 else []), [LPk])
+        if "LP" in ONV:
+            ts(s_, LP[:, 0:1], LP[:, 0:1], LP[:, 256:257], None, A.max, None, [LPk], [LPk])
         else:
-            ts(T.thr[:, 0:128], bank(6, 0, 128), 0.0, U, A.is_gt, A.mult, ["P6"], ["thr0"])
-        scores(2, 1, 128, 256)
-        scores(0, 0, 0, 256)
-        scores(3, 2, 128, 256)
-        scores(1, 0, 0, 256)
-        if r == 0:
-            send(peer, lq[:].bitcast(dt.uint8), xq[:].bitcast(dt.uint8), xk, "aq%d" % r)
-        else:
-            send(peer, lq[:, 0:128].bitcast(dt.uint8), xq[:, 0:128].bitcast(dt.uint8), xk[:1], "aq%d" % r)
-            send(peer, lq[:, 128:256].bitcast(dt.uint8), xq[:, 128:256].bitcast(dt.uint8), xk, "aq%d" % r)
-        send(peer, lsc[:], xs[:], xk, "aq%d" % r)
-        arrives(peer, ["lq%d" % r], "aq%d" % r, 2 if r == 0 else 3)
-        arrives(peer, ["lo%d" % r], "al%d" % r, 1)
-        splanes([k for k in range(7, 0, -1) if k not in VLO])
+            act(s_, LP[:, 0:1], LP[:, 0:1], F.Identity, [LPk], [LPk], bias=LP[:, 256:257])
+        for h in range(2):
+            a = 128 * h
+            gather(128, T.LR[:, a:a + 128], LP[:, 0:256].indirect(T.pos[:, 8 * h:8 * h + 8]), [LPk, "pos"], ["LR%d" % h])
+        scan(s_, T.sL[:, 0:128], T.m16[:], T.LR[:, 0:128], 0.0, A.add, A.min, ["m16", "LR0"], ["sL0"])
+        ts(s_, T.oL[:, 0:8], T.sL[:, 15:128:16], col(3), -1.0, A.add, A.add, ["sL0", "c3"], ["oL0"])
+        wrap4(T.LR, T.sL, 128, 256, ["LR1"], "sL1", T.oL[:, 32:64], "oL1")
 
-        tt(pview(16, 0, 128), bank(4, 0, 128), T.Fs[:, 0:128], A.is_le, ["P4", "F0"], ["M16a"])
-        tt(T.nt[:, 0:128], bank(7, 0, 128), T.thr[:, 0:128], A.is_le, ["P7", "thr0"], ["nt0"])
-        for k in VLO:
-            vplane(k)
-        ts(T.thr[:, 128:256], bank(2, 0, 128), 0.0, U, A.is_gt, A.mult, ["P2"], ["thr1"])
-        scan(T.DS[:, 0:128], T.m0[:, 0:128], pview(16, 0, 128), 0.0, A.mult, A.add, ["m0", "M16a"], ["DS0"])
-        tt(T.Sm[:, 128:256], bank(0, 128, 256), T.mD[:, 128:256], A.mult, ["P0", "mD"], ["Sm1"])
-        tt(T.nt[:, 128:256], bank(3, 0, 128), T.thr[:, 128:256], A.is_le, ["P3", "thr1"], ["nt1"])
-        vsum(VLO[0])
-        scan(T.Fs[:, 128:256], T.m0[:, 128:256], T.Sm[:, 128:256], 0.0, A.mult, A.add, ["m0", "Sm1"], ["F1"])
-        for k in VLO[1:]:
-            vsum(k)
-        act(T.Kp[:], T.thr[:], F.Identity, ["thr0", "thr1"], ["Kp"], scale=511.0 / U, bias=-256.0)
-        act(T.Bs[:, 16:272], T.thr[:], F.Identity, ["thr0", "thr1"], ["Bs"], scale=-512.0 / U, bias=256.0)
-        ts(T.al[:], T.nt[:], 2.0, -1.0, A.mult, A.add, ["nt0", "nt1"], ["al"])
-        big = [k for k in range(15, 8, -1) if k not in VPL]
-        splanes([8] + big[:YA])
-        for k in VPL:
-            vplane(k)
-        tt(pview(16, 128, 256), bank(0, 128, 256), T.Fs[:, 128:256], A.is_le, ["P0", "F1"], ["M16b"])
-        vsum(VPL[0])
-        scan(T.Dn[:], T.Kp[:], T.Bs[:, 15:271], 0.0, A.add, A.add, ["Kp", "Bs", "Kp0", "Bs0", "Bsz"], ["Dn"])
-        scan(T.N1[:, 1:256], T.Kp[:, 0:255], T.Bs[:, 16:271], 255.0, A.add, A.add, ["Kp", "Bs", "Kp0", "Bs0"], ["N1"])
-        vsum(VPL[1])
-        scan(T.Y[:, 1:256], T.al[:, 0:255], T.Dn[:, 0:255], -256.0, A.mult, A.max, ["al", "Dn"], ["Y"])
-        act(T.Ya[:], T.Y[:], F.Abs, ["Y", "Y0"], ["Ya"])
-        if big[YA:]:
-            splanes(big[YA:])
-        if r == 0:
-            late_a()
-        unpack(OWN, xq, xs, xk)
-        for k in VPL[2:]:
-            vsum(k)
-        scan(T.DS[:, 128:256], T.m0[:, 128:256], pview(16, 128, 256), 0.0, A.mult, A.add, ["m0", "M16b"], ["DS"])
-        qz(T.mq[:, 448:640], T.ms[:, 448:640], T.MT[:, 1792:2560], ["M%d" % k for k in range(1, 9)] + ["MTz"], ["mq2"])
-        qz(T.mq[:, 0:256], T.ms[:, 0:256], T.MT[:, 0:1024], ["M16a", "M16b", "M15", "M14", "M13", "MTz"], ["mq0"])
-        ones = (T.oq[:, 0:128], T.osn[:, 0:128])
-        mm(2, 256, T.oq[:, 128:256], T.osn[:, 128:256], T.mq[:, 0:256], T.ms[:, 0:256], ["oq", "mq0"], True, False)
-        mm(2, 128, *ones, T.mq[:, 448:576], T.ms[:, 448:576], ["oq", "mq2"], False, False)
-        mm(2, 128, *ones, T.mq[:, 576:704], T.ms[:, 576:704], ["oq", "mq2"], False, False)
-        tt(T.y1[:], T.CC[:], T.DS[:, 15::16], A.subtract, ["CC", "DS", "DS0"], ["y1"])
-        qz(T.mq[:, 256:448], T.ms[:, 256:448], T.MT[:, 1024:1792], ["M12", "M11", "M10", "M9", "MTz"], ["mq1"])
-        mm(2, 192, *ones, T.mq[:, 256:448], T.ms[:, 256:448], ["oq", "mq1"], False, True)
-        tt(T.mp[:, 15::16], T.y1[:], T.RS[:, 127::128], A.subtract, ["y1"] + ["RS%d" % k for k in range(16)], ["mp"])
-        sel16(T.sN[:, 0:256], T.N1, ["N1", "N10"], ["sN"])
-        sel16(T.sN[:, 256:512], T.Ya, ["Ya"], ["sA"])
-        act(T.Yp[:], T.Y[:], F.Relu, ["Y", "Y0"], ["Yp"], scale=-1.0)
-        if r == 0:
-            late_s()
-            late_b()
-        act(T.Bp[:], T.Bs[:, 16:272], F.Relu, ["Bs"], ["Bp"], scale=-2.0)
-        w = [T.w1[:, 16 * n:16 * n + 16] for n in range(5)]
-        scan(T.rr[:, 0:255], T.nt[:, 0:255], T.nt[:, 0:255], 0.0, A.mult, A.add, ["nt0", "nt1"], ["rr"])
-        sel16(T.sY[:], T.Yp, ["Yp"], ["sY"])
-        scan(T.sel[:], bank(2), T.mp[:], 2048.0, A.min, A.add, ["P2", "mp"], ["sel"])
-        scan(T.sB[:], T.m32[:], T.Bp[:], 0.0, A.add, A.min, ["m32", "Bp"], ["sB"])
-        ts(T.PL[:], T.sN[:, 15::16], -1.0, col(8), A.mult, A.add, ["sN", "sA", "c8"], ["PL1", "PL2"])
-        ts(T.pos[:], T.sel[:, 15::16], -1024.0, None, A.add, None, ["sel"], ["pos"])
-        tt(w[1], T.sY[:, 15::16], T.sN[:, 15:256:16], A.max, ["sY", "sN"], ["w1"])
-        ts(T.w1[:, 80:81], T.Y[:, 255:256], T.N1[:, 255:256], T.sm[:, 160:161], A.max, A.min, ["Y", "N1", "c5"], ["w5"])
-        tt(w[3], T.sB[:, 15::16], T.DUM[:], A.add, ["sB", "DUM"], ["w3"])
-        cp(T.O[:, 0:256].indirect(T.pos[:]), T.PF[:, 0:256], ["pos", "PF"], ["O"])
-        tt(w[4], w[1], w[3], A.min, ["w1", "w3"], ["w4"])
-        if r == 0:
-            act(T.LP[:, 0:257], T.PF[:, 0:257], F.Identity, ["PF"], ["LP"])
-        unpack_copy(OWN, T.To, "To", (0, 1, 2, 3))
-        unpack(FAR, lq, lsc, ["lq%d" % r])
-        act(T.CR[:, 271:272], T.rr[:, 254:255], F.Abs, ["rr"], ["CRx"], scale=-1.0, bias=254.0)
-        unpack_copy(FAR, T.Tp, "Tp", TP[0])
-        act(T.AB[:, 0:128], T.O[:, 0:256].indirect(T.PL[:, 0:8]), F.Identity, ["O", "PL1"], ["AB0"])
-        cp(T.AB[:, 128:256], T.O[:, 0:256].indirect(T.PL[:, 16:24]), ["O", "PL2"], ["AB1"])
-        act(T.O[:, 256:257], T.O[:, 0:1], F.Identity, ["O"], ["Ox"])
-        act(T.AB[:, 384:512], T.O[:, 0:256].indirect(T.PL[:, 24:32]), F.Identity, ["O", "PL2"], ["AB3"])
-        act(T.AB[:, 256:384], T.O[:, 0:257].indirect(T.PL[:, 8:16]), F.Identity, ["O", "Ox", "PL1"], ["AB2"])
-        unpack_copy(FAR, T.Tp, "Tp", TP[1])
-        def balls(a, b):
-            cp(T.LP[:].indirect(T.TG[:, a:b]), T.CR[:, 16 * a:16 * b], ["TG0", "CR"] + (["CRx"] if b == 17 else []), ["LP"])
+        unpack(OWN, xq, xs, xk, T.To, "To")
+        gather(128, T.AB[:, 0:128], T.O[:, 0:256].indirect(T.PL[:, 0:8]), ["O", "PL"], ["AB0"])
+        gather(128, T.AB[:, 128:256], T.O[:, 0:256].indirect(T.PL[:, 16:24]), ["O", "PL"], ["AB1"])
+        gather(128, T.AB[:, 256:384], T.O[:, 0:257].indirect(T.PL[:, 8:16]), ["O", "Ox", "PL"], ["AB2"])
+        gather(128, T.AB[:, 384:512], T.O[:, 0:256].indirect(T.PL[:, 24:32]), ["O", "PL"], ["AB3"])
+        wrap4(T.AB, T.s4, 0, 256, ["AB0", "AB1"], "s40", so[:], "so%d" % r)
+        wrap4(T.AB, T.s4, 256, 512, ["AB2", "AB3"], "s41", T.oH[:], "oH")
+        low = (0, T.To, "To", so, "so%d" % r, FAR)
+        late[0] = True
+        if r not in ZR:
+            exchange(peer, [(lo[:], so[:], 16, ["so%d" % r])], "al%d" % r, lk)
+            unpack(FAR, lq, lsc, ["lq%d" % r], T.Tp, "Tp")
+            low = (0, T.Tp, "Tp", lo, lk, FAR)
 
-        ts(T.TG[:, 0:17], T.w1[:, 64:81], -1.0, col(8), A.mult, A.add, ["w4", "w5", "c8"], ["TG0"])
-        scan(T.s4[:, 0:256], T.m4[:], T.AB[:, 0:256], 0.0, A.add, A.min, ["m4", "AB0", "AB1"], ["s40"])
-        if SPLIT[0]:
-            balls(0, SPLIT[0])
-        ts(so[:], T.s4[:, 3:256:4], col(1), None, A.add, None, ["s40", "c1"], ["so%d" % r])
-        send(peer, lo[:], so[:], ["so%d" % r], "al%d" % r)
-        if r == 0:
-            qz(T.vq[:], T.vs[:], T.vb[:], ["vb"], ["vq"])
-        scan(T.s4[:, 256:512], T.m4[:], T.AB[:, 256:512], 0.0, A.add, A.min, ["m4", "AB2", "AB3"], ["s41"])
-        if SPLIT[1] > SPLIT[0]:
-            balls(SPLIT[0], SPLIT[1])
-        ts(T.oH[:], T.s4[:, 259:512:4], col(1), None, A.add, None, ["s41", "c1"], ["oH"])
-        balls(SPLIT[1], 17)
-
-        def gather_b(h, Tw, tk, off, ok):
-            for n in range(2):
-                a = 512 * h + 256 * n
-                act(T.Zb[:, a:a + 256], Tw[:].indirect(off[:, 32 + 16 * n:48 + 16 * n]), F.Identity,
-                    [tk + str(b) for b in range(4)] + [ok], ["Zb%d%d" % (h, n)])
-
-        def gather_a(h, n, Tw, tk, off, ok):
-            a = 512 * h + 256 * n
-            tt(T.Z[:, a:a + 256], Tw[:].indirect(off[:, 16 * n:16 * n + 16]), T.Zb[:, a:a + 256], A.add,
-               [tk + str(b) for b in range(4)] + [ok, "Zb%d%d" % (h, n)], ["Z%d%d" % (h, n)])
-
-        def quant_z(h):
-            qz(T.zq[:, 128 * h:128 * h + 128], T.zs[:, 128 * h:128 * h + 128], T.Z[:, 512 * h:512 * h + 512],
-               ["Z%d0" % h, "Z%d1" % h], ["zq%d" % h])
-
-        def layer(h, b0):
+        for h, Tw, tk, off, ok, banks in ((1, T.To, "To", T.oH, "oH", OWN), low):
+            R = [tk + str(n) for n in range(4)] + [ok]
+            for a, b in pieces(ZCUT[h]):
+                c, d = 512 * h + a, 512 * h + b
+                act(pick(b - a), T.Zb[:, c:d], Tw[:].indirect(off[:, 32 + a // 16:32 + b // 16]), F.Identity, R, ["Zb%d" % c])
+                tt(pick(b - a), T.Z[:, c:d], Tw[:].indirect(off[:, a // 16:b // 16]), T.Zb[:, c:d], A.add, R + ["Zb%d" % c], ["Z%d" % c])
+            zq, zs, zk = T.zq[:, 128 * h:128 * h + 128], T.zs[:, 128 * h:128 * h + 128], "zq%d" % h
+            if h == 0 and r in ZR:
+                zq, zs, zk = lq[:, 128:256], lsc[:, 128:256], "zo%d" % r
+            qz(128, zq, zs, T.Z[:, 512 * h:512 * h + 512], ["Z%d" % (512 * h + a) for a in ZCUT[h][:-1]], [zk])
+            if h == 0 and r in ZR:
+                exchange(peer, [(lq[:, 0:128].bitcast(dt.uint8), zq.bitcast(dt.uint8), 64, [zk]), (lsc[:, 0:128], zs, 80, [zk])],
+                         "aq%d" % r, "lq%d" % r)
+                zq, zs, zk = lq[:, 0:128], lsc[:, 0:128], "lq%d" % r
             for k in range(4):
-                mm(b0 + k, 128, T.wq[:, 128 * k:128 * k + 128], T.wsc[:, 128 * k:128 * k + 128],
-                   T.zq[:, 128 * h:128 * h + 128], T.zs[:, 128 * h:128 * h + 128], ["w", "zq%d" % h])
+                mm(banks[k], 128, T.wq[:, 128 * k:128 * k + 128], T.wsc[:, 128 * k:128 * k + 128], zq, zs, ["w0", "w1_", zk])
+            for k in range(4):
+                lin(128, T.V[:, 256 * k + 128 * h:256 * k + 128 * h + 128], bank(banks[k], 0, 128), 0.03125, 0.0,
+                    ["P%d" % banks[k]], ["V%d%d" % (h, k)])
 
-        def vcopy(q, h, k, b):
-            out = T.V[:, 256 * k + 128 * h:256 * k + 128 * h + 128]
-            if q == "s":
-                act(out, bank(b, 0, 128), F.Identity, ["P%d" % b], ["V%d%d" % (h, k)], scale=0.03125)
-            else:
-                ts(out, bank(b, 0, 128), 0.03125, None, A.mult, None, ["P%d" % b], ["V%d%d" % (h, k)])
-
-        lk = "lo%d" % r
-        gather_b(1, T.To, "To", T.oH, "oH")
-        act(T.LP[:, 0:1], T.LP[:, 0:1], F.Identity, ["LP"], ["LP"], bias=T.LP[:, 256:257])
-        gather_b(0, T.Tp, "Tp", lo, lk)
-        gather_a(1, 0, T.To, "To", T.oH, "oH")
-        gather_a(1, 1, T.To, "To", T.oH, "oH")
-        gather_a(0, 0, T.Tp, "Tp", lo, lk)
-        quant_z(1)
-        layer(1, 4)
-        gather_a(0, 1, T.Tp, "Tp", lo, lk)
-        for k in range(4):
-            vcopy("s", 1, k, 4 + k)
-        cp(T.LR[:, 0:128], T.LP[:, 0:256].indirect(T.pos[:, 0:8]), ["LP", "pos"], ["LR0"])
-        quant_z(0)
-        layer(0, 0)
-        cp(T.LR[:, 128:256], T.LP[:, 0:256].indirect(T.pos[:, 8:16]), ["LP", "pos"], ["LR1"])
-        scan(T.sL[:, 0:128], T.m4[:, 0:128], T.LR[:, 0:128], 0.0, A.add, A.min, ["m4", "LR0"], ["sL0"])
-        scan(T.sL[:, 128:256], T.m4[:, 128:256], T.LR[:, 128:256], 0.0, A.add, A.min, ["m4", "LR1"], ["sL1"])
-        ts(T.oL[:, 0:32], T.sL[:, 3:128:4], col(1), None, A.add, None, ["sL0", "c1"], ["oL0"])
-        for k in range(4):
-            vcopy("v" if k in NV else "s", 0, k, k)
-        ts(T.oL[:, 32:64], T.sL[:, 131:256:4], col(1), None, A.add, None, ["sL1", "c1"], ["oL1"])
-
-    act(T.LF[:], T.LR[:], F.Identity, ["LR0", "LR1"], ["LF"])
-    dma("y", T.lb[:], T.LF[0:128:16, :], ["LF"], ["lb"], "o1")
-    state(3, 0, 512, ["X30"])
-    state(3, 512, 640, ["X31"])
+    now[0] = 3
+    lin(256, T.LF[:], T.LR[:], 1.0, -1.0, ["LR0", "LR1"], ["LF"])
+    dma("y", 8, T.lb[:], T.LF[0:128:16, :], ["LF"], ["lb"], "o1")
     for h in range(2):
         a, b = 128 * h, 128 * h + 128
-        if h == 1:
-            state(3, 640, 1024, ["X32"])
-        quant(3, h)
+        state(3, h)
         key = "xq3%d" % h
         mm(4 + h, 128, T.vq[:], T.vs[:], T.xq3[:, a:b], T.xs3[:, a:b], ["vq", key])
-        dma("y", T.oc[:, 4 * a:4 * b], T.xq3[:, a:b].bitcast(dt.uint8), [key], ["oc%d" % h], "o1")
+        dma("y", 64, T.oc[:, 4 * a:4 * b], T.xq3[:, a:b].bitcast(dt.uint8), [key], ["oc%d" % h], "o1")
         if h == 0:
-            act(T.yo[:, a:b], bank(4, 0, 128), F.Identity, ["P4"], ["yo0"])
-            dma("s", T.y[:, a:b], T.yo[:, a:b], ["yo0"], ["y0"], "o2")
+            act(h_, T.yo[:, a:b], bank(4, 0, 128), F.Identity, ["P4"], ["yo0"])
+            dma("s", 64, T.y[:, a:b], T.yo[:, a:b], ["yo0"], ["y0"], "o2")
         else:
-            cp(T.yo[:, a:b], bank(5, 0, 128), ["P5"], ["yo1"])
+            cp(h_, T.yo[:, a:b], bank(5, 0, 128), ["P5"], ["yo1"])
             for k in range(4):
-                dma("s" if k < 3 else "y", T.osc[4 * k:4 * k + 4, :], T.xs3[32 * k:32 * k + 4, :], ["xq30", "xq31"],
+                dma("s" if k < 3 else "y", 1, T.osc[4 * k:4 * k + 4, :], T.xs3[32 * k:32 * k + 4, :], ["xq30", "xq31"],
                     ["osc%d" % k], "o2" if k < 3 else "o1")
-            dma("y", T.y[:, a:b], T.yo[:, a:b], ["yo1"], ["y1o"], "o1")
+            dma("y", 64, T.y[:, a:b], T.yo[:, a:b], ["yo1"], ["y1o"], "o1")
 
-    g.wait_ge(T.sem.sent, nsent[0])
-    for s_, v_ in cnt.items():
-        need("y", (s_, v_))
+    order = listed_order(ops) if ORDER else issue_order(ops)
+    count, mark = {}, {}
+    for q in order:
+        for n in order[q]:
+            count[ops[n]["sem"]] = count.get(ops[n]["sem"], 0) + ops[n]["inc"]
+            mark[n] = count[ops[n]["sem"]]
+    for q in Q:
+        seen = {}
+        for n in order[q]:
+            want = {}
+            for d in ops[n]["after"]:
+                want[ops[d]["sem"]] = max(want.get(ops[d]["sem"], 0), mark[d])
+            for sem, val in want.items():
+                if seen.get(sem, 0) < val:
+                    Q[q].wait_ge(T.sem[sem], val)
+                    seen[sem] = val
+            ins = ops[n]["fn"]()
+            if ins is not None:
+                ins.then_inc(T.sem[ops[n]["sem"]], ops[n]["inc"])
+    for sem, val in count.items():
+        g.sync.wait_ge(T.sem[sem], val)

from concourse.mybir import dt, AluOpType, ActivationFunctionType, AxisListType

A = AluOpType
F = ActivationFunctionType
MASK = [1, 2, 4]
VPL = (15, 14, 7)
ONV = ("Kp", "Bs", "al", "AB1", "LR0", "V01", "V03")
XCUT = (0, 512, 640, 832, 1024)
ZCUT = ((0, 160, 352, 512), (0, 256, 512))
BCUT = (0, 17)
ORDER = {
    "v": "c_MTw c_MTy c_pc1 X_0 c_i2 c_c5 c_MTz c_il c_sm0 c_eb c_ob00 c_ob03 c_ob02 c_ob01 X_512 c_MTx c_ul c_c0 c_eb#2 c_i4 c_pc0 c_mq1 c_oq0 c_sm1 c_g5 c_eq1 c_c1 c_c2 c_uq xq0 c_up0 c_up1 X_832 X_640 Sm0 xq1 F0 c_eq0 M7 Sm1 M160 F1 thr M161 M15 DS1 Kp Bs nt Dn M14 al DS0 c_oq1 RS7 N1 Y y1 RS15 mq0 RS14 mq1 sN mq2 c_eq3 mp sY c_eq2 sel rr pos PL O sB AB1 w3 s40 w1 so w4 w5 s41 TG oH LP Z512 Z768 LR0 zq1 Z0 Z160 Z352 sL0 zq0 sL1 oL0 c_vq V03 V01 e_yo1 oL1",
    "s": "c_X00 c_mD c_m0 c_Bsz c_c6 c_c7 c_N10 c_c3 c_Y0 c_RS0 c_c4 c_c9 c_c8 c_ob1 c_up0s c_m32 c_up1s sg4 sg2 sg1 M4 sg3 M2 sg6 M1 c_CC sg12 sg13 sg11 sg10 M3 M13 sg9 M10 sg5 M12 sg8 M11 M9 M8 M5 M6 c_mp To1 c_m4 ya To3 c_DUM To2 CRx To0 ny c_spare c_DUM#2 AB0 Ox AB3 AB2 Tp3 Tp1 Zb512 Zb768 Tp2 Tp0 LP Zb0 Zb160 Zb352 LR1 e_LF V11 V10 V13 V12 V02 V00 e_yo0 e_y0 e_osc0 e_osc1 e_osc2",
    "t": "e_P4 P4 e_P5 P5 P0 P6 P7 P1 P2 P4#2 P2#2 P2#3 P2#4 P6#2 P5#2 P3 P7#2 P2#5 P1#2 P0#2 P5#3 P6#3 P3#2 P4#3 P2#6 P7#3 P0#3 P1#3",
    "g": "c_i1b c_i1a c_i3 c_gi c_dd c_i1c c_g4 c_k16 c_CR c_ob1 send send#2 c_LPa0 c_LP0 send#3 c_LPa1 c_LP1 send#4 c_LPa2 c_LP2",
    "y": "c_ub c_X01 c_w1_ c_vb c_w0 e_lb e_oc0 e_oc1 e_osc3 e_y1o",
}
VPL = (1, 2, 3, 4, 8, 9, 10)
ONV = ("Kp", "Bs", "al", "AB1", "LR0", "V01", "V03", "ny", "Ox", "CRx")
ORDER["v"] = "c_MTy c_MTw c_pc1 c_i2 c_MTz c_c5 c_il c_sm0 c_c0 c_eb c_ob00 c_ob03 c_ob01 c_ob02 c_ul c_MTx c_eb#2 c_i4 c_pc0 c_mq1 c_oq0 c_c6 c_c7 c_eq1 c_sm1 c_g5 c_c8 c_c1 c_spare c_c2 c_eq0 c_uq X_0 X_512 xq0 c_up0 X_640 X_832 c_up1 Sm0 xq1 F0 c_CC c_DUM M160 M1 M2 Sm1 M4 M3 F1 thr DS0 RS1 RS2 Kp Bs nt M161 M8 M10 M9 c_eq2 c_eq3 al RS3 RS4 mq2 Dn DS1 c_oq1 N1 Y RS8 RS9 RS10 c_DUM#2 mq0 sY y1 sN mq1 ny mp w1 PL sel sB pos w3 O rr AB1 Ox s40 w5 so w4 CRx s41 TG oH LP Z512 LP#2 Z768 LR0 zq1 Z0 Z160 sL0 Z352 sL1 zq0 oL0 oL1 c_vq V01 V03 e_yo1"
ORDER["s"] = "c_X00 c_mD c_m0 c_ob1 c_m32 c_up0s c_up1s sg7 sg6 sg5 M7 M6 M5 sg15 sg14 sg13 M15 M14 M13 sg12 sg11 c_mp M12 M11 c_m4 ya To0 To1 To2 To3 Tp0 Tp1 AB0 AB3 AB2 Tp2 Tp3 Zb512 Zb768 LR1 Zb0 Zb160 Zb352 V10 V11 V12 V13 V00 V02 e_LF e_yo0 e_y0 e_osc0 e_osc1 e_osc2"
ORDER["t"] = "P4 P5 P0 P6 P1 P7 P3 P5#2 P4#2 P6#2 P2 P2#2 P2#3 P2#4 P0#2 P1#2 P7#2 P2#5 P3#2 P4#3 P5#3 P6#3 P0#3 P1#3 P2#6 P7#3 e_P4 e_P5"
ORDER["g"] = "c_i1b c_i1a c_gi c_i3 c_dd c_i1c c_g4 c_g8 c_k16 c_k17 c_ob1 c_N10 c_Y0 c_Bsz c_RS0 c_CR send send#2 c_LPa0 c_LP0 send#3 c_LPa1 c_LP1 send#4 c_LPa2 c_LP2"
XCUT = (512, 640, 832, 1024)
VPL = (15, 14, 7)
ONV = ("thr1", "Kp1", "Bs1", "al1", "AB1", "LR0", "Ox")
ORDER["v"] = "c_MTy c_MTw c_pc1 c_i2 c_MTz c_c5 c_il c_sm0 c_c0 c_eb c_ob00 c_ob03 c_ob01 c_ob02 c_ul c_MTx c_eb#2 c_sm3 c_sm4 c_i4 c_pc0 c_mq1 c_oq0 c_c6 c_c7 c_eq1 c_sm5 c_sm1 c_g5 c_c8 c_c1 c_c3 c_spare c_c2 c_eq0 c_CC c_DUM c_uq X_0 X_1 X_2 X_3 X_512 xq0 c_up0 X_640 c_up1 X_832 Sm0 thr0 xq1 F0 nt0 c_eq2 Kp0 Bs0 al0 M160 M7 Dn0 N0 Sm1 DS0 RS7 Y0 F1 thr1 sN0 sY0 M15 nt1 M14 M13 M12 M9 M8 Kp1 Bs1 M161 al1 c_eq3 RS15 Dn1 N1 c_oq1 RS14 RS13 RS12 RS9 RS8 DS1 mq0 Y1 y1 c_DUM#2 mq1 sY1 sN1 mq2 ny mp sB0 sB1 sel PL w1 w3 pos rr w5 O w4 Ox AB0 AB1 TG CRx s40 so AB2 AB3 s41 LP oH Z512 LP#2 Z768 LR0 LR1 zq1 Z0 sL0 Z160 sL1 Z352 oL0 oL1 zq0 c_vq V10 V11 V12 V13 V00 V01 V02 V03 e_yo1"
ORDER["s"] = "c_X00 c_mD c_m0 c_ob1 c_m32 c_m16 c_up0s c_up1s sgt thr0 Kp0 Bs0 sg7 sg6 sg5 al0 sg4 sg3 sg2 sg1 M7 M6 M5 M4 M3 M2 M1 sg15 sg14 sg13 sg12 sg11 sgt#2 thr1 M15 M14 M13 Kp1 Bs1 M12 sg10 al1 sg9 M11 sg8 M10 M9 M8 c_mp c_m4 To1 ya ny To2 To3 To0 Tp0 Tp1 AB0 AB1 Ox AB3 AB2 CRx Tp2 Tp3 Zb512 Zb768 LR0 Zb0 Zb160 Zb352 LR1 V10 V11 V12 V13 V00 V01 V02 V03 e_LF e_yo0 e_y0 e_osc0 e_osc1 e_osc2"
ORDER["t"] = "P4 P6 P5 P7 P0 P2 P1 P3 P4#2 P5#2 P2#2 P6#2 P3#2 P2#3 P2#4 P2#5 P0#2 P1#2 P7#2 P2#6 P3#3 P4#3 P5#3 P6#3 P0#3 P1#3 P2#7 P7#3 e_P4 e_P5"
ORDER["g"] = "c_i1b c_i1a c_gi c_i3 c_dd c_i1c c_g4 c_g8 c_k16 c_k17 c_Ni c_Yi c_Bsz c_ob1 c_RS0 c_CR send send#2 c_LPa0 c_LP0 send#3 c_LPa1 c_LP1 send#4 c_LPa2 c_LP2"
SUMS0 = ((0, 256, "mq0"), (384, 576, "mq1"), (576, 704, "mq1"), (256, 384, "mq2"))
XCUT = (512, 640, 1024)
VPL = (15, 14, 9, 7)
ONV = ("thr1", "Kp1", "Bs1", "al1", "AB1")
ORDER["v"] = "c_MTy c_MTw c_pc1 c_i2 c_MTz c_c5 c_il c_sm0 c_c0 c_eb c_ob00 c_ob03 c_ob01 c_ob02 c_ul c_MTx c_eb#2 c_sm3 c_sm4 c_i4 c_pc0 c_mq1 c_oq0 c_c6 c_c7 c_eq1 c_sm5 c_sm1 c_g5 c_c8 c_c1 c_c3 c_spare c_c2 c_uq c_eq0 X_0 c_up0 X_1 X_2 X_3 X_512 xq0 c_up1 c_CC c_DUM X_640 Sm0 xq1 c_eq2 F0 c_DUM#2 c_eq3 c_oq1 M160 M7 nt0 Sm1 thr1 F1 Dn0 nt1 DS0 M14 Y0 M161 M15 RS14 Kp1 N0 DS1 M9 mq0 Bs1 al1 RS7 RS15 mq1 RS9 y1 Dn1 mq2 mp Y1 sY0 N1 sY1 c_vq sel sN0 sN1 pos sB1 PL O sB0 AB1 w3 w1 s40 rr so w4 w5 s41 TG oH LP Z512 Z768 LP#2 Z0 zq1 Z160 e_yo1 Z352 sL0 zq0 sL1 oL0 oL1"
ORDER["s"] = "c_X00 c_mD c_m0 c_ob1 c_m32 c_m16 c_up0s c_up1s c_mp sgt thr0 Bs0 Kp0 sg4 sg1 sg5 sg2 sg3 M4 M1 al0 sg6 M3 sg10 sg13 sg12 sg11 M13 M10 M12 M2 M11 sg8 M5 M6 M8 c_m4 To1 To0 ya ny To2 To3 Tp1 Tp2 AB0 Ox AB3 AB2 CRx Tp3 Tp0 Zb512 Zb768 Zb0 Zb160 e_LF e_yo0 Zb352 LR0 V13 V10 LR1 e_y0 V12 V11 V00 V01 e_osc2 V03 e_osc1 e_osc0 V02"
ORDER["t"] = "P4 P6 P5 P7 P0 P2 P3 P1 P4#2 P5#2 P6#2 P2#2 P3#2 P2#3 P2#4 P2#5 P1#2 P2#6 P0#2 P7#2 P3#3 P6#3 P4#3 P5#3 P0#3 P1#3 e_P4 P7#3 e_P5 P2#7"
ORDER["g"] = "c_i1b c_i1a c_gi c_i3 c_dd c_i1c c_g4 c_g8 c_k16 c_k17 c_Ni c_Yi c_Bsz c_ob1 c_RS0 c_CR send send#2 c_LPa0 c_LP0 c_LPa1 c_LP1 c_LPa2 send#3 c_LP2 send#4"
FIRST = ("xq0", "xq1", "P0", "P1", "Sm1", "F1")
VPL = (15, 14, 9)
ONV = ("thr0", "thr1", "Kp0", "Kp1", "Bs0", "Bs1", "al0", "al1", "AB1", "V00", "V01", "ny", "Ox")
ZCUT = ((0, 256, 512), (0, 256, 512))
ORDER["v"] = "c_MTy c_MTw c_pc1 c_i2 c_MTz c_c5 c_il c_sm0 c_c0 c_eb c_ob00 c_ob03 c_ob01 c_ob02 c_ul c_MTx c_eb#2 c_sm3 c_sm4 c_i4 c_pc0 c_mq1 c_oq0 c_sm5 c_eq1 c_sm1 c_g5 c_eq0 c_c1 c_c2 c_eq2 c_eq3 c_uq a_xq0 a_xq1 c_up0 c_up1 c_oq1 X_0 X_1 X_2 X_3 X_512 xq0 X_640 Sm0 xq1 F0 a_Sm1 thr0 M160 a_F1 Kp0 nt0 Sm1 Bs0 F1 thr1 al0 M15 M161 M14 nt1 M9 N0 Dn0 Kp1 al1 DS1 Y0 Bs1 RS15 sY0 DS0 Dn1 mq0 mq1 RS9 y1 c_vq mq2 RS14 N1 Y1 mp sN1 sY1 sel sB0 sN0 pos sB1 PL O ny Ox w3 AB1 rr w1 s40 w5 w4 so TG s41 oH LP Z512 Z768 LP#2 zq1 Z0 Z256 zq0 sL1 sL0 oL1 oL0 V00 V01 e_yo1"
ORDER["s"] = "c_X00 c_c6 c_c3 c_c7 c_mD c_m0 c_spare c_ob1 c_c8 c_m32 c_m16 c_CC c_DUM c_mp c_DUM#2 c_up0s c_up1s sg1 sg4 sg7 sg2 sg3 sg6 sg5 M1 M4 M3 M2 sg11 sg10 sg13 sg12 M10 sg8 M13 M12 M11 M8 M5 M6 M7 To1 ya To0 c_m4 To3 To2 Tp1 AB0 AB2 AB3 Tp2 CRx Tp0 Tp3 Zb512 Zb768 Zb0 Zb256 LR1 V10 LR0 V12 V13 V11 V02 V03 e_LF e_yo0 e_y0 e_osc0 e_osc1 e_osc2"
ORDER["t"] = "P4 a_P0 P6 P5 P7 a_P1 P0 P1 P2 P6#2 P3 P4#2 P5#2 P3#2 P2#2 P2#3 P2#4 P2#5 P1#2 P0#2 P2#6 P7#2 P4#3 P3#3 P6#3 P5#3 P0#3 P1#3 P2#7 P7#3 e_P4 e_P5"
ORDER["g"] = "c_i1b c_i1a c_gi c_i3 c_dd c_i1c c_g4 c_g8 c_k16 c_k17 c_Ni c_Yi c_Bsz c_ob1 c_RS0 c_CR send send#2 c_LPa0 c_LP0 c_LPa1 c_LP1 c_LPa2 send#3 c_LP2 send#4"
WHOLE = True
VPL = (15, 14, 7)
ONV = ("AB1", "Kp1", "Bs1", "al1")
ORDER["v"] = "c_MTy c_MTw c_pc1 c_i2 c_MTz c_c5 c_il c_sm0 c_c0 c_eb c_ob00 c_ob03 c_ob01 c_ob02 c_ul c_MTx c_eb#2 c_sm3 c_sm4 c_i4 c_pc0 c_mq1 c_oq0 c_sm5 c_eq1 c_sm1 c_g5 c_eq0 c_c1 c_c2 c_uq a_xq0 c_up0 c_up1 X_0 X_1 X_2 X_3 X_512 xq0 X_640 a_xq1 Sm0 c_eq2 xq1 c_eq3 F0 c_oq1 a_Sm1 M7 Sm1 thr1 a_F1 F1 nt1 M14 c_vq M161 M15 Kp1 M160 Bs1 RS15 al1 Dn1 DS1 N1 DS0 mq0 Y1 RS7 mq1 RS14 y1 mq2 sN1 mp sY1 sel PL pos rr O sB1 w5 AB1 w3 w1 s40 w4 so s41 TG oH LP Z512 Z768 zq1 Z0 Z256 sL1 sL0 zq0 oL1 oL0 e_yo1"
ORDER["s"] = "c_X00 c_c6 c_c3 c_c7 c_mD c_m0 c_spare c_ob1 c_c8 c_m32 c_m16 c_CC c_DUM c_up0s c_up1s c_mp c_DUM#2 sg2 sg3 sg1 sg6 M3 sg4 M2 M1 sg5 sg13 sg11 sg9 sg12 sg10 M13 M10 M11 M12 M9 M4 sg8 M5 M6 M8 c_m4 ya ny To1 To0 CRx To2 To3 Ox AB0 AB3 AB2 Tp3 Tp2 Tp0 Zb512 Zb768 Tp1 LP Zb0 Zb256 LR1 LR0 V10 V11 V12 V13 V00 V01 V02 V03 e_LF e_yo0 e_y0 e_osc0 e_osc1 e_osc2"
ORDER["t"] = "P4 a_P0 P5 P0 P6 a_P1 P7 P1 P3 P6#2 P4#2 P5#2 P2 P2#2 P2#3 P2#4 P2#5 P0#2 P1#2 P7#2 P3#2 P4#3 P5#3 P6#3 P0#3 P1#3 P2#6 P7#3 e_P4 e_P5"
ORDER["g"] = "c_i1b c_i1a c_gi c_i3 c_dd c_i1c c_g4 c_g8 c_k16 c_k17 c_Ni c_Yi c_Bsz c_ob1 c_RS0 c_CR send send#2 c_LPa0 c_LP0 c_LPa1 c_LP1 c_LPa2 send#3 c_LP2 send#4"
XQ = "y"
ORDER["y"] = "c_ub c_X00 c_X01 c_w0 c_w1_ c_vb e_lb e_oc0 e_oc1 e_y1o e_osc3"
ZR = ()
WHOLE = False
VPL = (15, 14, 13)
ONV = ("thr0", "thr1", "Kp0", "Kp1", "Bs0", "Bs1", "al0", "al1", "AB1", "V00", "V01", "Ox")
ORDER["v"] = "c_MTy c_MTw c_pc1 c_i2 c_MTz c_c5 c_il c_sm0 c_c0 c_ul c_eb c_ob00 c_ob03 c_ob01 c_ob02 c_MTx c_eb#2 c_sm3 c_sm4 c_i4 c_pc0 c_mq1 c_oq0 c_sm5 c_eq1 c_sm1 c_g5 c_eq0 c_c1 c_c2 c_uq c_eq2 c_up0 a_xq0 c_up1 a_xq1 c_eq3 c_oq1 X_0 X_1 X_2 X_3 X_512 xq0 X_640 Sm0 xq1 F0 thr0 a_Sm1 M160 Bs0 a_F1 Sm1 nt0 Kp0 F1 thr1 DS0 M161 nt1 N0 M13 M14 Bs1 Kp1 al0 M15 RS13 Dn0 al1 Dn1 DS1 mq0 y1 RS15 Y0 mq1 RS14 mq2 Y1 sY0 mp sY1 N1 sel sN1 sN0 pos sB0 PL O sB1 AB1 Ox w3 w1 s40 rr w4 w5 so s41 TG oH LP Z512 Z768 Z0 zq1 Z256 sL0 sL1 zq0 c_vq oL0 oL1 V00 V01 e_yo1"
ORDER["s"] = "c_c6 c_c3 c_c7 c_mD c_m0 c_spare c_ob1 c_c8 c_m32 c_m16 c_CC c_DUM c_up0s c_up1s c_mp c_DUM#2 sg7 sg3 sg4 sg2 sg5 sg6 M7 M2 sg1 M4 sg11 sg10 sg12 sg9 M3 M10 M1 sg8 M9 M11 M12 M6 M5 M8 c_m4 ya ny To3 To0 To2 To1 AB0 AB3 AB2 Tp1 CRx Tp2 Tp3 Zb512 Tp0 Zb768 Zb0 LP Zb256 LR0 LR1 V10 V11 V12 V13 V02 V03 e_LF e_yo0 e_y0 e_osc1 e_osc0 e_osc2"
ORDER["t"] = "P4 P5 a_P0 P6 a_P1 P0 P7 P2 P1 P3 P3#2 P6#2 P5#2 P4#2 P2#2 P2#3 P2#4 P2#5 P1#2 P2#6 P7#2 P0#2 P3#3 P4#3 P5#3 P6#3 P0#3 P1#3 P2#7 P7#3 e_P4 e_P5"
ORDER["g"] = "c_i1b c_i1a c_i3 c_gi c_dd c_i1c c_g4 c_g8 c_k16 c_k17 c_Ni c_Yi c_Bsz c_ob1 c_RS0 c_CR send send#2 c_LPa0 c_LP0 c_LPa1 c_LP1 c_LPa2 send#3 c_LP2 send#4"
ONV = ("thr0", "thr1", "Kp0", "Kp1", "Bs0", "Bs1", "al0", "al1", "AB1", "V00")
ORDER["v"] = "c_MTy c_MTw c_pc1 c_i2 c_MTz c_c5 c_il c_sm0 c_c0 c_ul c_eb c_ob00 c_ob03 c_ob01 c_ob02 c_MTx c_eb#2 c_sm3 c_sm4 c_i4 c_pc0 c_mq1 c_oq0 c_sm5 c_eq1 c_sm1 c_g5 c_eq0 c_c1 c_c2 c_uq c_eq2 c_up0 a_xq0 c_up1 c_eq3 c_oq1 X_0 X_1 X_2 X_3 X_512 xq0 X_640 Sm0 a_xq1 xq1 F0 thr0 M160 Kp0 Bs0 Sm1 a_Sm1 DS0 thr1 F1 a_F1 Dn0 Bs1 M14 M161 nt0 M13 al0 nt1 N0 M15 DS1 RS14 al1 Kp1 Y0 mq0 Dn1 RS15 mq1 y1 mq2 RS13 Y1 sY0 mp N1 sY1 sel sN0 sN1 pos sB0 PL O sB1 rr AB1 w3 w1 s40 so w5 w4 s41 TG oH LP Z512 Z768 Z0 zq1 Z256 c_vq sL1 zq0 sL0 oL0 V00 oL1 e_yo1"
ORDER["s"] = "c_c6 c_c3 c_c7 c_mD c_m0 c_spare c_ob1 c_c8 c_m32 c_m16 c_CC c_DUM c_up0s c_up1s c_mp c_DUM#2 sg2 sg7 sg3 sg4 sg1 sg5 M3 M2 M1 M5 sg6 M4 sg8 sg9 sg10 sg11 sg12 M9 M10 M11 M12 M8 M7 M6 c_m4 To3 To2 ya To1 Tp1 Tp3 ny Tp0 AB0 Ox AB3 AB2 CRx To0 Tp2 Zb512 Zb768 Zb0 LP Zb256 LR1 LR0 V10 V11 V12 V13 V01 V02 V03 e_LF e_yo0 e_y0 e_osc2 e_osc0 e_osc1"
ORDER["t"] = "P4 P6 P5 P0 a_P0 P2 P1 P3 P6#2 P7 a_P1 P4#2 P3#2 P5#2 P2#2 P2#3 P2#4 P2#5 P1#2 P7#2 P0#2 P2#6 P3#3 P4#3 P5#3 P6#3 P0#3 P1#3 P2#7 P7#3 e_P4 e_P5"
OWN, FAR = (3, 4, 5, 6), (0, 1, 2, 7)
WAKE, LOCAL, REMOTE, PER_KB = 200, 1500, 1400, 10
PASSES = 8
BF, F32, I32, U16, Q4, U8 = "bfloat16", "float32", "int32", "uint16", "float8_e4m3fn_x4", "uint8"

SCRATCH = {"P": ("psum", [128, 4096], F32)}
for _d, _names in (
    (BF, "ub:512 vb:512 sm:96 mD:272 m0:256 m16:128 m4:256 dd:128 gi:128 eb:516 ob:1024 CR:288 "
         "MT:2816 sg:2048 DS:256 O:272 thr:256 nt:256 al:256 Kp:256 Bs:288 N1:256 Dn:256 Y:256 "
         "rr:256 sN:512 m32:256 sB:256 LP0:592 LP1:592 LP2:592 LR:256 sL:256 AB:512 s4:512 "
         "To:1024 Tp:1024 Zb:1024 Z:1024 V:1024 X0:1024 X1:1024 X2:1024 X3:1024"),
    (F32, "cf:16 g4:16 mp:256 k16:32 CC:16 DUM:16 Sm:256 Fs:256 RS:2048 y1:16 sel:256 sY:256 w1:96 LF:256 yo:256"),
    (I32, "i1:56 i2:40 i3:24 i4:16 pc:8"),
    (U16, "ul:24 il:18 pos:16 PL:32 TG:18 oL:64 oH:64 so0:64 so1:64 so2:64 lo0:64 lo1:64 lo2:64"),
    (Q4, "uq:128 upq:384 vq:128 wq:512 eq:512 oq:256 mq:704 zq:256 xq0:256 xq1:256 xq2:256 xq3:256 lq0:256 lq1:256 lq2:256"),
    (U8, "us:128 ups:384 vs:128 wsc:512 es:512 osn:256 ms:704 zs:256 xs0:256 xs1:256 xs2:256 xs3:256 ls0:256 ls1:256 ls2:256"),
):
    for _e in _names.split():
        SCRATCH[_e.split(":")[0]] = ("sbuf", [128, int(_e.split(":")[1])], _d)

SEMAPHORES = ["v", "s", "t", "g", "dx0", "dx1", "du", "dw0", "dw1", "dv", "o1", "o2", "sent",
              "aq0", "aq1", "aq2", "al0", "al1", "al2"]

TILE0 = {0: 0, 1: 384, 2: 256, 3: 576}
SUMS = ((0, 256, "mq0"), (256, 384, "mq2"), (576, 704, "mq1"), (384, 576, "mq1"))
SUMS = SUMS0
MTZ = ["MTw", "MTx", "MTy", "MTz"]


def plane(k):
    n = 16 - k
    return TILE0[n // 4], n % 4


def pieces(cuts):
    return list(zip(cuts[:-1], cuts[1:]))


def issue_order(ops):
    ids = range(len(ops))
    before = [[(d, ops[d]["lat"] + WAKE) for d in o["after"]] + [(d, 0.0) for d in o["behind"]] for o in ops]
    behind = [[] for _ in ids]
    for n in ids:
        for d, gap in before[n]:
            behind[d].append((n, gap))

    def place(turn, edges, first):
        lines, end = {}, {}
        for n in turn:
            busy = ops[n]["busy"]
            t = max([first(n)] + [end[d] + gap for d, gap in edges[n]])
            line = lines.setdefault(ops[n]["q"], [])
            at = len(line)
            for i, (a, b, _) in enumerate(line):
                if t + busy <= a:
                    at = i
                    break
                t = max(t, b)
            line.insert(at, (t, t + busy, n))
            end[n] = t + busy
        return lines, end

    back = {}
    for n in reversed(ids):
        back[n] = ops[n]["busy"] + max([ops[n]["lat"]] + [back[d] + gap for d, gap in behind[n]])
    best = None
    for _ in range(PASSES):
        lines, end = place(sorted(ids, key=lambda n: (-back[n], n)), before, lambda n: 0.0)
        total = max(end[n] + ops[n]["lat"] for n in ids)
        if best is None or total < best[0]:
            best = (total, lines)
        back = place(sorted(ids, key=lambda n: (-end[n], -n)), behind, lambda n: ops[n]["lat"])[1]
    return {q: [n for _, _, n in line] for q, line in best[1].items()}


def listed_order(ops):
    place = {(q, k): i for q, text in ORDER.items() for i, k in enumerate(text.split())}
    order = {}
    for n, o in enumerate(ops):
        order.setdefault(o["q"], []).append(n)
    return {q: sorted(l, key=lambda n: (max(ops[n]["rnd"], 0), place.get((q, ops[n]["name"]), 0), n)) for q, l in order.items()}


def rank_program(g, core, T, topo):
    rank = T.rank_of(core)
    if rank is None:
        return
    Q = {"v": g.vector, "s": g.scalar, "t": g.tensor, "g": g, "y": g.sync}
    ops, lastw, readers = [], {}, {}
    now, named, late = [-1], {}, [False]

    def name(q, W):
        k = W[0] if W else "send"
        for head in ("X", "xq", "LP", "lq", "lo", "so"):
            if now[0] >= 0 and k.startswith(head) and k[len(head)].isdigit():
                k = head + k[len(head) + 1:]
        k = ("c_" if now[0] < 0 else "e_" if now[0] == 3 and k[0] not in "Xx" else "") + k
        c = named[now[0], q, k] = named.get((now[0], q, k), 0) + 1
        k = k if c == 1 else "%s#%d" % (k, c)
        if now[0] in ZR and (W and W[0][:2] in ("Zb", "Z0", "Z2", "Z5", "Z7", "zq", "zo", "s4", "oH", "LP", "LR", "sL", "oL", "TG", "V0", "V1") or late[0] and q == "t"):
            return "z_" + k.replace("zo1", "zo").replace("zo2", "zo")
        return "a_" + k if now[0] == 0 and k in FIRST else k

    def op(q, busy, fn, R=(), W=(), sem=None, inc=1, lat=0.0, acc=False, behind=()):
        after, behind = set(), set(behind)
        for k in R:
            if k in lastw:
                after.add(lastw[k])
            if k[0] == "P" and k[1:].isdigit():
                after.update(d for d in readers.get(k, []) if ops[d]["q"] != q)
        for k in W:
            if k in lastw:
                (behind if acc else after).add(lastw[k])
            after.update(readers.get(k, []))
        ops.append(dict(q=q, busy=busy, fn=fn, after=after, behind=behind, sem=sem or q, inc=inc, lat=lat,
                        rnd=now[0], name=name(q, W)))
        for k in R:
            readers.setdefault(k, []).append(len(ops) - 1)
        for k in W:
            lastw[k] = len(ops) - 1
            readers[k] = []
        return len(ops) - 1

    vec, sca, ten = g.vector, g.scalar, g.tensor

    def cyc(n):
        return max(64, n) * 0.83

    def pick(n):
        return 55 + 1.25 * n

    def ts(c, out, in0, s1, s2, o0, o1, R, W):
        if o1 is None:
            op("v", c, lambda: vec.tensor_scalar(out, in0, s1, None, o0), R, W)
        else:
            op("v", c, lambda: vec.tensor_scalar(out, in0, s1, s2, o0, o1), R, W)

    def tt(c, out, a, b, o, R, W):
        op("v", c, lambda: vec.tensor_tensor(out, a, b, o), R, W)

    def scan(c, out, d0, d1, init, o0, o1, R, W):
        op("v", c, lambda: vec.tensor_tensor_scan(out, d0, d1, init, o0, o1), R, W)

    def cp(c, out, in_, R, W):
        op("v", c, lambda: vec.tensor_copy(out, in_), R, W)

    def ms(c, ap, x, W):
        op("v", c, lambda: vec.memset(ap, x), (), W)

    def act(c, out, in_, f, R, W, **kw):
        op("s", c, lambda: sca.activation(out, in_, f, **kw), R, W)

    def lin(n, out, in_, scale, bias, R, W, narrow=False):
        if W[0] in ONV:
            ts(cyc(n / 2 if narrow else n), out, in_, scale, bias, A.mult, A.add, R, W)
        else:
            act(cyc(n), out, in_, F.Identity, R, W, scale=scale, bias=bias)

    def gather(n, out, in_, R, W):
        if W[0] in ONV:
            cp(pick(n), out, in_, R, W)
        else:
            act(pick(n), out, in_, F.Identity, R, W)

    def qz(n, q, s, in_, R, W):
        op("v", 12 + 0.88 * n, lambda: vec.quantize_mx(q, s, in_), R, W)

    def mm(bank, n, lq, lsc, rq, rsc, R, start=True, stop=True):
        op("t", 0.6 * (n + 16), lambda: ten.matmul_mx(T.P[:, 512 * bank:512 * bank + n], lq, lsc, rq, rsc, start, stop),
           R, ["P%d" % bank], acc=not start)

    def iota(n, out, pat, base, cm, W, fl=False):
        if fl:
            op("g", 130 + 1.66 * n, lambda: g.iota(out, pat, base, cm, allow_small_or_imprecise_dtypes=True), (), W)
        else:
            op("g", 130 + 1.66 * n, lambda: g.iota(out, pat, base, cm), (), W)

    def dma(q, kb, out, in_, R, W, sem):
        op(q, 60, lambda: Q[q].dma_start(out, in_), R, W, sem=sem, inc=16, lat=LOCAL + 4 * kb)

    def bank(b, lo=0, hi=256):
        return T.P[:, 512 * b + lo:512 * b + hi]

    def col(j):
        return T.cf[:, j:j + 1]

    sends = []

    def exchange(peer, pairs, sem, key):
        eng = topo.engines(core, peer)
        rid, pid, _ = topo.addr(peer)
        mine = []
        for dst, src, kb, R in pairs:
            def fn(dst=dst, src=src):
                g.remote_dma(dst, src, T.sem[sem], T.sem.sent, pid, rid, sum(1 << e for e in eng))
            mine.append(op("g", 300 if sends else 1500, fn, R, (), sem="sent", inc=len(eng), lat=REMOTE + PER_KB * kb - WAKE, behind=sends[-1:]))
            sends.append(mine[-1])
        n = op("r", 0.0, None, (), [key], sem=sem, inc=len(topo.engines(peer, core)) * len(pairs))
        ops[n]["after"].update(mine)

    dma("y", 128, T.ub[:], T.u[:], (), ["ub"], "du")
    dma(XQ, 128, T.X0[:, 0:512], T.x[:, 0:512], (), ["X00"], "dx0")
    dma("y", 128, T.X0[:, 512:1024], T.x[:, 512:1024], (), ["X01"], "dx1")
    dma("y", 256, T.wq[:].bitcast(dt.uint8), T.wc[:], ["X01"], ["w0"], "dw0")
    dma("y", 64, T.wsc[:], T.ws[:], ["X01"], ["w1_"], "dw1")
    dma("y", 128, T.vb[:], T.v[:], ["X01"], ["vb"], "dv")

    iota(16, T.i1[:, 0:16], [[1, 16]], 128, -1, ["i1a"])
    iota(18, T.i1[:, 16:34], [[0, 18]], 0, 1, ["i1b"])
    iota(24, T.i3[:], [[1, 3], [16, 8]], 0, 0, ["i3"])
    iota(16, T.i1[:, 40:56], [[0, 4], [4, 4]], 131, -1, ["i1c"])
    iota(3, T.g4[:, 0:3], [[-4, 3]], 11, 0, ["g4"], True)
    iota(4, T.g4[:, 8:12], [[1, 2], [1024, 2]], -512, 0, ["g8"], True)
    iota(16, T.k16[:, 0:16], [[16, 16]], 1025, 0, ["k16"], True)
    iota(16, T.k16[:, 16:32], [[-16, 16]], 240, 0, ["k17"], True)
    iota(128, T.dd[:], [[1, 128]], 0, -1, ["dd"], True)
    iota(128, T.gi[:], [[1, 8], [0, 16]], 0, 0, ["gi"], True)
    iota(288, T.CR[:], [[1, 288]], 0, 0, ["CR", "CRx"], True)
    for r in range(3):
        iota(256, T["LP%d" % r][:, 0:256], [[1, 256]], 1, 0, ["LPa%d" % r], True)
        iota(1, T["LP%d" % r][:, 256:257], [[0, 1]], 0, 0, ["LP%d" % r], True)

    s_ = cyc(16)
    for key, a, b in (("MTy", 2304, 2816), ("MTx", 832, 1024), ("MTw", 1344, 1536), ("MTz", 2112, 2304)):
        ms(cyc((b - a) / 2), T.MT[:, a:b], 0.0, [key])
    ms(cyc(258), T.eb[:], 0.0, ["eb"])
    ts(s_, T.i2[:, 0:34], T.i1[:, 0:34], 15, None, A.bitwise_and, None, ["i1a", "i1b"], ["i2"])
    cp(s_, T.il[:], T.i2[:, 16:34], ["i2"], ["il"])
    ts(s_, T.sm[:, 0:16], T.i2[:, 0:16], 0.0, None, A.is_equal, None, ["i2"], ["sm0"])
    cp(s_, col(0), T.i2[:, 15:16], ["i2"], ["c0"])
    gather(272, T.mD[:], T.sm[:, 0:16].indirect(T.il[:, 0:17]), ["sm0", "il"], ["mD"])
    lin(256, T.m0[:], T.mD[:, 0:256], -1.0, 1.0, ["mD"], ["m0"], True)
    lin(256, T.m32[:], T.mD[:, 0:256], 8704.0, -512.0, ["mD"], ["m32"], True)
    lin(256, T.mp[:], T.mD[:, 1:257], 16896.0, -512.0, ["mD"], ["mp"])
    cp(s_, T.ul[:], T.i3[:], ["i3"], ["ul"])
    ts(s_, T.i4[:], T.i1[:, 40:56], 12, None, A.bitwise_and, None, ["i1c"], ["i4"])
    ts(s_, T.pc[:, 0:1], T.i1[:, 16:17], 3, None, A.bitwise_and, None, ["i1b"], ["pc0"])
    ts(s_, T.pc[:, 1:2], T.i1[:, 16:17], 4, None, A.arith_shift_right, None, ["i1b"], ["pc1"])
    ts(s_, T.sm[:, 16:32], T.i4[:], 0.0, 256.0, A.not_equal, A.mult, ["i4"], ["sm1"])
    gather(256, T.m4[:], T.sm[:, 16:32].indirect(T.il[:, 0:16]), ["sm1", "il"], ["m4"])
    ts(s_, col(1), T.pc[:, 0:1], 256.0, -1.0, A.mult, A.add, ["pc0"], ["c1"])
    cp(s_, col(5), T.pc[:, 1:2], ["pc1"], ["c5"])
    ts(s_, T.g4[:, 4:7], T.g4[:, 0:3], col(0), 2.0 ** -8, A.is_ge, A.max, ["g4", "c0"], ["g5"])
    op("v", s_, lambda: vec.tensor_reduce(col(2), T.g4[:, 4:7], AxisListType.X, A.mult), ["g5"], ["c2"])
    qz(128, T.mq[:, 576:704], T.ms[:, 576:704], T.MT[:, 2304:2816], ["MTy"], ["mq1"])
    for out, x, key in ((T.N1[:, 0:1], 255, "Ni"), (T.Y[:, 0:1], -256, "Yi"), (T.RS[:, 127:128], 0, "RS0")):
        iota(1, out, [[0, 1]], x, 0, [key], True)
    iota(2, T.Bs[:, 15:160:144], [[0, 2]], -255, 0, ["Bsz"], True)
    ts(s_, T.sm[:, 48:64], T.i2[:, 0:16], 1.0, -256.0, A.is_equal, A.mult, ["i2"], ["sm3"])
    ts(s_, T.sm[:, 64:80], T.i2[:, 0:16], 0.0, 1024.0, A.is_equal, A.mult, ["i2"], ["sm4"])
    tt(s_, T.sm[:, 80:96], T.sm[:, 48:64], T.sm[:, 64:80], A.add, ["sm3", "sm4"], ["sm5"])
    gather(128, T.m16[:], T.sm[:, 80:96].indirect(T.il[:, 0:8]), ["sm5", "il"], ["m16"])
    lin(4, T.cf[:, 8:12], T.g4[:, 8:12], col(0), 0.0, ["g8", "c0"], ["c8"])
    lin(1, col(6), T.sm[:, 15:16], 2000.0, 0.0, ["sm0"], ["c6"])
    lin(1, col(3), T.sm[:, 15:16], -256.0, 256.0, ["sm0"], ["c3"])
    lin(1, col(7), col(0), -4.0, -260.0, ["c0"], ["c7"])
    lin(16, T.CC[:], T.k16[:, 0:16], 1.0, col(11), ["k16", "c8"], ["CC"])
    lin(16, T.DUM[:], T.k16[:, 16:32], 1.0, col(10), ["k17", "c8"], ["DUM"])
    lin(1, T.sm[:, 32:33], col(7), 1.0, col(6), ["c6", "c7"], ["spare"])
    lin(1, T.DUM[:, 15:16], T.DUM[:, 15:16], 1.0, col(6), ["c6", "DUM"], ["DUM"])

    ts(s_, T.eb[:, 3:515:4], T.dd[:], 0.0, None, A.is_equal, None, ["dd"], ["eb"])
    for b in range(4):
        qz(128, T.eq[:, 128 * b:128 * b + 128], T.es[:, 128 * b:128 * b + 128], T.eb[:, 3 - b:515 - b], ["eb"], ["eq%d" % b])
    ob0 = ["ob0%d" % t for t in range(4)]
    for t in range(4):
        ts(s_, T.ob[:, t:512:4], T.gi[:], col(5), None, A.is_equal, None, ["gi", "c5"], [ob0[t]])
    lin(512, T.ob[:, 512:1024], T.ob[:, 0:512], 1.0, 0.0, ob0, ["ob1"])
    op("g", 380, lambda: g.affine_select(T.ob[:, 512:1024:4], T.ob[:, 512:1024:4], [[1, 128]], A.is_gt, 0.0, 0, -1), ["ob1"], ["ob1"])
    qz(128, T.oq[:, 0:128], T.osn[:, 0:128], T.ob[:, 0:512], ob0, ["oq0"])
    qz(128, T.oq[:, 128:256], T.osn[:, 128:256], T.ob[:, 512:1024], ["ob1"], ["oq1"])

    qz(128, T.uq[:], T.us[:], T.ub[:], ["ub"], ["uq"])
    for a, b, key in ((0, 8, "up0"), (8, 24, "up1")):
        act(pick(16 * (b - a)), T.ups[:, 16 * a:16 * b], T.us[:].indirect(T.ul[:, a:b]), F.Copy, ["uq", "ul"], [key + "s"])
        cp(pick(16 * (b - a)), T.upq[:, 16 * a:16 * b].bitcast(dt.uint32), T.uq[:].bitcast(dt.uint32).indirect(T.ul[:, a:b]),
           ["uq", "ul"], [key])
    qz(128, T.vq[:], T.vs[:], T.vb[:], ["vb"], ["vq"])

    def unpack(banks, q, s, keys, dst, key):
        for b in range(4):
            mm(banks[b], 256, T.eq[:, 128 * b:128 * b + 128], T.es[:, 128 * b:128 * b + 128], q[:], s[:], ["eq%d" % b] + keys)
        for b in range(4):
            lin(256, dst[:, 256 * b:256 * b + 256], bank(banks[b]), 0.5, 0.0, ["P%d" % banks[b]], [key + str(b)])

    def pview(k, a, b):
        c0, t = plane(k)
        return T.MT[:, 4 * (c0 + a) + t:4 * (c0 + b):4]

    def compare(k):
        n, score, fk = 16 * k, T.Fs[:, 16 * k + 15:16 * k + 16], "F%d" % (k // 8)
        if k in VPL:
            b = 4 if k < 8 else 0
            ts(cyc(n), pview(k, 0, n), bank(b, 0, n), score, None, A.is_lt, None, ["P%d" % b, fk] + MTZ, ["M%d" % k])
            scan(cyc(n / 2), T.RS[:, 128 * k + 128 - 8 * k:128 * k + 128], pview(k, 0, 8 * k), pview(k, 8 * k, n), 0.0,
                 A.add, A.add, ["M%d" % k], ["RS%d" % k])
        else:
            b, sg = (5 if k < 8 else 1), T.sg[:, 8 * k * (k - 1):8 * k * (k + 1)]
            act(cyc(n), sg, bank(b, 0, n), F.Sign, ["P%d" % b, fk], ["sg%d" % k], scale=-1.0, bias=score)
            act(cyc(n) + 20, pview(k, 0, n), sg, F.Relu, ["sg%d" % k] + MTZ, ["M%d" % k, "RS%d" % k],
                accum_out=T.RS[:, 128 * k + 127:128 * k + 128])

    def xkeys(r, h):
        return ["X0%d" % h] if r == 0 else ["X%d_%d" % (r, a) for a in (XCUT[:-1] if h else range(4))]

    def state(r, h):
        X = T["X%d" % r]
        if r > 0:
            old = T["X%d" % (r - 1)]
            for t in range(4 - 4 * h):
                tt(pick(128), X[:, t:512:4], T.V[:, 256 * t:256 * t + 256].indirect(T.oL[:, 0:8]), old[:, t:512:4], A.add,
                   ["V0%d" % t, "V1%d" % t, "oL0"] + xkeys(r - 1, 0), ["X%d_%d" % (r, t)])
            for a, b in pieces(XCUT) * h:
                R = ["V%d%d" % (n, k) for n in range(2) for k in range(4)] + ["oL1"] + xkeys(r - 1, 1)
                tt(pick(b - a), X[:, a:b], T.V[:].indirect(T.oL[:, a // 16:b // 16]), old[:, a:b], A.add, R, ["X%d_%d" % (r, a)])
        a, b = 128 * h, 128 * h + 128
        qz(128, T["xq%d" % r][:, a:b], T["xs%d" % r][:, a:b], X[:, 4 * a:4 * b], xkeys(r, h), ["xq%d%d" % (r, h)])

    def whole(xq, xs, xk):
        for j in (1, 2):
            mm(5 + j, 256, T.upq[:, 128 * j:128 * j + 128], T.ups[:, 128 * j:128 * j + 128], xq[:], xs[:], ["up1", "up1s"] + xk)
        ts(cyc(256), T.thr[:], bank(6), 0.0, U, A.is_gt, A.mult, ["P6"], ["thr1"])
        tt(cyc(256), T.nt[:], bank(7), T.thr[:], A.is_le, ["P7", "thr1"], ["nt1"])
        lin(256, T.Kp[:], T.thr[:], 511.0 / U, -256.0, ["thr1"], ["Kp1"], True)
        lin(256, T.Bs[:, 16:272], T.thr[:], -512.0 / U, 256.0, ["thr1"], ["Bs1"], True)
        lin(256, T.al[:], T.nt[:], 2.0, -1.0, ["nt1"], ["al1"], True)
        scan(h_, T.Dn[:], T.Kp[:], T.Bs[:, 15:271], 255.0, A.add, A.add, ["Kp1", "Bs1", "Bsz"], ["Dn1"])
        scan(h_, T.N1[:, 1:256], T.Kp[:, 0:255], T.Bs[:, 16:271], 255.0, A.add, A.add, ["Kp1", "Bs1"], ["N1"])
        scan(h_, T.Y[:, 1:256], T.al[:, 0:255], T.Dn[:, 0:255], -256.0, A.mult, A.max, ["al1", "Dn1"], ["Y1"])
        scan(cyc(256), T.sY[:], T.m32[:], T.Y[:], 0.0, A.add, A.min, ["m32", "Y1", "Yi"], ["sY1"])
        scan(h_, T.sN[:, 0:256], T.m0[:], T.N1[:], 0.0, A.mult, A.max, ["m0", "N1", "Ni"], ["sN1"])
        scan(h_, T.sB[:], T.m32[:], T.Bs[:, 16:272], 0.0, A.add, A.min, ["m32", "Bs1"], ["sB1"])

    def outs(h, xq, xs, xk):
        if WHOLE:
            return whole(xq, xs, xk) if h else None
        a, b, e, n, H = 128 * h, 128 * h + 128, 128 * h + 128 - h, 6 - 4 * h, str(h)
        c = 16 + 144 * h
        for j in (1, 2):
            mm(n + j - 1, 128, T.upq[:, 128 * j:128 * j + 128], T.ups[:, 128 * j:128 * j + 128], xq[:, a:b], xs[:, a:b], ["up1", "up1s", xk[h]])
        if "thr" + H in ONV:
            ts(h_, T.thr[:, a:b], bank(n, 0, 128), 0.0, U, A.is_gt, A.mult, ["P%d" % n], ["thr" + H])
        else:
            act(h_, T.sg[:, 1920:2048], bank(n, 0, 128), F.Sign, ["P%d" % n], ["sgt"])
            act(h_, T.thr[:, a:b], T.sg[:, 1920:2048], F.Relu, ["sgt"], ["thr" + H], scale=U)
        tt(h_, T.nt[:, a:b], bank(n + 1, 0, 128), T.thr[:, a:b], A.is_le, ["P%d" % (n + 1), "thr" + H], ["nt" + H])
        lin(128, T.Kp[:, a:b], T.thr[:, a:b], 511.0 / U, -256.0, ["thr" + H], ["Kp" + H], True)
        lin(128, T.Bs[:, c:c + 128], T.thr[:, a:b], -512.0 / U, 256.0, ["thr" + H], ["Bs" + H], True)
        lin(128, T.al[:, a:b], T.nt[:, a:b], 2.0, -1.0, ["nt" + H], ["al" + H], True)
        n0, y0, prev = (T.N1[:, 128:129], T.Y[:, 128:129], ["N0", "Y0"]) if h else (255.0, -256.0, ["Ni", "Yi"])
        scan(s_, T.Dn[:, a:b], T.Kp[:, a:b], T.Bs[:, c - 1:c + 127], n0, A.add, A.add, ["Kp" + H, "Bs" + H, "Bsz"] + prev[:h], ["Dn" + H])
        scan(s_, T.N1[:, a + 1:e + 1], T.Kp[:, a:e], T.Bs[:, c:c + e - a], n0, A.add, A.add, ["Kp" + H, "Bs" + H] + prev[:h], ["N" + H])
        scan(s_, T.Y[:, a + 1:e + 1], T.al[:, a:e], T.Dn[:, a:e], y0, A.mult, A.max, ["al" + H, "Dn" + H] + prev[2 - h:], ["Y" + H])
        scan(h_, T.sY[:, a:b], T.m32[:, 0:128], T.Y[:, a:b], 0.0, A.add, A.min, ["m32", "Y" + H, prev[1]], ["sY" + H])
        scan(s_, T.sN[:, a:b], T.m0[:, 0:128], T.N1[:, a:b], 0.0, A.mult, A.max, ["m0", "N" + H, prev[0]], ["sN" + H])
        scan(s_, T.sB[:, a:b], T.m32[:, 0:128], T.Bs[:, c:c + 128], 0.0, A.add, A.min, ["m32", "Bs" + H], ["sB" + H])

    def wrap4(src, dst, a, b, R, key, out, okey):
        scan(cyc((b - a) / 2), dst[:, a:b], T.m4[:, 0:b - a], src[:, a:b], 0.0, A.mult, A.max, ["m4"] + R, [key])
        ts(s_, out, dst[:, a + 3:b:4], col(2), col(1), A.mult, A.add, [key, "c1", "c2"], [okey])

    U = 2.0 ** 80
    w = [T.w1[:, 16 * n:16 * n + 16] for n in range(5)]
    h_ = cyc(128)

    for r in range(3):
        now[0], late[0] = r, False
        peer = T.cores[rank ^ MASK[r]]
        xq, xs = T["xq%d" % r], T["xs%d" % r]
        xk = ["xq%d0" % r, "xq%d1" % r]
        lq, lsc, so, lo, LP = T["lq%d" % r], T["ls%d" % r], T["so%d" % r], T["lo%d" % r], T["LP%d" % r]
        LPk, lk = "LP%d" % r, "lo%d" % r

        def scores(b, j, n):
            up = "up%d" % min(j, 1)
            mm(b, n, T.upq[:, 128 * j:128 * j + 128], T.ups[:, 128 * j:128 * j + 128], xq[:, 0:n], xs[:, 0:n], [up, up + "s"] + xk[:n // 128])

        for h in range(2):
            a, b, n = 128 * h, 128 * h + 128, 4 - 4 * h
            state(r, h)
            scores(n, 0, b)
            scores(n + 1, 0, b)
            tt(h_, T.Sm[:, a:b], bank(n, a, b), T.mD[:, a:b], A.mult, ["P%d" % n, "mD"], ["Sm%d" % h])
            scan(h_, T.Fs[:, a:b], T.m0[:, a:b], T.Sm[:, a:b], 0.0, A.mult, A.add, ["m0", "Sm%d" % h], ["F%d" % h])
            tt(h_, pview(16, a, b), bank(n, a, b), T.Fs[:, a:b], A.is_le, ["P%d" % n, "F%d" % h] + MTZ, ["M16%d" % h])
            scan(s_, T.DS[:, a:b], T.m0[:, a:b], pview(16, a, b), 0.0, A.mult, A.add, ["m0", "M16%d" % h], ["DS%d" % h])
            for k in range(8 * h + 7, max(8 * h - 1, 0), -1):
                compare(k)
            outs(h, xq, xs, xk)
        if r == 0:
            pairs = [(lq[:].bitcast(dt.uint8), xq[:].bitcast(dt.uint8), 128, xk)]
        else:
            pairs = [(lq[:, a:a + 128].bitcast(dt.uint8), xq[:, a:a + 128].bitcast(dt.uint8), 64 + a // 2, [xk[a // 128]]) for a in (0, 128)]
        if r not in ZR:
            exchange(peer, pairs + [(lsc[:], xs[:], 160, xk)], "aq%d" % r, "lq%d" % r)

        for a, b, ks, key in ((0, 256, (160, 161, 15, 14, 13), "mq0"), (384, 640, (12, 11, 10, 9, 4, 3, 2, 1), "mq1"),
                              (256, 384, (8, 7, 6, 5), "mq2")):
            qz(b - a, T.mq[:, a:b], T.ms[:, a:b], T.MT[:, 4 * a:4 * b], ["M%d" % k for k in ks] + MTZ, [key])
        for n, (a, b, key) in enumerate(SUMS):
            c = 128 if a == 0 else 0
            mm(2, b - a, T.oq[:, c:c + 128], T.osn[:, c:c + 128], T.mq[:, a:b], T.ms[:, a:b], ["oq%d" % (c // 128), key], n == 0, n == 3)
        tt(s_, T.y1[:], T.CC[:], T.DS[:, 15::16], A.subtract, ["CC", "DS0", "DS1"], ["y1"])
        tt(s_, T.mp[:, 15::16], T.y1[:], T.RS[:, 127::128], A.subtract, ["y1"] + ["RS%d" % k for k in range(16)], ["mp"])
        scan(cyc(256), T.sel[:], bank(2), T.mp[:], 2048.0, A.min, A.add, ["P2", "mp"], ["sel"])
        ts(s_, T.pos[:], T.sel[:, 15::16], -1024.0, None, A.add, None, ["sel"], ["pos"])
        cp(50 + 2.7 * 256, T.O[:, 0:256].indirect(T.pos[:]), T.CR[:, 1:257], ["pos", "CR"], ["O"])
        lin(1, T.O[:, 256:257], T.O[:, 0:1], 1.0, 0.0, ["O"], ["Ox"])

        act(s_, T.sN[:, 271::16], T.sY[:, 15::16], F.Abs, ["sY0", "sY1", "c8"], ["ya"], bias=col(9))
        lin(16, w[2], T.sY[:, 15::16], -1.0, col(8), ["sY0", "sY1", "c8"], ["ny"])
        ts(s_, T.PL[:], T.sN[:, 15::16], -1.0, 256.0, A.mult, A.add, ["sN0", "sN1", "ya"], ["PL"])
        scan(h_, T.rr[:, 0:255], T.nt[:, 0:255], T.nt[:, 0:255], -2.0, A.mult, A.add, ["nt0", "nt1"], ["rr"])
        lin(1, T.CR[:, 272:273], T.rr[:, 254:255], -1.0, 255.0, ["rr"], ["CRx"])
        tt(s_, w[1], w[2], T.sN[:, 15:256:16], A.max, ["ny", "sN0", "sN1"], ["w1"])
        tt(s_, w[3], T.DUM[:], T.sB[:, 15::16], A.subtract, ["sB0", "sB1", "DUM"], ["w3"])
        ts(s_, T.w1[:, 80:81], T.Y[:, 255:256], T.N1[:, 255:256], T.sm[:, 32:33], A.max, A.min, ["Y1", "N1", "spare"], ["w5"])
        tt(s_, w[4], w[1], w[3], A.min, ["w1", "w3"], ["w4"])
        ts(s_, T.TG[:, 0:17], T.w1[:, 64:81], -1.0, 256.0, A.mult, A.add, ["w4", "w5"], ["TG"])
        for a, b in pieces(BCUT):
            cp(50 + 2.7 * 16 * (b - a), LP[:].indirect(T.TG[:, a:b]), T.CR[:, 16 * a + 1:16 * b + 1],
               ["TG", "CR", "LPa%d" % r] + (["CRx"] if b == 17 else []), [LPk])
        if "LP" in ONV:
            ts(s_, LP[:, 0:1], LP[:, 0:1], LP[:, 256:257], None, A.max, None, [LPk], [LPk])
        else:
            act(s_, LP[:, 0:1], LP[:, 0:1], F.Identity, [LPk], [LPk], bias=LP[:, 256:257])
        for h in range(2):
            a = 128 * h
            gather(128, T.LR[:, a:a + 128], LP[:, 0:256].indirect(T.pos[:, 8 * h:8 * h + 8]), [LPk, "pos"], ["LR%d" % h])
        scan(s_, T.sL[:, 0:128], T.m16[:], T.LR[:, 0:128], 0.0, A.add, A.min, ["m16", "LR0"], ["sL0"])
        ts(s_, T.oL[:, 0:8], T.sL[:, 15:128:16], col(3), -1.0, A.add, A.add, ["sL0", "c3"], ["oL0"])
        wrap4(T.LR, T.sL, 128, 256, ["LR1"], "sL1", T.oL[:, 32:64], "oL1")

        unpack(OWN, xq, xs, xk, T.To, "To")
        gather(128, T.AB[:, 0:128], T.O[:, 0:256].indirect(T.PL[:, 0:8]), ["O", "PL"], ["AB0"])
        gather(128, T.AB[:, 128:256], T.O[:, 0:256].indirect(T.PL[:, 16:24]), ["O", "PL"], ["AB1"])
        gather(128, T.AB[:, 256:384], T.O[:, 0:257].indirect(T.PL[:, 8:16]), ["O", "Ox", "PL"], ["AB2"])
        gather(128, T.AB[:, 384:512], T.O[:, 0:256].indirect(T.PL[:, 24:32]), ["O", "PL"], ["AB3"])
        wrap4(T.AB, T.s4, 0, 256, ["AB0", "AB1"], "s40", so[:], "so%d" % r)
        wrap4(T.AB, T.s4, 256, 512, ["AB2", "AB3"], "s41", T.oH[:], "oH")
        low = (0, T.To, "To", so, "so%d" % r, FAR)
        late[0] = True
        if r not in ZR:
            exchange(peer, [(lo[:], so[:], 16, ["so%d" % r])], "al%d" % r, lk)
            unpack(FAR, lq, lsc, ["lq%d" % r], T.Tp, "Tp")
            low = (0, T.Tp, "Tp", lo, lk, FAR)

        for h, Tw, tk, off, ok, banks in ((1, T.To, "To", T.oH, "oH", OWN), low):
            R = [tk + str(n) for n in range(4)] + [ok]
            for a, b in pieces(ZCUT[h]):
                c, d = 512 * h + a, 512 * h + b
                act(pick(b - a), T.Zb[:, c:d], Tw[:].indirect(off[:, 32 + a // 16:32 + b // 16]), F.Identity, R, ["Zb%d" % c])
                tt(pick(b - a), T.Z[:, c:d], Tw[:].indirect(off[:, a // 16:b // 16]), T.Zb[:, c:d], A.add, R + ["Zb%d" % c], ["Z%d" % c])
            zq, zs, zk = T.zq[:, 128 * h:128 * h + 128], T.zs[:, 128 * h:128 * h + 128], "zq%d" % h
            if h == 0 and r in ZR:
                zq, zs, zk = lq[:, 128:256], lsc[:, 128:256], "zo%d" % r
            qz(128, zq, zs, T.Z[:, 512 * h:512 * h + 512], ["Z%d" % (512 * h + a) for a in ZCUT[h][:-1]], [zk])
            if h == 0 and r in ZR:
                exchange(peer, [(lq[:, 0:128].bitcast(dt.uint8), zq.bitcast(dt.uint8), 64, [zk]), (lsc[:, 0:128], zs, 80, [zk])],
                         "aq%d" % r, "lq%d" % r)
                zq, zs, zk = lq[:, 0:128], lsc[:, 0:128], "lq%d" % r
            for k in range(4):
                mm(banks[k], 128, T.wq[:, 128 * k:128 * k + 128], T.wsc[:, 128 * k:128 * k + 128], zq, zs, ["w0", "w1_", zk])
            for k in range(4):
                lin(128, T.V[:, 256 * k + 128 * h:256 * k + 128 * h + 128], bank(banks[k], 0, 128), 0.03125, 0.0,
                    ["P%d" % banks[k]], ["V%d%d" % (h, k)])

    now[0] = 3
    lin(256, T.LF[:], T.LR[:], 1.0, -1.0, ["LR0", "LR1"], ["LF"])
    dma("y", 8, T.lb[:], T.LF[0:128:16, :], ["LF"], ["lb"], "o1")
    for h in range(2):
        a, b = 128 * h, 128 * h + 128
        state(3, h)
        key = "xq3%d" % h
        mm(4 + h, 128, T.vq[:], T.vs[:], T.xq3[:, a:b], T.xs3[:, a:b], ["vq", key])
        dma("y", 64, T.oc[:, 4 * a:4 * b], T.xq3[:, a:b].bitcast(dt.uint8), [key], ["oc%d" % h], "o1")
        if h == 0:
            act(h_, T.yo[:, a:b], bank(4, 0, 128), F.Identity, ["P4"], ["yo0"])
            dma("s", 64, T.y[:, a:b], T.yo[:, a:b], ["yo0"], ["y0"], "o2")
        else:
            cp(h_, T.yo[:, a:b], bank(5, 0, 128), ["P5"], ["yo1"])
            for k in range(4):
                dma("s" if k < 3 else "y", 1, T.osc[4 * k:4 * k + 4, :], T.xs3[32 * k:32 * k + 4, :], ["xq30", "xq31"],
                    ["osc%d" % k], "o2" if k < 3 else "o1")
            dma("y", 64, T.y[:, a:b], T.yo[:, a:b], ["yo1"], ["y1o"], "o1")

    order = listed_order(ops) if ORDER else issue_order(ops)
    count, mark = {}, {}
    for q in order:
        for n in order[q]:
            count[ops[n]["sem"]] = count.get(ops[n]["sem"], 0) + ops[n]["inc"]
            mark[n] = count[ops[n]["sem"]]
    for q in Q:
        seen = {}
        for n in order[q]:
            want = {}
            for d in ops[n]["after"]:
                want[ops[d]["sem"]] = max(want.get(ops[d]["sem"], 0), mark[d])
            for sem, val in want.items():
                if seen.get(sem, 0) < val:
                    Q[q].wait_ge(T.sem[sem], val)
                    seen[sem] = val
            ins = ops[n]["fn"]()
            if ins is not None:
                ins.then_inc(T.sem[ops[n]["sem"]], ops[n]["inc"])
    for sem, val in count.items():
        g.sync.wait_ge(T.sem[sem], val)
